import numpy as np, ml_dtypes
CORES = [16,17,18,19,32,33,34,35]
N = 8
import mx_ref
BF = ml_dtypes.bfloat16
def gcols(t, e):
    v = np.concatenate([t.reshape(8, 16, -1, 4), np.zeros((8, 16, 1, 4), BF)], axis=2)
    return np.ascontiguousarray(np.stack([v[g][:, e[g]] for g in range(8)])).reshape(128, -1)
def tile(rs):
    return np.stack(rs, axis=2).reshape(128, -1).astype(BF)
def cut(t, i, w=512):
    return t[:, w * i:w * i + w]
def pick(q, e):
    c = np.concatenate([q[0].reshape(128, -1, 4), np.zeros((128, 1, 4), np.uint8)], axis=1); s = np.concatenate([q[1], np.ones((16, 1), np.uint8)], axis=1)
    return (np.ascontiguousarray(c[:, e].reshape(128, -1)), np.ascontiguousarray(s[:, e]))
def join(*qs):
    return (np.concatenate([q[0] for q in qs], axis=1), np.concatenate([q[1] for q in qs], axis=1))
def put(q, e, v):
    c, s = q[0].reshape(128, -1, 4).copy(), q[1].copy(); c[:, e] = v[0].reshape(128, -1, 4); s[:, e] = v[1]
    return (c.reshape(128, -1), s)
def pk(c, s):
    return (np.ascontiguousarray(c), mx_ref.live(s))
def emit(q):
    return q[0], q[1]
def packed(v, rng):
    q = [mx_ref.quantize(np.ascontiguousarray(v[r])) for r in range(N)]
    return np.stack([a for a, b in q]), np.stack([mx_ref.plane(b, rng) for a, b in q])
def values_of_codes():
    e, c = np.zeros((128, 128, 4), np.float32), np.zeros((128, 2, 4), np.uint8)
    e[np.arange(128), np.arange(128), 0] = 1
    c[:127, :, 0] = np.arange(256).reshape(2, 128).T[:127]
    return mx_ref.matmul(mx_ref.quantize(e.reshape(128, 512).astype(BF)), (c.reshape(128, 8), np.full((16, 2), 127, np.uint8))).T.reshape(-1).astype(np.float64)
CODE_VALUE, SCALE_VALUE = values_of_codes(), 2.0 ** (np.arange(256) - 127.0)
def decode(q):
    return (CODE_VALUE[q[0]].reshape(16, 8, -1, 4) * SCALE_VALUE[q[1]][:, None, :, None] + 0.0).reshape(128, -1).astype(np.float32)
def f(rng, *shape):
    return mx_ref.flush((rng.standard_normal(shape, dtype=np.float32) * np.exp2(rng.integers(-2, 3, shape[:-1] + (1,)))).astype(BF))
def wide(rng, *shape, cols=0):
    v = rng.standard_normal(shape, dtype=np.float32) * np.exp2(rng.integers(-12, 13, shape)).astype(np.float32)
    if cols: v *= np.repeat(np.exp2(rng.integers(-cols, cols + 1, shape[:-2] + (1, shape[-1] // 4))) * (rng.random(shape[:-2] + (1, shape[-1] // 4)) > 0.0625), 4, axis=-1).astype(np.float32)
    return mx_ref.flush(v.astype(BF))
C, H, E, R = 384, 64, 448, 3
def big(v):
    v = v.astype(np.float32)
    v[np.abs(v) < np.float32(2.0 ** -16)] = 0
    return v.astype(BF)
def numbers_of(rng):
    return {"x": big(f(rng, N, 128, 4 * C)), "u": np.array(f(rng, N, 128, 512)), "v": np.array(f(rng, N, 128, 512))}
def layers(rng):
    return big(f(rng, N, 128, 2048)).reshape(N, 8, 16, 4, 8, 16, 4)
def weights(rng, w):
    c, p = packed(np.ascontiguousarray(w).reshape(N, 128, 2048), rng)
    return {"wc": c, "ws": p}
def setup_inputs(rng):
    return {**numbers_of(rng), **weights(rng, layers(rng))}
def setup_inputs_ties(rng):
    d = numbers_of(rng)
    e = rng.permutation(N)
    x = d["x"].reshape(N, 8, 16, C, 4)
    for r in range(N):
        k = rng.permutation(C) % 3
        if r == e[0]: k = np.zeros(C, int)
        elif r in e[2::2]: k = rng.permutation(3)[np.arange(C) % 3]
        a = x[r][:, :8, :3].copy()
        a[:, :, 2] = 0
        x[r][:, :8] = a[:, :, k]
    x[e[1]] = 0
    u = d["u"].reshape(N, 8, 16, 128, 4)
    u[:, :, 8:, ::16] = 0
    u[:, :, 8:, 1::16] = 0
    w = layers(rng)
    w[:, :, :, :, :, :8] = 0
    return {"x": x.reshape(N, 128, 4 * C), "u": u.reshape(N, 128, 512), "v": d["v"], **weights(rng, w)}
def setup_inputs_near(rng):
    d = numbers_of(rng)
    x = d["x"].reshape(N, 8, 16, C, 4)
    u = d["u"].reshape(N, 128, 128, 4)
    o = rng.permutation(N) % 4
    x[:, :, :8] = 0
    u[:, :, ::16] = 0
    u[:, :, 1::16] = 0
    for r in range(N):
        s = rng.integers(-1, 2, (8, 2, C)).astype(np.float32)
        if o[r] % 2 == 1: s = s[:, :, np.arange(C) // 16]
        if o[r] < 2: s = s * np.float32(2.0 ** -29)
        for g in rng.permutation(8)[:4]: s[g, :, rng.integers(C)] = 2.0 ** 29 * rng.choice([-1.0, 1.0], 2)
        x[r, :, :2, :, 0] = s.astype(BF)
        for h in range(0, 128, 16):
            u[r, h, h, 0] = 2.0 ** -30 if o[r] < 2 else 1.0
            u[r, h + 1, h + 1, 0] = 2.0 ** -30 if o[r] < 2 else 1.0
    w = layers(rng)
    w[:, :, :8] = 0
    w[:, :, :, :, :, :8] = 0
    return {"x": x.reshape(N, 128, 4 * C), "u": u.reshape(N, 128, 512), "v": d["v"], **weights(rng, w)}
def setup_inputs_late(rng):
    d = numbers_of(rng)
    x = d["x"].reshape(N, 8, 16, C, 4)
    c = (rng.permutation(N) % 2 * 2.0 - 1.0).astype(np.float32).astype(BF)
    x[:, :, 0] = c[:, None, None, None]
    u = d["u"].reshape(N, 128, 128, 4)
    u[:, :, ::16] = 0
    u[:, :, 1::16] = 0
    for h in range(0, 128, 16):
        u[:, h, h, 0] = 1
        u[:, h, h + 1, 1] = 1
    return {"x": x.reshape(N, 128, 4 * C), "u": u.reshape(N, 128, 512), "v": d["v"], **weights(rng, layers(rng))}
def setup_inputs_huge(rng):
    d = numbers_of(rng)
    h = rng.permutation(8)
    x = -0.95 - 0.05 * rng.random((N, 8, 16, C, 4))
    x[:, h[4:]] = (0.75 + 0.1 * rng.random((N, 4, 16, C, 4))) * rng.choice([-1.0, 1.0], (N, 4, 1, C, 1))
    u = d["u"].reshape(N, 128, 128, 4)
    u[:, :, ::16] = 0
    u[:, :, 1::16] = 0
    for r in range(N):
        for g in range(8):
            for b in range(2):
                a = 16 * int(rng.choice(h[4:]))
                u[r, a:a + 16, 16 * g + b] = (2.0 ** 30 * (1 - 0.1 * rng.random((16, 4))) * rng.choice([-1.0, 1.0])).astype(np.float32).astype(BF)
    w = np.zeros((N, 128, 4, 128, 4), np.float32)
    i = np.arange(128)
    for b in range(4): w[:, i, b, i, b] = -1
    return {"x": (2.0 ** 30 * x).astype(np.float32).reshape(N, 128, 4 * C).astype(BF), "u": u.reshape(N, 128, 512), "v": d["v"], **weights(rng, w.astype(BF))}
def setup_inputs_spread(rng):
    d = setup_inputs(rng)
    d["x"] = big(wide(rng, N, 128, 4 * C, cols=6))
    return d
def check_inputs(d):
    b = []
    for k in ("x", "u", "v"):
        a = np.abs(d[k].astype(np.float32))
        if not (np.isfinite(a).all() and ((a == 0) | (a >= 2.0 ** -30) & (a <= 2.0 ** 30)).all()): b.append("a value of " + k)
    none, least, most = [emit(mx_ref.quantize(np.full((128, 16), k, np.float32).astype(BF)))[1][0, 0] for k in (0.0, 2.0 ** -30, 2.0 ** 30)]
    for r in range(N):
        if ((d["wc"][r] == 0x7F) | (d["wc"][r] == 0xFF)).any(): b.append("wc: a code that is no number")
        s = mx_ref.live(d["ws"][r])
        if ((s != none) & ((s < least) | (s > most))).any(): b.append("ws: a scale out of range")
    return b
def reference(x, u, v, wc, ws):
    qu = [mx_ref.quantize(u[r]) for r in range(N)]
    lay = [pk(wc[r], ws[r]) for r in range(N)]
    now = [x[r] for r in range(N)]
    level = np.zeros((N, 8, E), np.int64)
    for t in range(R):
        d = 2 ** t
        q = [mx_ref.quantize(now[r]) for r in range(N)]
        halo = [pick(q[r], np.arange(H)) for r in range(N)]
        came = decode(join(*halo)).astype(BF)
        made = []
        for r in range(N):
            e = (r + 1) % N
            s = mx_ref.matmul(qu[r], join(q[r], halo[e]))
            if t == 0: word = 2 * (s[::16] > 0) + (s[1::16] > 0)
            else: word = 2 * level[r] + (s[::16] > 0)
            key = 1024 * word
            key[:, :E - d] += 1 + word[:, d:]
            o = np.argsort(key, axis=1, kind="stable")
            for g in range(8): level[r, g] = np.searchsorted(key[g, o[g]], key[g])
            n, m = np.zeros((8, E), np.int64), np.zeros((8, E), np.int64)
            np.put_along_axis(n, o, np.concatenate([o[:, :1], o[:, :-1]], axis=1), axis=1)
            np.put_along_axis(m, o, np.concatenate([o[:, 1:], o[:, -1:]], axis=1), axis=1)
            a = np.concatenate([now[r], cut(came, e, 4 * H)], axis=1)
            most = np.maximum(gcols(a, n[:, :C]).astype(np.float32), gcols(a, m[:, :C]).astype(np.float32))
            z = mx_ref.quantize(((now[r].astype(np.float32) + most) * np.float32(0.5)).astype(BF))
            made.append(tile([mx_ref.matmul(pick(lay[r], np.arange(128 * b, 128 * b + 128)), z) * np.float32(0.03125) + now[r][:, b::4].astype(np.float32) for b in range(4)]))
        now = made
    y, lv = np.zeros((N, 128, C), np.float32), np.zeros((N, 8, E), np.float32)
    oc, osc = np.zeros((N, 128, 4 * C), np.uint8), np.zeros((N, 16, C), np.uint8)
    for r in range(N):
        q = mx_ref.quantize(now[r])
        y[r] = mx_ref.matmul(mx_ref.quantize(v[r]), q)
        lv[r] = level[r]
        oc[r], osc[r] = emit(q)
    return {"y": y, "lv": lv, "oc": oc, "osc": osc}

@@ -1,0 +1,410 @@
+from concourse.mybir import dt, AluOpType, ActivationFunctionType
+
+C, H, E, NR = 384, 64, 448, 3
+OFF = 16
+NS = (0, 16, 18)
+
+SCRATCH = {}
+for _k, _n in (("qu", 128), ("qur", 256), ("qv", 128), ("qw", 512), ("qe", 512), ("qc", 512), ("qz", C), ("qq", 212), ("qg", 128), ("qh", E + 32)):
+    SCRATCH[_k] = ("sbuf", [128, _n], "float8_e4m3fn_x4")
+    SCRATCH[{"qc": "cs"}.get(_k, "s" + _k[1:])] = ("sbuf", [128, _n], "uint8")
+for _k, _n in (("ut", 512), ("vt", 512), ("et", 2048), ("ct", 2048), ("gt", 512), ("ga", 512), ("hl", 4 * (E + 32)), ("zt", 4 * C), ("vp", 4 * E),
+               ("x32", 4 * C), ("vs", 4 * E), ("mm", 4 * E), ("hb", 128), ("ident", 128), ("iom", E), ("ones", 512), ("t1", E), ("t2", E),
+               ("w5", E + 16), ("w6", E), ("er", E + 16), ("ar1", E + 16), ("ar2", E + 16), ("junk", 4 * E), ("cb", 16 * E), ("sc", 8 * E),
+               ("ordr", E + 32), ("oa", E), ("ob", E + 32), ("eq", 848), ("eqs", E)):
+    SCRATCH[_k] = ("sbuf", [128, _n], "bfloat16")
+for _k, _n in (("iof", E), ("ev", 1), ("od", 1), ("pl", 1), ("pq", 1), ("lama", 1), ("lam", 1), ("lamb", 1), ("lams", 1), ("first", 1),
+               ("qi", 16), ("behind", 16), ("lr", E + 16), ("al", E), ("ag", E), ("g1", E),
+               ("s1", E), ("s2", E), ("kr", E + 32), ("ka", E), ("kb", E + 32), ("ma", 28), ("mb", 28), ("o1", 28), ("o2", 28),
+               ("own", 28), ("acc", 28), ("posf", 28), ("posg", 28), ("p3", 28), ("d2", 2 * E), ("ks", E + 16), ("rr", E), ("lw", E),
+               ("lvr", E), ("yr", C)):
+    SCRATCH[_k] = ("sbuf", [128, _n], "float32")
+for _k, _n in (("uo", 16), ("pin", 1), ("pod", 1), ("pla", 1), ("plq", 1)):
+    SCRATCH[_k] = ("sbuf", [128, _n], "int32")
+for _k, _n in (("uo16", 16), ("pos", 28), ("ordl", 28)):
+    SCRATCH[_k] = ("sbuf", [128, _n], "uint16")
+SCRATCH["ps"] = ("psum", [128, 4096], "float32")
+for _t in range(NR + 1):
+    SCRATCH["xt%d" % _t] = ("sbuf", [128, 4 * C], "bfloat16")
+    SCRATCH["qx%d" % _t] = ("sbuf", [128, E], "float8_e4m3fn_x4")
+    SCRATCH["sx%d" % _t] = ("sbuf", [128, E], "uint8")
+DMAS = ["dxa", "dxb", "du", "dv", "dwc", "dws", "dlv", "dya", "dyb", "dca", "dcb"] + ["ds%d" % k for k in range(4)]
+SEMAPHORES = ["vec", "act", "ten", "pool", "left"] + ["arr%d" % t for t in range(NR)] + DMAS
+
+ADD, SUB, MUL, MAX = AluOpType.add, AluOpType.subtract, AluOpType.mult, AluOpType.max
+GT, LT, GE, EQ = AluOpType.is_gt, AluOpType.is_lt, AluOpType.is_ge, AluOpType.is_equal
+COPY, IDEN, SIGN = ActivationFunctionType.Copy, ActivationFunctionType.Identity, ActivationFunctionType.Sign
+CENTER = 5380840.0
+
+
+def rank_program(g, core, T, topo):
+    rank = T.rank_of(core)
+    if rank is None:
+        return
+    n = len(T.cores)
+    prev, nxt = T.cores[(rank - 1) % n], T.cores[(rank + 1) % n]
+
+    def send_engines(src, dst):
+        return topo.engines(src, dst)[:8]
+
+    queue = {"v": g.vector, "a": g.scalar, "t": g.tensor, "g": g, "s": g.sync}
+    semof = {"v": "vec", "a": "act", "t": "ten", "g": "pool"}
+    count = {"vec": 0, "act": 0, "ten": 0, "pool": 0}
+    seen = {q: {} for q in queue}
+    hist = {}
+
+    def waits(q, reads, writes):
+        need = {}
+        for regs, isw in ((reads, False), (writes, True)):
+            for name, lo, hi in regs:
+                for l, h, w, oq, sem, val in hist.get(name, ()):
+                    if l < hi and lo < h and (w or isw):
+                        if oq == q and isw and not w:
+                            continue
+                        need[sem] = max(need.get(sem, 0), val)
+        for sem in sorted(need):
+            if seen[q].get(sem, 0) < need[sem]:
+                queue[q].wait_ge(T.sem[sem], need[sem])
+                seen[q][sem] = need[sem]
+
+    def note(q, reads, writes, sem, val):
+        for name, lo, hi in writes:
+            hist[name] = [e for e in hist.get(name, ()) if not (lo <= e[0] and e[1] <= hi)] + [(lo, hi, True, q, sem, val)]
+        for name, lo, hi in reads:
+            hist.setdefault(name, []).append((lo, hi, False, q, sem, val))
+
+    def op(q, reads, writes, fn, *args, **kw):
+        waits(q, reads, writes)
+        sem = semof[q]
+        fn(*args, **kw).then_inc(T.sem[sem], 1)
+        count[sem] += 1
+        note(q, reads, writes, sem, count[sem])
+
+    def dma(q, sem, reads, writes, out, in_):
+        waits(q, reads, writes)
+        queue[q].dma_start(out, in_).then_inc(T.sem[sem], 16)
+        note("dma", reads, writes, sem, 16)
+
+    def V(name, lo, hi, step=1):
+        return T[name][:, lo:hi] if step == 1 else T[name][:, lo:hi:step]
+
+    def tt(out, a, b, o, R, W):
+        op("v", R, W, g.vector.tensor_tensor, out, a, b, o)
+
+    def ts(out, a, s1, s2, o0, o1, R, W):
+        if o1 is None:
+            op("v", R, W, g.vector.tensor_scalar, out, a, s1, None, o0)
+        else:
+            op("v", R, W, g.vector.tensor_scalar, out, a, s1, s2, o0, o1)
+
+    def tc(out, in_, R, W):
+        op("v", R, W, g.vector.tensor_copy, out, in_)
+
+    def act(out, in_, f, R, W, **kw):
+        op("a", R, W, g.scalar.activation, out, in_, f, **kw)
+
+    def fill(name, lo, hi, c):
+        op("v", [], [(name, lo, hi)], g.vector.memset, V(name, lo, hi), c)
+
+    def quant(codes, plane, src, lo, hi, R):
+        op("v", R, [(codes, lo, hi)], g.vector.quantize_mx, V(codes, lo, hi), V(plane, lo, hi), V(src, 4 * lo, 4 * hi))
+
+    def mx(bank, cols, l, ls, llo, r, rs, rlo, rhi, start=True, stop=True):
+        op("t", [(l, llo, llo + 128), (r, rlo, rhi)], [("b%d" % bank, 0, 512)], g.tensor.matmul_mx,
+           T.ps[:, 512 * bank:512 * bank + cols], V(l, llo, llo + 128), V(ls, llo, llo + 128),
+           V(r, rlo, rhi), V(rs, rlo, rhi), start, stop)
+
+    def bank(k, lo, hi):
+        return T.ps[:, 512 * k + lo:512 * k + hi]
+
+    def send(t):
+        waits("g", [("qx%d" % t, 0, H)], [])
+        rid, pid = topo.addr(prev)[0], topo.addr(prev)[1]
+        m = 0
+        for e in send_engines(core, prev):
+            m |= 1 << e
+        q, s = "qx%d" % t, "sx%d" % t
+        g.remote_dma(V(q, C, E).bitcast(dt.uint8), V(q, 0, H).bitcast(dt.uint8), T.sem["arr%d" % t], T.sem.left, pid, rid, m)
+        g.remote_dma(V(s, C, E), V(s, 0, H), T.sem["arr%d" % t], T.sem.left, pid, rid, m)
+        note("remote", [], [(q, C, E)], "arr%d" % t, 2 * len(send_engines(nxt, core)))
+
+    xr = lambda t, lo, hi: [("x%d_%d" % (t, b), lo, hi) for b in range(4)]
+    dma("s", "dxa", [], xr(0, 0, 128), T.xt0[:, 0:512], T.x[:, 0:512])
+    dma("a", "du", [], [("ut", 0, 128)], T.ut[:, :], T.u[:, :])
+    dma("s", "dxb", [], xr(0, 128, C), T.xt0[:, 512:1536], T.x[:, 512:1536])
+    dma("s", "dwc", [], [("qw", 0, 512)], T.qw[:, 0:512].bitcast(dt.uint8), T.wc[:, :])
+    dma("s", "dws", [], [("qw", 0, 512)], T.sw[:, :], T.ws[:, :])
+    dma("a", "dv", [], [("vt", 0, 128)], T.vt[:, :], T.v[:, :])
+    hist["qw"] = [(0, 512, True, "dma", "dwc", 16), (0, 512, True, "dma", "dws", 16)]
+    fill("hb", 0, 128, 0.5)
+    op("g", [], [("uo", 0, 16)], g.iota, T.uo[:, :], [[1, 2], [16, 8]], 0, 0)
+    op("g", [], [("pin", 0, 1)], g.iota, T.pin[:, :], [[0, 1]], 0, 1)
+    op("g", [], [("qi", 0, 16)], g.iota, T.qi[:, :], [[1, 16]], 0, 0, allow_small_or_imprecise_dtypes=True)
+    op("g", [("hb", 0, 128)], [("ident", 0, 128)], g.affine_select, T.ident[:, :], T.hb[:, :], [[-1, 128]], EQ, 0.0, 0, 1)
+    fill("ones", 0, 512, 1.0)
+    fill("w5", E, E + 16, -512.0)
+    fill("er", E, E + 16, -256.0)
+    for lo, hi in ((0, OFF), (OFF + E, E + 32)):
+        fill("ordr", lo, hi, 0.0)
+    tc(T.uo16[:, :], T.uo[:, :], [("uo", 0, 16)], [("uo16", 0, 16)])
+    for nm, a, b in (("pla", 15, None), ("plq", 2, 3), ("pod", 4, 1)):
+        if b is None:
+            op("v", [("pin", 0, 1)], [(nm, 0, 1)], g.vector.tensor_scalar, T[nm][:, :], T.pin[:, :], a, b, AluOpType.bitwise_and)
+        else:
+            op("v", [("pin", 0, 1)], [(nm, 0, 1)], g.vector.tensor_scalar, T[nm][:, :], T.pin[:, :], a, b, AluOpType.logical_shift_right, AluOpType.bitwise_and)
+    for nm, src in (("pl", "pla"), ("pq", "plq"), ("od", "pod")):
+        tc(T[nm][:, :], T[src][:, :], [(src, 0, 1)], [(nm, 0, 1)])
+    ts(T.ev[:, :], T.od[:, :], -1.0, 1.0, MUL, ADD, [("od", 0, 1)], [("ev", 0, 1)])
+    ts(T.lama[:, :], T.pq[:, :], 512.0, 512.0, MUL, ADD, [("pq", 0, 1)], [("lama", 0, 1)])
+    ts(T.lam[:, :], T.pl[:, :], 512.0, T.lama[:, 0:1], MUL, ADD, [("pl", 0, 1), ("lama", 0, 1)], [("lam", 0, 1)])
+    for nm, c in (("lamb", -512.0), ("lams", -256.0)):
+        ts(T[nm][:, :], T.lam[:, :], c, None, ADD, None, [("lam", 0, 1)], [(nm, 0, 1)])
+    fill("et", 0, 2048, 0.0)
+    for b in range(4):
+        tc(T.et[:, 512 * b + b:512 * b + 512:4], T.ident[:, :], [("ident", 0, 128)], [("et", 512 * b, 512 * b + 512)])
+    quant("qx0", "sx0", "xt0", 0, 128, xr(0, 0, 128))
+    send(0)
+    op("g", [("ones", 0, 512)], [("ga", 0, 512)], g.affine_select, T.ga[:, :], T.ones[:, :], [[-16, 8], [0, 64]], GE, 0.0, 0, 1)
+    op("g", [("ga", 0, 512)], [("gt", 0, 512)], g.affine_select, T.gt[:, :], T.ga[:, :], [[16, 8], [0, 64]], GE, 0.0, 15, -1)
+    op("g", [], [("iom", 0, E)], g.iota, T.iom[:, :], [[1, E]], -192, 0, allow_small_or_imprecise_dtypes=True)
+    op("g", [], [("iof", 0, E)], g.iota, T.iof[:, :], [[1, E]], 0, 0, allow_small_or_imprecise_dtypes=True)
+    quant("qu", "su", "ut", 0, 128, [("ut", 0, 128)])
+    op("v", [("qu", 0, 128), ("uo16", 0, 16)], [("qur", 0, 256)], g.vector.tensor_copy,
+       T.qur[:, 0:256].bitcast(dt.uint32), T.qu[:, 0:128].bitcast(dt.uint32).indirect(T.uo16[:, 0:16]))
+    act(V("hl", 2, 1920, 4), V("ones", 0, 480), COPY, [("ones", 0, 512)], [("hl", 2, 3)], scale=0.0)
+    act(V("hl", 3, 1920, 4), V("ones", 0, 480), COPY, [("ones", 0, 512)], [("hl", 3, 4)], scale=0.0)
+    op("a", [("qu", 0, 128), ("uo16", 0, 16)], [("qurs", 0, 256)], g.scalar.activation,
+       T.sur[:, 0:256], T.su[:, 0:128].indirect(T.uo16[:, 0:16]), COPY)
+    for b in range(2):
+        act(V("hl", b, 64, 4), V("ones", 0, 16), COPY, [("ones", 0, 512)], [("hl", 4 + b, 5 + b)], scale=0.0)
+        act(V("hl", 4 * (OFF + E) + b, 1920, 4), V("ones", 0, 16), COPY, [("ones", 0, 512)], [("hl", 6 + b, 7 + b)], scale=0.0)
+    quant("qx0", "sx0", "xt0", 128, C, xr(0, 128, C))
+    quant("qe", "se", "et", 0, 512, [("et", 0, 2048)])
+    for b in range(4):
+        act(V("vp", E * b, E * b + C), V("xt0", b, 4 * C, 4), COPY, [("x0_%d" % b, 0, C)], [("vp%d" % b, 0, C)], scale=0.5)
+    waits("t", [("qurs", 0, 256)], [])
+
+    def wrap(row, reg, ta, tb, out):
+        op("v", reg, [(ta, 0, E)], g.vector.transpose, V(ta, 0, E), row(OFF, OFF + E))
+        op("v", reg, [(tb, 0, E)], g.vector.transpose, V(tb, 0, E + 32), row(0, E + 32))
+        tt(V("o1", 0, 28), V(ta, 0, E, 16), V("ma", 0, 28), MUL, [(ta, 0, E), ("ma", 0, 2)], [("o1", 0, 28)])
+        tt(V("o2", 0, 28), V(tb, 16, E + 16, 16), V("mb", 0, 28), MUL, [(tb, 0, E), ("mb", 0, 2)], [("o2", 0, 28)])
+        tt(V(out, 0, 28), V("o1", 0, 28), V("o2", 0, 28), ADD, [("o1", 0, 28), ("o2", 0, 28)], [(out, 0, 28)])
+
+    def words0(k, sl, sh, lo, hi, klo, khi):
+        ts(V("t1", lo, hi), bank(k, sl, sh), 0.0, 1024.0, GT, MUL, [("b%d" % k, 0, 1)], [("t1", lo, hi)])
+        ts(V("t2", lo, hi), bank(k + 1, sl, sh), 0.0, 512.0, GT, MUL, [("b%d" % (k + 1), 0, 1)], [("t2", lo, hi)])
+        tt(V("w5", lo, hi), V("t1", lo, hi), V("t2", lo, hi), ADD, [("t1", lo, hi), ("t2", lo, hi)], [("w5", lo, hi)])
+        ts(V("w6", klo, khi), V("w5", klo, khi), 5.0, 512.0, MUL, ADD, [("w5", klo, khi)], [("w6", klo, khi)])
+        tt(V("er", klo, khi), V("w6", klo, khi), V("w5", klo + 1, khi + 1), ADD, [("w6", klo, khi), ("w5", klo + 1, khi + 1)], [("er", klo, khi)])
+
+    def words(t, k, sl, sh, lo, hi):
+        d = 2 ** t
+        ar, klo, khi = "ar%d" % t, max(lo - d, 0), hi if hi == E else hi - d
+        unit, fac = ((512.0, 41.0), (1.0, 3281.0))[t - 1]
+        ts(V(ar, lo, hi), bank(k, sl, sh), 0.0, unit, GT, MUL, [("b%d" % k, 0, 1)], [(ar, lo, hi)])
+        ts(V("al", klo, khi), V(ar, klo, khi), fac, None, MUL, None, [(ar, klo, khi)], [("al", klo, khi)])
+        tt(V("ag", klo, khi), V("al", klo, khi), V("g1", klo, khi), ADD, [("al", klo, khi), ("g1", klo, khi)], [("ag", klo, khi)])
+        tt(V("kr", OFF + klo, OFF + khi), V("ag", klo, khi), V(ar, klo + d, khi + d), ADD,
+           [("ag", klo, khi), (ar, klo + d, khi + d)], [("kr", OFF + klo, OFF + khi)])
+        if t == NR - 1:
+            for o, e in ((0, 0.5), (E, -0.5)):
+                act(V("d2", o + klo, o + khi), V("kr", OFF + klo, OFF + khi), IDEN, [("kr", OFF + klo, OFF + khi)], [("d2", o + klo, o + khi)], bias=e)
+
+    K = V("kr", OFF, OFF + E)
+    KR = [("kr", OFF, OFF + E)]
+
+    for t in range(NR):
+        qx, sx = "qx%d" % t, "sx%d" % t
+        last = t == NR - 1
+        if t == 0:
+            mx(0, C, "qur", "sur", 0, qx, sx, 0, C)
+            mx(1, C, "qur", "sur", 128, qx, sx, 0, C)
+            words0(0, 0, C, 0, C, 0, C - 1)
+            for nm, a, b in (("ma", "ev", "od"), ("mb", "od", "ev")):
+                ts(V(nm, 0, 28, 2), V("ones", 0, 14), T[a][:, 0:1], None, MUL, None, [("ones", 0, 512), (a, 0, 1)], [(nm, 0, 1)])
+                ts(V(nm, 1, 28, 2), V("ones", 0, 14), T[b][:, 0:1], None, MUL, None, [("ones", 0, 512), (b, 0, 1)], [(nm, 1, 2)])
+            mx(2, 128, "qur", "sur", 0, qx, sx, E - 128, E)
+            mx(3, 128, "qur", "sur", 128, qx, sx, E - 128, E)
+        else:
+            mx(1, E - 128, "qur", "sur", 0, qx, sx, 128, E)
+        for b in range(4):
+            mx(4 + b, 128, "qe", "se", 128 * b, qx, sx, E - 128, E)
+        if t == 0:
+            words0(2, 64, 128, C, E, C - 1, E)
+            act(V("junk", 0, E), V("er", 0, E), SIGN, [("er", 0, E), ("lams", 0, 1)], [("junk0", 0, 1), ("acc", 0, 1)],
+                bias=T.lams[:, 0:1], scale=-1.0, accum_out=T.acc[:, 0:1])
+        else:
+            words(t, 1, 0, E - 128, 128, E)
+        for b in range(4):
+            act(V("vp", E * b + C, E * b + E), bank(4 + b, 64, 128), COPY, [("b%d" % (4 + b), 0, 1)], [("vp%d" % b, C, E)])
+        ns = NS[t]
+        nv = 28 - ns
+        if t == 0:
+            act(V("s1", 0, E), V("er", 0, E), IDEN, [("er", 0, E)], [("s1", 0, E)], bias=512.0, scale=82.0)
+            act(V("s2", 0, E), V("er", 2, E + 2), COPY, [("er", 0, E + 16)], [("s2", 0, E)], scale=2.0)
+            for b in range(4):
+                act(V("x32", C * b, C * b + C), V("xt0", b, 4 * C, 4), COPY, [("x0_%d" % b, 0, C)], [("x32_%d" % b, 0, C)], scale=32.0)
+            O = V("cb", 0, E)
+            ts(V("cb", 0, E - 1), V("er", 0, E - 1), T.lam[:, 0:1], None, EQ, None, [("er", 0, E), ("lam", 0, 1)], [("cb", 0, 1)])
+            ts(V("cb", E - 1, E), V("er", E - 1, E), T.lamb[:, 0:1], None, EQ, None, [("er", 0, E), ("lamb", 0, 1)], [("cb", 1, 2)])
+            quant("qg", "sg", "gt", 0, 128, [("gt", 0, 512)])
+            ts(T.first[:, :], T.acc[:, 0:1], 0.5, 31.0, MUL, ADD, [("acc", 0, 1)], [("first", 0, 1)])
+            op("v", [("cb", 0, 2), ("ones", 0, 512), ("first", 0, 1)], [("t1", 0, E)], g.vector.tensor_tensor_scan,
+               V("t1", 0, E), V("ones", 0, E), O, T.first[:, 0:1], MUL, ADD)
+            tc(V("t1", E - 1, E), T.first[:, 0:1], [("first", 0, 1)], [("t1", E - 1, E)])
+            tt(V("t2", 0, E), V("t1", 0, E), O, MUL, [("t1", 0, E), ("cb", 0, 2)], [("t2", 0, E)])
+            ts(V("w6", 0, E), V("t2", 0, E), 3072.0, None, ADD, None, [("t2", 0, E)], [("w6", 0, E)])
+            d0, d1 = V("hl", 4 * OFF, 4 * (OFF + E), 4), V("hl", 4 * OFF + 1, 4 * (OFF + E), 4)
+            ts(d0, V("w6", 0, E), -3072.0, None, ADD, None, [("w6", 0, E)], [("hl", 0, 1)])
+            tt(d1, V("t2", 0, E), d0, SUB, [("t2", 0, E), ("hl", 0, 1)], [("hl", 1, 2)])
+            quant("qh", "sh", "hl", 0, E + 32, [("hl", 0, 8)])
+            mx(3, E + 32, "qg", "sg", 0, "qh", "sh", 0, E + 32)
+            tt(V("g1", 0, E), V("s1", 0, E), V("iof", 0, E), ADD, [("s1", 0, E), ("iof", 0, E)], [("g1", 0, E)])
+            wrap(lambda lo, hi: bank(3, lo, hi), [("b3", 0, 1)], "ka", "kb", "p3")
+            ts(V("pos", 0, 28), V("p3", 0, 28), 192.0, None, ADD, None, [("p3", 0, 28)], [("pos", 0, 28)])
+        else:
+            wrap(lambda lo, hi: V("kr", lo, hi), [("kr", 0, E + 32)], "ka", "kb", "own")
+
+            def row(c):
+                if not last:
+                    return K, KR
+                return V("d2", 16 * c + 16, 16 * c + 16 + E), [("d2", 16 * c + 16, 16 * c + 16 + E)]
+
+            for c in range(ns):
+                v, r = row(c)
+                j = c % 4
+                act(V("junk", E * j, E * j + E), v, SIGN, r + [("own", 0, 28)], [("junk%d" % j, 0, 1), ("acc", c, c + 1)],
+                    bias=T.own[:, c:c + 1], scale=-1.0, accum_out=T.acc[:, c:c + 1])
+            if last:
+                for q in range(1, 16):
+                    o = 112 * (q // 4) + q % 4
+                    tt(V("eq", o, 112 * (q // 4) + 112, 4), V("kr", OFF + q, OFF + E, 16), V("own", 0, 28), EQ, KR + [("own", 0, 28)], [("eq", 1000 + q, 1001 + q)])
+                quant("qq", "sq", "eq", 0, 212, [("eq", 0, 1016)])
+                for k in range(4):
+                    mx(3, 128, "qc", "cs", 128 * k, "qq", "sq", 28 * k, 28 * k + 128, k == 0, k == 3)
+            for k in range(nv):
+                v, r = row(ns + k)
+                ts(V("cb", E * k, E * k + E), v, T.own[:, ns + k:ns + k + 1], None, LT, None, r + [("own", 0, 28)], [("cb", k, k + 1)])
+            for k in range(nv):
+                op("v", [("cb", k, k + 1)], [("sc", k, k + 1)], g.vector.tensor_tensor_scan, V("sc", 224 * k, 224 * k + 224),
+                   V("cb", E * k, E * k + 224), V("cb", E * k + 224, E * k + E), -192.0, ADD, ADD)
+            cnt = V("sc", 223, 224 * nv, 224)
+            if not last:
+                ts(V("pos", ns, 28), cnt, 192.0, None, ADD, None, [("sc", 0, nv)], [("pos", ns, 28)])
+                ts(V("pos", 0, ns), V("acc", 0, ns), 0.5, 223.5, MUL, ADD, [("acc", 0, ns)], [("pos", 0, ns)])
+            else:
+                ts(V("posf", ns, 28), cnt, 191.0, None, ADD, None, [("sc", 0, nv)], [("posf", ns, 28)])
+                ts(V("posf", 0, ns), V("acc", 0, ns), 0.5, 223.0, MUL, ADD, [("acc", 0, ns)], [("posf", 0, ns)])
+                tt(V("posg", 0, 28), V("posf", 0, 28), bank(3, 0, 28), SUB, [("posf", 0, 28), ("b3", 0, 1)], [("posg", 0, 28)])
+                tc(V("pos", 0, 28), V("posg", 0, 28), [("posg", 0, 28)], [("pos", 0, 28)])
+        tc(V("ordr", OFF, OFF + E).indirect(V("pos", 0, 28)), V("iom", 0, E), [("iom", 0, E), ("pos", 0, 28)], [("ordr", OFF, OFF + E)])
+        wrap(lambda lo, hi: V("ordr", lo, hi), [("ordr", 0, E + 32)], "oa", "ob", "p3")
+        ts(V("ordl", 0, 28), V("p3", 0, 28), 192.0, None, ADD, None, [("p3", 0, 28)], [("ordl", 0, 28)])
+        for b in range(4):
+            act(V("vs", E * b, E * b + E), V("vp", E * b, E * b + E).indirect(V("ordl", 0, 28)), COPY,
+                [("vp%d" % b, 0, E), ("ordl", 0, 28)], [("vs%d" % b, 0, 1)])
+        if last:
+            act(V("ks", 1, 1 + E), K.indirect(V("ordl", 0, 28)), COPY, KR + [("ordl", 0, 28)], [("ks", 1, 1 + E)])
+        if t == 0:
+            tt(V("g1", 0, E), V("g1", 0, E), V("s2", 0, E), ADD, [("g1", 0, E), ("s2", 0, E)], [("g1", 0, E)])
+        elif t == 1:
+            fill("lr", E, E + 16, -256.0)
+            tt(V("lr", 0, E), K, V("iof", 0, E), SUB, KR + [("iof", 0, E)], [("lr", 0, E)])
+            act(V("s1", 0, E), V("lr", 0, E), IDEN, [("lr", 0, E)], [("s1", 0, E)], bias=1.0 - CENTER, scale=6562.0 / 512.0)
+            act(V("s2", 0, E), V("lr", 4, E + 4), COPY, [("lr", 0, E + 16)], [("s2", 0, E)], scale=1.0 / 256.0)
+        for b in range(4):
+            o = E * b
+            tt(V("mm", o + 1, o + E - 1), V("vs", o, o + E - 2), V("vs", o + 2, o + E), MAX, [("vs%d" % b, 0, 1)], [("mm%d" % b, 0, 1)])
+        ends = [("vs%d" % b, 0, 1) for b in range(4)]
+        tt(V("mm", 0, 4 * E, E), V("vs", 0, 4 * E, E), V("vs", 1, 4 * E, E), MAX, ends, [("mm%d" % b, 1, 2) for b in range(4)])
+        tt(V("mm", E - 1, 4 * E, E), V("vs", E - 1, 4 * E, E), V("vs", E - 2, 4 * E, E), MAX, ends, [("mm%d" % b, 2, 3) for b in range(4)])
+
+        def fused(b, lo, hi):
+            tt(V("zt", 4 * lo + b, 4 * hi, 4), V("mm", E * b, E * b + E).indirect(V("pos", lo // 16, hi // 16)), V("vp", E * b + lo, E * b + hi), ADD,
+               [("mm%d" % b, 0, 3), ("pos", 0, 28), ("vp%d" % b, lo, hi)], [("z%d" % b, lo, hi)])
+
+        def product(lo, hi, b0):
+            quant("qz", "sz", "zt", lo, hi, [("z%d" % b, lo, hi) for b in range(4)])
+            for b in range(4):
+                mx(b0 + b, hi - lo, "qw", "sw", 128 * b, "qz", "sz", lo, hi)
+
+        xn = "xt%d" % (t + 1)
+
+        def update(lo, hi, b0):
+            for b in range(4):
+                r = [("x32_%d" % b, lo, hi)]
+                tt(V("x32", C * b + lo, C * b + hi), bank(b0 + b, 0, hi - lo), V("x32", C * b + lo, C * b + hi), ADD, [("b%d" % (b0 + b), 0, 1)] + r, r)
+            for b in range(4):
+                o, i, W = V(xn, 4 * lo + b, 4 * hi, 4), V("x32", C * b + lo, C * b + hi), [("x%d_%d" % (t + 1, b), lo, hi)]
+                if b < 3:
+                    act(o, i, COPY, [("x32_%d" % b, lo, hi)], W, scale=0.03125)
+                else:
+                    ts(o, i, 0.03125, None, MUL, None, [("x32_%d" % b, lo, hi)], W)
+
+        def planes(lo, hi):
+            for b in range(4):
+                act(V("vp", E * b + lo, E * b + hi), V("x32", C * b + lo, C * b + hi), COPY, [("x32_%d" % b, lo, hi)], [("vp%d" % b, lo, hi)], scale=2.0 ** -6)
+
+        qn, sn = "qx%d" % (t + 1), "sx%d" % (t + 1)
+        for b in range(4):
+            fused(b, 0, 128)
+        product(0, 128, 0)
+        fused(0, 128, C)
+        update(0, 128, 0)
+        fused(1, 128, C)
+        quant(qn, sn, xn, 0, 128, xr(t + 1, 0, 128))
+        if not last:
+            send(t + 1)
+            mx(0, 128, "qur", "sur", 0, qn, sn, 0, 128)
+            planes(0, 128)
+        else:
+            dma("s", "dca", [(qn, 0, 128)], [], T.oc[:, 0:512], V(qn, 0, 128).bitcast(dt.uint8))
+            mx(0, 128, "qv", "sv", 0, qn, sn, 0, 128)
+            act(V("yr", 0, 128), bank(0, 0, 128), COPY, [("b0", 0, 1)], [("yr", 0, 128)])
+            dma("s", "dya", [("yr", 0, 128)], [], T.y[:, 0:128], T.yr[:, 0:128])
+        fused(2, 128, C)
+        fused(3, 128, C)
+        product(128, C, 4)
+        if t == 0:
+            fill("ar1", E, E + 16, 0.0)
+            fill("ar2", E, E + 16, 0.0)
+            for lo, hi in ((0, OFF), (OFF + E, E + 32)):
+                fill("kr", lo, hi, 0.0)
+            fill("eq", 0, 848, 0.0)
+            ts(T.behind[:, :], T.qi[:, :], T.pl[:, 0:1], 2.0, GT, MUL, [("qi", 0, 16), ("pl", 0, 1)], [("behind", 0, 16)])
+        elif t == 1:
+            tt(V("g1", 0, E), V("s1", 0, E), V("s2", 0, E), ADD, [("s1", 0, E), ("s2", 0, E)], [("g1", 0, E)])
+        else:
+            tt(V("eqs", 0, E), V("ks", 1, E + 1), V("ks", 0, E), EQ, [("ks", 0, E + 1)], [("eqs", 0, E)])
+            op("v", [("ones", 0, 512), ("eqs", 0, E)], [("rr", 0, E)], g.vector.tensor_tensor_scan, V("rr", 0, E), V("ones", 0, E), V("eqs", 0, E), 0.0, ADD, MUL)
+        update(128, C, 4)
+        quant(qn, sn, xn, 128, C, xr(t + 1, 128, C))
+        if t == 1:
+            quant("qc", "cs", "ct", 0, 512, [("ct", 0, 16)])
+            quant("qv", "sv", "vt", 0, 128, [("vt", 0, 128)])
+            fill("ks", 0, 8, -9.0e6)
+        if not last:
+            words(t + 1, 0, 0, 128, 0, 128)
+            planes(128, C)
+            if t == 0:
+                for q in range(16):
+                    o = 512 * (q // 4)
+                    act(T.ct[:, o + q % 4:o + 512:4], T.ident[:, :], COPY, [("ident", 0, 128), ("behind", 0, 16)], [("ct", q, q + 1)], scale=T.behind[:, q:q + 1])
+        else:
+            tt(V("lw", 0, E), V("iof", 0, E), V("rr", 0, E), SUB, [("iof", 0, E), ("rr", 0, E)], [("lw", 0, E)])
+
+    q, s = "qx%d" % NR, "sx%d" % NR
+    mx(1, C - 128, "qv", "sv", 0, q, s, 128, C)
+    dma("s", "dcb", [(q, 128, C)], [], T.oc[:, 512:1536], V(q, 128, C).bitcast(dt.uint8))
+    for k in range(4):
+        dma("s", "ds%d" % k, [(q, 0, C)], [], T.osc[4 * k:4 * k + 4, 0:C], T[s][32 * k:32 * k + 4, 0:C])
+    act(V("yr", 128, C), bank(1, 0, C - 128), COPY, [("b1", 0, 1)], [("yr", 128, C)])
+    dma("a", "dyb", [("yr", 128, C)], [], T.y[:, 128:C], T.yr[:, 128:C])
+    act(V("lvr", 0, E), V("lw", 0, E).indirect(V("pos", 0, 28)), COPY, [("lw", 0, E), ("pos", 0, 28)], [("lvr", 0, E)])
+    dma("s", "dlv", [("lvr", 0, E)], [], T.lv[:, :], T.lvr[0:128:16, 0:E])
+    for sem in count:
+        g.wait_ge(T.sem[sem], count[sem])
+    for sem in DMAS:
+        g.wait_ge(T.sem[sem], 16)
+    g.wait_ge(T.sem.left, 2 * NR * len(send_engines(core, prev)))

@@ -1,27 +1,29 @@
 from concourse.mybir import dt, AluOpType, ActivationFunctionType
 
 C, H, E, NR = 384, 64, 448, 3
-OFF = 16
-NS = (0, 16, 18)
+NV = (0, 11, 10)
+NE = (0, 22, 22)
+PL = 912
+BIG = 1.0e29
+CAP = 2.0 ** 25
+WHOLE = 12582912.0
 
 SCRATCH = {}
-for _k, _n in (("qu", 128), ("qur", 256), ("qv", 128), ("qw", 512), ("qe", 512), ("qc", 512), ("qz", C), ("qq", 212), ("qg", 128), ("qh", E + 32)):
+for _k, _n in (("qu", 128), ("qur", 256), ("qv", 128), ("qw", 512), ("qe", 512), ("qz", C), ("qg", 128), ("qh", E)):
     SCRATCH[_k] = ("sbuf", [128, _n], "float8_e4m3fn_x4")
-    SCRATCH[{"qc": "cs"}.get(_k, "s" + _k[1:])] = ("sbuf", [128, _n], "uint8")
-for _k, _n in (("ut", 512), ("vt", 512), ("et", 2048), ("ct", 2048), ("gt", 512), ("ga", 512), ("hl", 4 * (E + 32)), ("zt", 4 * C), ("vp", 4 * E),
-               ("x32", 4 * C), ("vs", 4 * E), ("mm", 4 * E), ("hb", 128), ("ident", 128), ("iom", E), ("ones", 512), ("t1", E), ("t2", E),
-               ("w5", E + 16), ("w6", E), ("er", E + 16), ("ar1", E + 16), ("ar2", E + 16), ("junk", 4 * E), ("cb", 16 * E), ("sc", 8 * E),
-               ("ordr", E + 32), ("oa", E), ("ob", E + 32), ("eq", 848), ("eqs", E)):
+    SCRATCH["s" + _k[1:]] = ("sbuf", [128, _n], "uint8")
+for _k, _n in (("ut", 512), ("vt", 512), ("et", 2048), ("gt", 512), ("hl", 4 * E), ("zt", 4 * C), ("vp", 4 * E), ("x32", 4 * C),
+               ("vs", 4 * PL), ("mm", 4 * PL), ("hb", 128), ("ident", 128), ("grp", 128), ("ones", E), ("t1", E), ("t2", E), ("w", E + 16),
+               ("w6", E), ("er", E + 16), ("junk", 4 * E), ("cb", 16 * E), ("sc", 8 * E), ("lane", E), ("cap", E), ("tri", E), ("hit", E),
+               ("hw", 4 * E), ("eq", E), ("eqs", E)):
     SCRATCH[_k] = ("sbuf", [128, _n], "bfloat16")
-for _k, _n in (("iof", E), ("ev", 1), ("od", 1), ("pl", 1), ("pq", 1), ("lama", 1), ("lam", 1), ("lamb", 1), ("lams", 1), ("first", 1),
-               ("qi", 16), ("behind", 16), ("lr", E + 16), ("al", E), ("ag", E), ("g1", E),
-               ("s1", E), ("s2", E), ("kr", E + 32), ("ka", E), ("kb", E + 32), ("ma", 28), ("mb", 28), ("o1", 28), ("o2", 28),
-               ("own", 28), ("acc", 28), ("posf", 28), ("posg", 28), ("p3", 28), ("d2", 2 * E), ("ks", E + 16), ("rr", E), ("lw", E),
-               ("lvr", E), ("yr", C)):
+for _k, _n in (("iof", E), ("iq", E), ("pl", 1), ("pq", 1), ("pg", 1), ("lama", 1), ("lam", 1), ("lamb", 1), ("lams", 1), ("acc0", 2),
+               ("hin", 4 * E), ("kr", 4 * E), ("held", E), ("own", 28), ("acc", 28), ("eq2", 28), ("posf", 28), ("d2", 2 * E),
+               ("ordr", E), ("held2", E), ("yl", E), ("ks", E + 16), ("dk", E), ("lw", E), ("lvr", E), ("yr", C)):
     SCRATCH[_k] = ("sbuf", [128, _n], "float32")
-for _k, _n in (("uo", 16), ("pin", 1), ("pod", 1), ("pla", 1), ("plq", 1)):
+for _k, _n in (("uo", 16), ("bo", 28), ("pin", 1), ("pla", 1), ("plq", 1), ("plg", 1)):
     SCRATCH[_k] = ("sbuf", [128, _n], "int32")
-for _k, _n in (("uo16", 16), ("pos", 28), ("ordl", 28)):
+for _k, _n in (("uo16", 16), ("bo16", 28), ("pos", 28), ("pos2", 28), ("ordl", 28)):
     SCRATCH[_k] = ("sbuf", [128, _n], "uint16")
 SCRATCH["ps"] = ("psum", [128, 4096], "float32")
 for _t in range(NR + 1):
@@ -31,10 +33,10 @@ for _t in range(NR + 1):
 DMAS = ["dxa", "dxb", "du", "dv", "dwc", "dws", "dlv", "dya", "dyb", "dca", "dcb"] + ["ds%d" % k for k in range(4)]
 SEMAPHORES = ["vec", "act", "ten", "pool", "left"] + ["arr%d" % t for t in range(NR)] + DMAS
 
-ADD, SUB, MUL, MAX = AluOpType.add, AluOpType.subtract, AluOpType.mult, AluOpType.max
+ADD, SUB, MUL, MAX, MIN = AluOpType.add, AluOpType.subtract, AluOpType.mult, AluOpType.max, AluOpType.min
 GT, LT, GE, EQ = AluOpType.is_gt, AluOpType.is_lt, AluOpType.is_ge, AluOpType.is_equal
+SHR, AND = AluOpType.logical_shift_right, AluOpType.bitwise_and
 COPY, IDEN, SIGN = ActivationFunctionType.Copy, ActivationFunctionType.Identity, ActivationFunctionType.Sign
-CENTER = 5380840.0
 
 
 def rank_program(g, core, T, topo):
@@ -53,14 +55,29 @@ def rank_program(g, core, T, topo):
     seen = {q: {} for q in queue}
     hist = {}
 
+    def V(name, lo, hi, step=1):
+        k = (hi - lo + step - 1) // step
+        mask = ((1 << (k * step)) - 1) // ((1 << step) - 1) << lo
+        return (T[name][:, lo:hi] if step == 1 else T[name][:, lo:hi:step], [(name, mask)])
+
+    def bank(k, lo, hi):
+        return (T.ps[:, 512 * k + lo:512 * k + hi], [("ps", 1 << k)])
+
+    def by(win, off):
+        return (win[0].indirect(off[0]), win[1], off[1])
+
+    def words32(v):
+        return (v[0].bitcast(dt.uint32), v[1])
+
+    def bytes8(v):
+        return (v[0].bitcast(dt.uint8), v[1])
+
     def waits(q, reads, writes):
         need = {}
         for regs, isw in ((reads, False), (writes, True)):
-            for name, lo, hi in regs:
-                for l, h, w, oq, sem, val in hist.get(name, ()):
-                    if l < hi and lo < h and (w or isw):
-                        if oq == q and isw and not w:
-                            continue
+            for name, mask in regs:
+                for m, w, oq, sem, val in hist.get(name, ()):
+                    if m & mask and (w or (oq != q and (isw or name == "ps"))):
                         need[sem] = max(need.get(sem, 0), val)
         for sem in sorted(need):
             if seen[q].get(sem, 0) < need[sem]:
@@ -68,341 +85,335 @@ def rank_program(g, core, T, topo):
                 seen[q][sem] = need[sem]
 
     def note(q, reads, writes, sem, val):
-        for name, lo, hi in writes:
-            hist[name] = [e for e in hist.get(name, ()) if not (lo <= e[0] and e[1] <= hi)] + [(lo, hi, True, q, sem, val)]
-        for name, lo, hi in reads:
-            hist.setdefault(name, []).append((lo, hi, False, q, sem, val))
+        for name, mask in writes:
+            hist[name] = [e for e in hist.get(name, ()) if e[0] & ~mask] + [(mask, True, q, sem, val)]
+        for name, mask in reads:
+            hist.setdefault(name, []).append((mask, False, q, sem, val))
 
-    def op(q, reads, writes, fn, *args, **kw):
+    def op(q, nout, fn, *args, **kw):
+        reads, writes = [], []
+        for k, a in list(enumerate(args)) + list(kw.items()):
+            if isinstance(a, tuple):
+                (writes if k == "accum_out" or (k in range(nout)) else reads).extend(a[1])
+                if len(a) == 3:
+                    reads.extend(a[2])
         waits(q, reads, writes)
         sem = semof[q]
-        fn(*args, **kw).then_inc(T.sem[sem], 1)
+        plain = lambda a: a[0] if isinstance(a, tuple) else a
+        fn(*[plain(a) for a in args], **{k: plain(a) for k, a in kw.items()}).then_inc(T.sem[sem], 1)
         count[sem] += 1
         note(q, reads, writes, sem, count[sem])
 
-    def dma(q, sem, reads, writes, out, in_):
+    def dma(q, sem, out, in_):
+        reads, writes = (in_[1] if isinstance(in_, tuple) else []), (out[1] if isinstance(out, tuple) else [])
         waits(q, reads, writes)
-        queue[q].dma_start(out, in_).then_inc(T.sem[sem], 16)
+        queue[q].dma_start(out[0] if writes else out, in_[0] if reads else in_).then_inc(T.sem[sem], 16)
         note("dma", reads, writes, sem, 16)
 
-    def V(name, lo, hi, step=1):
-        return T[name][:, lo:hi] if step == 1 else T[name][:, lo:hi:step]
+    def tt(out, a, b, o):
+        op("v", 1, g.vector.tensor_tensor, out, a, b, o)
 
-    def tt(out, a, b, o, R, W):
-        op("v", R, W, g.vector.tensor_tensor, out, a, b, o)
+    def ts(out, a, s1, s2, *o):
+        op("v", 1, g.vector.tensor_scalar, out, a, s1, s2, *o)
 
-    def ts(out, a, s1, s2, o0, o1, R, W):
-        if o1 is None:
-            op("v", R, W, g.vector.tensor_scalar, out, a, s1, None, o0)
-        else:
-            op("v", R, W, g.vector.tensor_scalar, out, a, s1, s2, o0, o1)
+    def tc(out, in_):
+        op("v", 1, g.vector.tensor_copy, out, in_)
 
-    def tc(out, in_, R, W):
-        op("v", R, W, g.vector.tensor_copy, out, in_)
+    def scan(out, d0, d1, init, o0, o1):
+        op("v", 1, g.vector.tensor_tensor_scan, out, d0, d1, init, o0, o1)
 
-    def act(out, in_, f, R, W, **kw):
-        op("a", R, W, g.scalar.activation, out, in_, f, **kw)
+    def act(out, in_, f, **kw):
+        op("a", 1, g.scalar.activation, out, in_, f, **kw)
 
-    def fill(name, lo, hi, c):
-        op("v", [], [(name, lo, hi)], g.vector.memset, V(name, lo, hi), c)
+    def fill(v, c):
+        op("v", 1, g.vector.memset, v, c)
 
-    def quant(codes, plane, src, lo, hi, R):
-        op("v", R, [(codes, lo, hi)], g.vector.quantize_mx, V(codes, lo, hi), V(plane, lo, hi), V(src, 4 * lo, 4 * hi))
+    def const(v, k, c):
+        act(v, V("ones", 0, k), COPY, scale=c)
 
-    def mx(bank, cols, l, ls, llo, r, rs, rlo, rhi, start=True, stop=True):
-        op("t", [(l, llo, llo + 128), (r, rlo, rhi)], [("b%d" % bank, 0, 512)], g.tensor.matmul_mx,
-           T.ps[:, 512 * bank:512 * bank + cols], V(l, llo, llo + 128), V(ls, llo, llo + 128),
-           V(r, rlo, rhi), V(rs, rlo, rhi), start, stop)
+    def iota(v, pattern, base, mult, **kw):
+        op("g", 1, g.iota, v, pattern, base, mult, **kw)
 
-    def bank(k, lo, hi):
-        return T.ps[:, 512 * k + lo:512 * k + hi]
+    def quant(codes, src, lo, hi):
+        op("v", 2, g.vector.quantize_mx, V(codes, lo, hi), V("s" + codes[1:], lo, hi), V(src, 4 * lo, 4 * hi))
+
+    def mx(k, l, llo, r, rlo, rhi):
+        op("t", 1, g.tensor.matmul_mx, bank(k, 0, rhi - rlo), V(l, llo, llo + 128), V("s" + l[1:], llo, llo + 128),
+           V(r, rlo, rhi), V("s" + r[1:], rlo, rhi), True, True)
 
     def send(t):
-        waits("g", [("qx%d" % t, 0, H)], [])
+        q, s = "qx%d" % t, "sx%d" % t
+        waits("g", V(q, 0, H)[1] + V(s, 0, H)[1], [])
         rid, pid = topo.addr(prev)[0], topo.addr(prev)[1]
         m = 0
         for e in send_engines(core, prev):
             m |= 1 << e
-        q, s = "qx%d" % t, "sx%d" % t
-        g.remote_dma(V(q, C, E).bitcast(dt.uint8), V(q, 0, H).bitcast(dt.uint8), T.sem["arr%d" % t], T.sem.left, pid, rid, m)
-        g.remote_dma(V(s, C, E), V(s, 0, H), T.sem["arr%d" % t], T.sem.left, pid, rid, m)
-        note("remote", [], [(q, C, E)], "arr%d" % t, 2 * len(send_engines(nxt, core)))
+        g.remote_dma(bytes8(V(q, C, E))[0], bytes8(V(q, 0, H))[0], T.sem["arr%d" % t], T.sem.left, pid, rid, m)
+        g.remote_dma(V(s, C, E)[0], V(s, 0, H)[0], T.sem["arr%d" % t], T.sem.left, pid, rid, m)
+        note("remote", [], V(q, C, E)[1] + V(s, C, E)[1], "arr%d" % t, 2 * len(send_engines(nxt, core)))
 
-    xr = lambda t, lo, hi: [("x%d_%d" % (t, b), lo, hi) for b in range(4)]
-    dma("s", "dxa", [], xr(0, 0, 128), T.xt0[:, 0:512], T.x[:, 0:512])
-    dma("a", "du", [], [("ut", 0, 128)], T.ut[:, :], T.u[:, :])
-    dma("s", "dxb", [], xr(0, 128, C), T.xt0[:, 512:1536], T.x[:, 512:1536])
-    dma("s", "dwc", [], [("qw", 0, 512)], T.qw[:, 0:512].bitcast(dt.uint8), T.wc[:, :])
-    dma("s", "dws", [], [("qw", 0, 512)], T.sw[:, :], T.ws[:, :])
-    dma("a", "dv", [], [("vt", 0, 128)], T.vt[:, :], T.v[:, :])
-    hist["qw"] = [(0, 512, True, "dma", "dwc", 16), (0, 512, True, "dma", "dws", 16)]
-    fill("hb", 0, 128, 0.5)
-    op("g", [], [("uo", 0, 16)], g.iota, T.uo[:, :], [[1, 2], [16, 8]], 0, 0)
-    op("g", [], [("pin", 0, 1)], g.iota, T.pin[:, :], [[0, 1]], 0, 1)
-    op("g", [], [("qi", 0, 16)], g.iota, T.qi[:, :], [[1, 16]], 0, 0, allow_small_or_imprecise_dtypes=True)
-    op("g", [("hb", 0, 128)], [("ident", 0, 128)], g.affine_select, T.ident[:, :], T.hb[:, :], [[-1, 128]], EQ, 0.0, 0, 1)
-    fill("ones", 0, 512, 1.0)
-    fill("w5", E, E + 16, -512.0)
-    fill("er", E, E + 16, -256.0)
-    for lo, hi in ((0, OFF), (OFF + E, E + 32)):
-        fill("ordr", lo, hi, 0.0)
-    tc(T.uo16[:, :], T.uo[:, :], [("uo", 0, 16)], [("uo16", 0, 16)])
-    for nm, a, b in (("pla", 15, None), ("plq", 2, 3), ("pod", 4, 1)):
-        if b is None:
-            op("v", [("pin", 0, 1)], [(nm, 0, 1)], g.vector.tensor_scalar, T[nm][:, :], T.pin[:, :], a, b, AluOpType.bitwise_and)
-        else:
-            op("v", [("pin", 0, 1)], [(nm, 0, 1)], g.vector.tensor_scalar, T[nm][:, :], T.pin[:, :], a, b, AluOpType.logical_shift_right, AluOpType.bitwise_and)
-    for nm, src in (("pl", "pla"), ("pq", "plq"), ("od", "pod")):
-        tc(T[nm][:, :], T[src][:, :], [(src, 0, 1)], [(nm, 0, 1)])
-    ts(T.ev[:, :], T.od[:, :], -1.0, 1.0, MUL, ADD, [("od", 0, 1)], [("ev", 0, 1)])
-    ts(T.lama[:, :], T.pq[:, :], 512.0, 512.0, MUL, ADD, [("pq", 0, 1)], [("lama", 0, 1)])
-    ts(T.lam[:, :], T.pl[:, :], 512.0, T.lama[:, 0:1], MUL, ADD, [("pl", 0, 1), ("lama", 0, 1)], [("lam", 0, 1)])
-    for nm, c in (("lamb", -512.0), ("lams", -256.0)):
-        ts(T[nm][:, :], T.lam[:, :], c, None, ADD, None, [("lam", 0, 1)], [(nm, 0, 1)])
-    fill("et", 0, 2048, 0.0)
+    def hold(out, row):
+        scan(V(out, 0, E), row, V("cap", 0, E), 0.0, MAX, MUL)
+
+    def ends(name, lo=0, hi=28):
+        return V(name, 16 * lo + 15, 16 * hi, 16)
+
+    FL = {"allow_small_or_imprecise_dtypes": True}
+    dma("s", "dxa", V("xt0", 0, 512), T.x[:, 0:512])
+    dma("a", "du", V("ut", 0, 512), T.u[:, :])
+    dma("s", "dxb", V("xt0", 512, 1536), T.x[:, 512:1536])
+    fill(V("hb", 0, 128), 0.5)
+    iota(V("pin", 0, 1), [[0, 1]], 0, 1)
+    op("g", 1, g.affine_select, V("ident", 0, 128), V("hb", 0, 128), [[-1, 128]], EQ, 0.0, 0, 1)
+    iota(V("uo", 0, 16), [[1, 2], [16, 8]], 0, 0)
+    iota(V("lane", 0, E), [[0, 28], [1, 16]], 0, 0, **FL)
+    iota(V("grp", 0, 128), [[1, 8], [0, 16]], 0, 0, **FL)
+    fill(V("ones", 0, E), 1.0)
+    fill(V("et", 0, 2048), 0.0)
+    ts(V("pla", 0, 1), V("pin", 0, 1), 15, None, AND)
+    ts(V("plq", 0, 1), V("pin", 0, 1), 2, 3, SHR, AND)
+    ts(V("plg", 0, 1), V("pin", 0, 1), 4, None, SHR)
+    for nm, src in (("pl", "pla"), ("pq", "plq"), ("pg", "plg")):
+        tc(V(nm, 0, 1), V(src, 0, 1))
+    tc(V("uo16", 0, 16), V("uo", 0, 16))
     for b in range(4):
-        tc(T.et[:, 512 * b + b:512 * b + 512:4], T.ident[:, :], [("ident", 0, 128)], [("et", 512 * b, 512 * b + 512)])
-    quant("qx0", "sx0", "xt0", 0, 128, xr(0, 0, 128))
+        act(V("et", 512 * b + b, 512 * b + 512, 4), V("ident", 0, 128), COPY)
+    const(V("w", E, E + 16), 16, -0.5)
+    const(V("er", E, E + 16), 16, -0.75)
+    const(V("hl", 3, 4 * E, 4), E, 0.0)
+    act(V("lama", 0, 1), V("pq", 0, 1), IDEN, scale=0.5, bias=0.5)
+    act(V("lam", 0, 1), V("pl", 0, 1), IDEN, bias=V("lama", 0, 1))
+    act(V("lamb", 0, 1), V("lam", 0, 1), IDEN, bias=-0.5)
+    act(V("lams", 0, 1), V("lam", 0, 1), IDEN, bias=-0.25)
+    quant("qx0", "xt0", 0, 128)
     send(0)
-    op("g", [("ones", 0, 512)], [("ga", 0, 512)], g.affine_select, T.ga[:, :], T.ones[:, :], [[-16, 8], [0, 64]], GE, 0.0, 0, 1)
-    op("g", [("ga", 0, 512)], [("gt", 0, 512)], g.affine_select, T.gt[:, :], T.ga[:, :], [[16, 8], [0, 64]], GE, 0.0, 15, -1)
-    op("g", [], [("iom", 0, E)], g.iota, T.iom[:, :], [[1, E]], -192, 0, allow_small_or_imprecise_dtypes=True)
-    op("g", [], [("iof", 0, E)], g.iota, T.iof[:, :], [[1, E]], 0, 0, allow_small_or_imprecise_dtypes=True)
-    quant("qu", "su", "ut", 0, 128, [("ut", 0, 128)])
-    op("v", [("qu", 0, 128), ("uo16", 0, 16)], [("qur", 0, 256)], g.vector.tensor_copy,
-       T.qur[:, 0:256].bitcast(dt.uint32), T.qu[:, 0:128].bitcast(dt.uint32).indirect(T.uo16[:, 0:16]))
-    act(V("hl", 2, 1920, 4), V("ones", 0, 480), COPY, [("ones", 0, 512)], [("hl", 2, 3)], scale=0.0)
-    act(V("hl", 3, 1920, 4), V("ones", 0, 480), COPY, [("ones", 0, 512)], [("hl", 3, 4)], scale=0.0)
-    op("a", [("qu", 0, 128), ("uo16", 0, 16)], [("qurs", 0, 256)], g.scalar.activation,
-       T.sur[:, 0:256], T.su[:, 0:128].indirect(T.uo16[:, 0:16]), COPY)
-    for b in range(2):
-        act(V("hl", b, 64, 4), V("ones", 0, 16), COPY, [("ones", 0, 512)], [("hl", 4 + b, 5 + b)], scale=0.0)
-        act(V("hl", 4 * (OFF + E) + b, 1920, 4), V("ones", 0, 16), COPY, [("ones", 0, 512)], [("hl", 6 + b, 7 + b)], scale=0.0)
-    quant("qx0", "sx0", "xt0", 128, C, xr(0, 128, C))
-    quant("qe", "se", "et", 0, 512, [("et", 0, 2048)])
-    for b in range(4):
-        act(V("vp", E * b, E * b + C), V("xt0", b, 4 * C, 4), COPY, [("x0_%d" % b, 0, C)], [("vp%d" % b, 0, C)], scale=0.5)
-    waits("t", [("qurs", 0, 256)], [])
+    iota(V("iof", 0, E), [[1, E]], 1, 0, **FL)
+    iota(V("bo", 0, 28), [[1, 28]], 0, 0)
+    quant("qu", "ut", 0, 128)
+    tc(words32(V("qur", 0, 256)), by(words32(V("qu", 0, 128)), V("uo16", 0, 16)))
+    act(V("sur", 0, 256), by(V("su", 0, 128), V("uo16", 0, 16)), COPY)
+    quant("qx0", "xt0", 128, C)
+    quant("qe", "et", 0, 512)
+    waits("s", V("qx0", C, E)[1], [])
+    dma("s", "dwc", bytes8(V("qw", 0, 512)), T.wc[:, :])
+    dma("s", "dws", V("sw", 0, 512), T.ws[:, :])
+    dma("s", "dv", V("vt", 0, 512), T.v[:, :])
 
-    def wrap(row, reg, ta, tb, out):
-        op("v", reg, [(ta, 0, E)], g.vector.transpose, V(ta, 0, E), row(OFF, OFF + E))
-        op("v", reg, [(tb, 0, E)], g.vector.transpose, V(tb, 0, E + 32), row(0, E + 32))
-        tt(V("o1", 0, 28), V(ta, 0, E, 16), V("ma", 0, 28), MUL, [(ta, 0, E), ("ma", 0, 2)], [("o1", 0, 28)])
-        tt(V("o2", 0, 28), V(tb, 16, E + 16, 16), V("mb", 0, 28), MUL, [(tb, 0, E), ("mb", 0, 2)], [("o2", 0, 28)])
-        tt(V(out, 0, 28), V("o1", 0, 28), V("o2", 0, 28), ADD, [("o1", 0, 28), ("o2", 0, 28)], [(out, 0, 28)])
+    def words0(k, sl, lo, hi, klo, khi):
+        ts(V("t1", lo, hi), bank(k, sl, sl + hi - lo), 0.0, 2.0, GT, MUL)
+        ts(V("t2", lo, hi), bank(k + 1, sl, sl + hi - lo), 0.0, None, GT)
+        tt(V("w", lo, hi), V("t1", lo, hi), V("t2", lo, hi), ADD)
+        ts(V("w6", klo, khi), V("w", klo, khi), 4.5, 0.5, MUL, ADD)
+        tt(V("er", klo, khi), V("w6", klo, khi), V("w", klo + 1, khi + 1), ADD)
 
-    def words0(k, sl, sh, lo, hi, klo, khi):
-        ts(V("t1", lo, hi), bank(k, sl, sh), 0.0, 1024.0, GT, MUL, [("b%d" % k, 0, 1)], [("t1", lo, hi)])
-        ts(V("t2", lo, hi), bank(k + 1, sl, sh), 0.0, 512.0, GT, MUL, [("b%d" % (k + 1), 0, 1)], [("t2", lo, hi)])
-        tt(V("w5", lo, hi), V("t1", lo, hi), V("t2", lo, hi), ADD, [("t1", lo, hi), ("t2", lo, hi)], [("w5", lo, hi)])
-        ts(V("w6", klo, khi), V("w5", klo, khi), 5.0, 512.0, MUL, ADD, [("w5", klo, khi)], [("w6", klo, khi)])
-        tt(V("er", klo, khi), V("w6", klo, khi), V("w5", klo + 1, khi + 1), ADD, [("w6", klo, khi), ("w5", klo + 1, khi + 1)], [("er", klo, khi)])
-
-    def words(t, k, sl, sh, lo, hi):
+    def words(t, k, lo, hi):
         d = 2 ** t
-        ar, klo, khi = "ar%d" % t, max(lo - d, 0), hi if hi == E else hi - d
-        unit, fac = ((512.0, 41.0), (1.0, 3281.0))[t - 1]
-        ts(V(ar, lo, hi), bank(k, sl, sh), 0.0, unit, GT, MUL, [("b%d" % k, 0, 1)], [(ar, lo, hi)])
-        ts(V("al", klo, khi), V(ar, klo, khi), fac, None, MUL, None, [(ar, klo, khi)], [("al", klo, khi)])
-        tt(V("ag", klo, khi), V("al", klo, khi), V("g1", klo, khi), ADD, [("al", klo, khi), ("g1", klo, khi)], [("ag", klo, khi)])
-        tt(V("kr", OFF + klo, OFF + khi), V("ag", klo, khi), V(ar, klo + d, khi + d), ADD,
-           [("ag", klo, khi), (ar, klo + d, khi + d)], [("kr", OFF + klo, OFF + khi)])
+        top = hi - 1 if (t, hi) == (1, E) else hi
+        klo, khi = max(lo - d, 0), hi if hi == E else hi - d
+        ts(V("hin", 4 * lo + 1, 4 * top, 4), bank(k, 0, top - lo), 0.0, 2.0, GT, MUL)
+        act(V("hin", 4 * klo + 3, 4 * (top - d), 4), bank(k + 1, klo + d - lo, top - lo), SIGN, bias=-1.0e-36)
+        scan(V("kr", 4 * klo, 4 * khi), V("hw", 0, 4 * (khi - klo)), V("hin", 4 * klo, 4 * khi), 0.0, MUL, ADD)
         if t == NR - 1:
-            for o, e in ((0, 0.5), (E, -0.5)):
-                act(V("d2", o + klo, o + khi), V("kr", OFF + klo, OFF + khi), IDEN, [("kr", OFF + klo, OFF + khi)], [("d2", o + klo, o + khi)], bias=e)
+            for o, e in ((0, 1.0), (E, -1.0)):
+                act(V("d2", o + klo, o + khi), V("kr", 4 * klo + 3, 4 * khi, 4), IDEN, bias=e)
 
-    K = V("kr", OFF, OFF + E)
-    KR = [("kr", OFF, OFF + E)]
+    K = V("kr", 3, 4 * E, 4)
 
     for t in range(NR):
-        qx, sx = "qx%d" % t, "sx%d" % t
+        qx = "qx%d" % t
         last = t == NR - 1
         if t == 0:
-            mx(0, C, "qur", "sur", 0, qx, sx, 0, C)
-            mx(1, C, "qur", "sur", 128, qx, sx, 0, C)
-            words0(0, 0, C, 0, C, 0, C - 1)
-            for nm, a, b in (("ma", "ev", "od"), ("mb", "od", "ev")):
-                ts(V(nm, 0, 28, 2), V("ones", 0, 14), T[a][:, 0:1], None, MUL, None, [("ones", 0, 512), (a, 0, 1)], [(nm, 0, 1)])
-                ts(V(nm, 1, 28, 2), V("ones", 0, 14), T[b][:, 0:1], None, MUL, None, [("ones", 0, 512), (b, 0, 1)], [(nm, 1, 2)])
-            mx(2, 128, "qur", "sur", 0, qx, sx, E - 128, E)
-            mx(3, 128, "qur", "sur", 128, qx, sx, E - 128, E)
-        else:
-            mx(1, E - 128, "qur", "sur", 0, qx, sx, 128, E)
-        for b in range(4):
-            mx(4 + b, 128, "qe", "se", 128 * b, qx, sx, E - 128, E)
-        if t == 0:
-            words0(2, 64, 128, C, E, C - 1, E)
-            act(V("junk", 0, E), V("er", 0, E), SIGN, [("er", 0, E), ("lams", 0, 1)], [("junk0", 0, 1), ("acc", 0, 1)],
-                bias=T.lams[:, 0:1], scale=-1.0, accum_out=T.acc[:, 0:1])
-        else:
-            words(t, 1, 0, E - 128, 128, E)
-        for b in range(4):
-            act(V("vp", E * b + C, E * b + E), bank(4 + b, 64, 128), COPY, [("b%d" % (4 + b), 0, 1)], [("vp%d" % b, C, E)])
-        ns = NS[t]
-        nv = 28 - ns
-        if t == 0:
-            act(V("s1", 0, E), V("er", 0, E), IDEN, [("er", 0, E)], [("s1", 0, E)], bias=512.0, scale=82.0)
-            act(V("s2", 0, E), V("er", 2, E + 2), COPY, [("er", 0, E + 16)], [("s2", 0, E)], scale=2.0)
+            mx(0, "qur", 0, qx, 0, C)
+            mx(1, "qur", 128, qx, 0, C)
+            words0(0, 0, 0, C, 0, C - 1)
+            act(V("junk", 0, C - 1), V("er", 0, C - 1), SIGN, bias=V("lams", 0, 1), scale=-1.0, accum_out=V("acc0", 0, 1))
+            O = lambda lo, hi: V("hl", 4 * lo + 2, 4 * hi, 4)
+            ts(O(0, C - 1), V("er", 0, C - 1), V("lam", 0, 1), None, EQ)
+            ts(V("tri", 0, E), V("lane", 0, E), V("pl", 0, 1), None, GT)
+            ts(V("hit", 0, E), V("lane", 0, E), V("pl", 0, 1), CAP, EQ, MUL)
+            for b, c in enumerate((1.0, 1.0, 256.0, 0.0)):
+                ts(V("gt", b, 512, 4), V("grp", 0, 128), V("pg", 0, 1), c, EQ, MUL)
+            act(V("acc0", 0, 1), V("acc0", 0, 1), IDEN, scale=0.5, bias=31.0)
+            tt(V("cap", 0, E), V("tri", 0, E), V("hit", 0, E), ADD)
+            ts(ends("cap"), ends("cap"), -1.0 / CAP, None, MUL)
+            quant("qg", "gt", 0, 128)
+            mx(2, "qur", 0, qx, E - 128, E)
+            mx(3, "qur", 128, qx, E - 128, E)
             for b in range(4):
-                act(V("x32", C * b, C * b + C), V("xt0", b, 4 * C, 4), COPY, [("x0_%d" % b, 0, C)], [("x32_%d" % b, 0, C)], scale=32.0)
-            O = V("cb", 0, E)
-            ts(V("cb", 0, E - 1), V("er", 0, E - 1), T.lam[:, 0:1], None, EQ, None, [("er", 0, E), ("lam", 0, 1)], [("cb", 0, 1)])
-            ts(V("cb", E - 1, E), V("er", E - 1, E), T.lamb[:, 0:1], None, EQ, None, [("er", 0, E), ("lamb", 0, 1)], [("cb", 1, 2)])
-            quant("qg", "sg", "gt", 0, 128, [("gt", 0, 512)])
-            ts(T.first[:, :], T.acc[:, 0:1], 0.5, 31.0, MUL, ADD, [("acc", 0, 1)], [("first", 0, 1)])
-            op("v", [("cb", 0, 2), ("ones", 0, 512), ("first", 0, 1)], [("t1", 0, E)], g.vector.tensor_tensor_scan,
-               V("t1", 0, E), V("ones", 0, E), O, T.first[:, 0:1], MUL, ADD)
-            tc(V("t1", E - 1, E), T.first[:, 0:1], [("first", 0, 1)], [("t1", E - 1, E)])
-            tt(V("t2", 0, E), V("t1", 0, E), O, MUL, [("t1", 0, E), ("cb", 0, 2)], [("t2", 0, E)])
-            ts(V("w6", 0, E), V("t2", 0, E), 3072.0, None, ADD, None, [("t2", 0, E)], [("w6", 0, E)])
-            d0, d1 = V("hl", 4 * OFF, 4 * (OFF + E), 4), V("hl", 4 * OFF + 1, 4 * (OFF + E), 4)
-            ts(d0, V("w6", 0, E), -3072.0, None, ADD, None, [("w6", 0, E)], [("hl", 0, 1)])
-            tt(d1, V("t2", 0, E), d0, SUB, [("t2", 0, E), ("hl", 0, 1)], [("hl", 1, 2)])
-            quant("qh", "sh", "hl", 0, E + 32, [("hl", 0, 8)])
-            mx(3, E + 32, "qg", "sg", 0, "qh", "sh", 0, E + 32)
-            tt(V("g1", 0, E), V("s1", 0, E), V("iof", 0, E), ADD, [("s1", 0, E), ("iof", 0, E)], [("g1", 0, E)])
-            wrap(lambda lo, hi: bank(3, lo, hi), [("b3", 0, 1)], "ka", "kb", "p3")
-            ts(V("pos", 0, 28), V("p3", 0, 28), 192.0, None, ADD, None, [("p3", 0, 28)], [("pos", 0, 28)])
+                act(V("vp", E * b, E * b + C), V("xt0", b, 4 * C, 4), COPY, scale=0.5)
         else:
-            wrap(lambda lo, hi: V("kr", lo, hi), [("kr", 0, E + 32)], "ka", "kb", "own")
-
-            def row(c):
-                if not last:
-                    return K, KR
-                return V("d2", 16 * c + 16, 16 * c + 16 + E), [("d2", 16 * c + 16, 16 * c + 16 + E)]
-
-            for c in range(ns):
-                v, r = row(c)
-                j = c % 4
-                act(V("junk", E * j, E * j + E), v, SIGN, r + [("own", 0, 28)], [("junk%d" % j, 0, 1), ("acc", c, c + 1)],
-                    bias=T.own[:, c:c + 1], scale=-1.0, accum_out=T.acc[:, c:c + 1])
-            if last:
-                for q in range(1, 16):
-                    o = 112 * (q // 4) + q % 4
-                    tt(V("eq", o, 112 * (q // 4) + 112, 4), V("kr", OFF + q, OFF + E, 16), V("own", 0, 28), EQ, KR + [("own", 0, 28)], [("eq", 1000 + q, 1001 + q)])
-                quant("qq", "sq", "eq", 0, 212, [("eq", 0, 1016)])
-                for k in range(4):
-                    mx(3, 128, "qc", "cs", 128 * k, "qq", "sq", 28 * k, 28 * k + 128, k == 0, k == 3)
-            for k in range(nv):
-                v, r = row(ns + k)
-                ts(V("cb", E * k, E * k + E), v, T.own[:, ns + k:ns + k + 1], None, LT, None, r + [("own", 0, 28)], [("cb", k, k + 1)])
-            for k in range(nv):
-                op("v", [("cb", k, k + 1)], [("sc", k, k + 1)], g.vector.tensor_tensor_scan, V("sc", 224 * k, 224 * k + 224),
-                   V("cb", E * k, E * k + 224), V("cb", E * k + 224, E * k + E), -192.0, ADD, ADD)
-            cnt = V("sc", 223, 224 * nv, 224)
-            if not last:
-                ts(V("pos", ns, 28), cnt, 192.0, None, ADD, None, [("sc", 0, nv)], [("pos", ns, 28)])
-                ts(V("pos", 0, ns), V("acc", 0, ns), 0.5, 223.5, MUL, ADD, [("acc", 0, ns)], [("pos", 0, ns)])
-            else:
-                ts(V("posf", ns, 28), cnt, 191.0, None, ADD, None, [("sc", 0, nv)], [("posf", ns, 28)])
-                ts(V("posf", 0, ns), V("acc", 0, ns), 0.5, 223.0, MUL, ADD, [("acc", 0, ns)], [("posf", 0, ns)])
-                tt(V("posg", 0, 28), V("posf", 0, 28), bank(3, 0, 28), SUB, [("posf", 0, 28), ("b3", 0, 1)], [("posg", 0, 28)])
-                tc(V("pos", 0, 28), V("posg", 0, 28), [("posg", 0, 28)], [("pos", 0, 28)])
-        tc(V("ordr", OFF, OFF + E).indirect(V("pos", 0, 28)), V("iom", 0, E), [("iom", 0, E), ("pos", 0, 28)], [("ordr", OFF, OFF + E)])
-        wrap(lambda lo, hi: V("ordr", lo, hi), [("ordr", 0, E + 32)], "oa", "ob", "p3")
-        ts(V("ordl", 0, 28), V("p3", 0, 28), 192.0, None, ADD, None, [("p3", 0, 28)], [("ordl", 0, 28)])
+            mx(2, "qur", 0, qx, 128, E)
+            mx(3, "qur", 0, qx, 128, E)
         for b in range(4):
-            act(V("vs", E * b, E * b + E), V("vp", E * b, E * b + E).indirect(V("ordl", 0, 28)), COPY,
-                [("vp%d" % b, 0, E), ("ordl", 0, 28)], [("vs%d" % b, 0, 1)])
-        if last:
-            act(V("ks", 1, 1 + E), K.indirect(V("ordl", 0, 28)), COPY, KR + [("ordl", 0, 28)], [("ks", 1, 1 + E)])
+            mx(4 + b, "qe", 128 * b, qx, E - 128, E)
         if t == 0:
-            tt(V("g1", 0, E), V("g1", 0, E), V("s2", 0, E), ADD, [("g1", 0, E), ("s2", 0, E)], [("g1", 0, E)])
-        elif t == 1:
-            fill("lr", E, E + 16, -256.0)
-            tt(V("lr", 0, E), K, V("iof", 0, E), SUB, KR + [("iof", 0, E)], [("lr", 0, E)])
-            act(V("s1", 0, E), V("lr", 0, E), IDEN, [("lr", 0, E)], [("s1", 0, E)], bias=1.0 - CENTER, scale=6562.0 / 512.0)
-            act(V("s2", 0, E), V("lr", 4, E + 4), COPY, [("lr", 0, E + 16)], [("s2", 0, E)], scale=1.0 / 256.0)
+            words0(2, 64, C, E, C - 1, E)
+            act(V("junk", E, E + 65), V("er", C - 1, E), SIGN, bias=V("lams", 0, 1), scale=-1.0, accum_out=V("acc0", 1, 2))
+        else:
+            words(t, 2, 128, E)
+
+        def halo_planes():
+            for b in range(4):
+                act(V("vp", E * b + C, E * b + E), bank(4 + b, 64, 128), COPY)
+
+        def scatter(lo, hi):
+            tc(by(V("ordr", 0, E), V("pos", lo, hi)), V("iof", 16 * lo, 16 * hi))
+
+        nv, ne = NV[t], NE[t]
+        if t == 0:
+            halo_planes()
+            ts(O(C - 1, E - 1), V("er", C - 1, E - 1), V("lam", 0, 1), None, EQ)
+            ts(O(E - 1, E), V("er", E - 1, E), V("lamb", 0, 1), None, EQ)
+            ts(V("t1", E - 1, E), V("acc0", 1, 2), 0.5, V("acc0", 0, 1), MUL, ADD)
+            scan(V("t1", 0, E - 1), V("ones", 0, E - 1), O(0, E - 1), V("t1", E - 1, E), MUL, ADD)
+            tt(V("t2", 0, E), V("t1", 0, E), O(0, E), MUL)
+            ts(V("hl", 0, 4 * E, 4), V("t2", 0, E), 16 * WHOLE, -16 * WHOLE, ADD, ADD)
+            tt(V("hl", 1, 4 * E, 4), V("t2", 0, E), V("hl", 0, 4 * E, 4), SUB)
+            quant("qh", "hl", 0, E)
+            mx(3, "qg", 0, "qh", 0, E)
+            for b in range(4):
+                const(V("vs", PL * b, PL * b + 896, 2), E, BIG)
+                const(V("vs", PL * b + 896, PL * b + 904, 2), 4, BIG)
+            for b in range(4):
+                act(V("x32", C * b, C * b + C), V("xt0", b, 4 * C, 4), COPY, scale=32.0)
+            hold("held", bank(3, 0, E))
+            ts(V("pos", 0, 28), ends("held"), -1.0, -64.0, MUL, ADD)
+            scatter(0, 28)
+        else:
+            hold("held", K)
+            halo_planes()
+            row = lambda c, lo=0, hi=E: V("d2", 16 * c + 16, 16 * c + 16 + E) if last else K
+            for c in range(nv, 28):
+                act(V("junk", E * (c % 4), E * (c % 4) + E), row(c), SIGN, bias=ends("held", c, c + 1), accum_out=V("acc", c, c + 1))
+            if last:
+                ts(V("own", 0, 28), ends("held"), -1.0, None, MUL)
+                tt(V("eq", 0, E), by(V("own", 0, 28), V("bo16", 0, 28)), K, EQ)
+                scan(V("eqs", 0, E), V("eq", 0, E), V("tri", 0, E), 0.0, ADD, MUL)
+            for c in range(nv):
+                if last:
+                    ts(V("cb", E * c, E * c + E), row(c), V("own", c, c + 1), -0.5, GE, ADD)
+                else:
+                    ts(V("cb", E * c, E * c + E), row(c), ends("held", c, c + 1), 0.0, ADD, LT)
+            if last:
+                ts(V("eq2", 0, 28), ends("eqs"), 2.0, None, MUL)
+            for c in range(nv):
+                scan(V("sc", 224 * c, 224 * c + 224), V("cb", E * c, E * c + 224), V("cb", E * c + 224, E * c + E),
+                     ends("eqs", c, c + 1) if last else -192.0, ADD, ADD)
+
+            def signs(lo, hi):
+                if last:
+                    tt(V("posf", lo, hi), V("acc", lo, hi), V("eq2", lo, hi), ADD)
+                    ts(V("pos", lo, hi), V("posf", lo, hi), -0.5, 223.0, MUL, ADD)
+                else:
+                    ts(V("pos", lo, hi), V("acc", lo, hi), -0.5, 223.5, MUL, ADD)
+
+            signs(nv, ne)
+            ts(V("pos", 0, nv), V("sc", 223, 224 * nv, 224), *((-1.0, 223.0) if last else (1.0, 192.0)), MUL, ADD)
+            scatter(0, ne)
+            if ne < 28:
+                signs(ne, 28)
+                scatter(ne, 28)
+        hold("held2", V("ordr", 0, E))
+        ts(V("ordl", 0, 28), ends("held2"), -1.0, -1.0, MUL, ADD)
         for b in range(4):
-            o = E * b
-            tt(V("mm", o + 1, o + E - 1), V("vs", o, o + E - 2), V("vs", o + 2, o + E), MAX, [("vs%d" % b, 0, 1)], [("mm%d" % b, 0, 1)])
-        ends = [("vs%d" % b, 0, 1) for b in range(4)]
-        tt(V("mm", 0, 4 * E, E), V("vs", 0, 4 * E, E), V("vs", 1, 4 * E, E), MAX, ends, [("mm%d" % b, 1, 2) for b in range(4)])
-        tt(V("mm", E - 1, 4 * E, E), V("vs", E - 1, 4 * E, E), V("vs", E - 2, 4 * E, E), MAX, ends, [("mm%d" % b, 2, 3) for b in range(4)])
+            o = PL * b
+            act(V("vs", o + 3, o + 3 + 2 * E - 1, 2), by(V("vp", E * b, E * b + E), V("ordl", 0, 28)), COPY)
+            act(V("vs", o + 1, o + 900, 898), V("vs", o + 3, o + 898, 894), COPY)
+        ts(V("pos2", 0, 28), V("pos", 0, 28), 2.0, 1.0, MUL, ADD)
+        if t == 0:
+            act(V("iq", 0, E), V("iof", 0, E), IDEN, scale=1.0 / 1024, bias=1.25 - 225.0 / 1024)
+            act(V("hin", 0, 4 * E, 4), V("er", 0, E), COPY)
+            for b, c in enumerate((0.0, 4.0, 9.25, 4.0)):
+                const(V("hw", b, 1296, 4), 324, c)
+            const(V("hin", 4 * (E - 2) + 3, 4 * E, 4), 2, 0.0)
+            const(V("hin", 4 * (E - 3) + 3, 4 * (E - 2)), 1, -1.0)
+            const(V("hin", 4 * (E - 1) + 1, 4 * (E - 1) + 2), 1, 0.0)
+            tc(V("bo16", 0, 28), V("bo", 0, 28))
+        elif t == 1:
+            act(V("yl", 0, E), K, IDEN, scale=0.5, bias=WHOLE)
+            act(V("hin", 0, 4 * E, 4), V("yl", 0, E), IDEN, bias=-WHOLE)
+            act(V("hin", 2, 4 * (E - 4), 4), V("yl", 4, E), IDEN, bias=-WHOLE)
+            const(V("hw", 2, 1296, 4), 324, 668.0)
+            for b in (2, 3):
+                const(V("hin", 4 * (E - 4) + b, 4 * E, 4), 4, 0.0)
+            const(V("ks", 0, 8), 8, 0.0)
+        else:
+            act(V("ks", 1, 1 + E), by(V("d2", 0, E), V("ordl", 0, 28)), COPY, scale=256.0)
+
+        def most(b):
+            o = PL * b
+            scan(V("mm", o, o + 2 * E), V("vs", o + 4, o + 4 + 2 * E), V("vs", o + 1, o + 1 + 2 * E), 0.0, MAX, MIN)
 
         def fused(b, lo, hi):
-            tt(V("zt", 4 * lo + b, 4 * hi, 4), V("mm", E * b, E * b + E).indirect(V("pos", lo // 16, hi // 16)), V("vp", E * b + lo, E * b + hi), ADD,
-               [("mm%d" % b, 0, 3), ("pos", 0, 28), ("vp%d" % b, lo, hi)], [("z%d" % b, lo, hi)])
+            tt(V("zt", 4 * lo + b, 4 * hi, 4), by(V("mm", PL * b, PL * b + 2 * E), V("pos2", lo // 16, hi // 16)), V("vp", E * b + lo, E * b + hi), ADD)
 
         def product(lo, hi, b0):
-            quant("qz", "sz", "zt", lo, hi, [("z%d" % b, lo, hi) for b in range(4)])
+            quant("qz", "zt", lo, hi)
             for b in range(4):
-                mx(b0 + b, hi - lo, "qw", "sw", 128 * b, "qz", "sz", lo, hi)
+                mx(b0 + b, "qw", 128 * b, "qz", lo, hi)
 
-        xn = "xt%d" % (t + 1)
+        xn, qn = "xt%d" % (t + 1), "qx%d" % (t + 1)
 
         def update(lo, hi, b0):
             for b in range(4):
-                r = [("x32_%d" % b, lo, hi)]
-                tt(V("x32", C * b + lo, C * b + hi), bank(b0 + b, 0, hi - lo), V("x32", C * b + lo, C * b + hi), ADD, [("b%d" % (b0 + b), 0, 1)] + r, r)
+                x = V("x32", C * b + lo, C * b + hi)
+                tt(x, bank(b0 + b, 0, hi - lo), x, ADD)
             for b in range(4):
-                o, i, W = V(xn, 4 * lo + b, 4 * hi, 4), V("x32", C * b + lo, C * b + hi), [("x%d_%d" % (t + 1, b), lo, hi)]
+                o, i = V(xn, 4 * lo + b, 4 * hi, 4), V("x32", C * b + lo, C * b + hi)
                 if b < 3:
-                    act(o, i, COPY, [("x32_%d" % b, lo, hi)], W, scale=0.03125)
+                    act(o, i, COPY, scale=0.03125)
                 else:
-                    ts(o, i, 0.03125, None, MUL, None, [("x32_%d" % b, lo, hi)], W)
+                    ts(o, i, 0.03125, None, MUL)
 
         def planes(lo, hi):
             for b in range(4):
-                act(V("vp", E * b + lo, E * b + hi), V("x32", C * b + lo, C * b + hi), COPY, [("x32_%d" % b, lo, hi)], [("vp%d" % b, lo, hi)], scale=2.0 ** -6)
+                act(V("vp", E * b + lo, E * b + hi), V("x32", C * b + lo, C * b + hi), COPY, scale=2.0 ** -6)
 
-        qn, sn = "qx%d" % (t + 1), "sx%d" % (t + 1)
+        cut = 256 if last else 128
         for b in range(4):
-            fused(b, 0, 128)
-        product(0, 128, 0)
-        fused(0, 128, C)
-        update(0, 128, 0)
-        fused(1, 128, C)
-        quant(qn, sn, xn, 0, 128, xr(t + 1, 0, 128))
+            most(b)
+            fused(b, 0, cut)
+        product(0, cut, 0)
+        if t == 0:
+            tt(V("hin", 2, 4 * E, 4), V("er", 2, E + 2), V("iq", 0, E), ADD)
+        fused(0, cut, C)
+        update(0, cut, 0)
+        fused(1, cut, C)
+        quant(qn, xn, 0, cut)
         if not last:
             send(t + 1)
-            mx(0, 128, "qur", "sur", 0, qn, sn, 0, 128)
-            planes(0, 128)
+            mx(0, "qur", 0, qn, 0, cut)
+            mx(1, "qur", 0, qn, 0, cut)
+            planes(0, cut)
         else:
-            dma("s", "dca", [(qn, 0, 128)], [], T.oc[:, 0:512], V(qn, 0, 128).bitcast(dt.uint8))
-            mx(0, 128, "qv", "sv", 0, qn, sn, 0, 128)
-            act(V("yr", 0, 128), bank(0, 0, 128), COPY, [("b0", 0, 1)], [("yr", 0, 128)])
-            dma("s", "dya", [("yr", 0, 128)], [], T.y[:, 0:128], T.yr[:, 0:128])
-        fused(2, 128, C)
-        fused(3, 128, C)
-        product(128, C, 4)
-        if t == 0:
-            fill("ar1", E, E + 16, 0.0)
-            fill("ar2", E, E + 16, 0.0)
-            for lo, hi in ((0, OFF), (OFF + E, E + 32)):
-                fill("kr", lo, hi, 0.0)
-            fill("eq", 0, 848, 0.0)
-            ts(T.behind[:, :], T.qi[:, :], T.pl[:, 0:1], 2.0, GT, MUL, [("qi", 0, 16), ("pl", 0, 1)], [("behind", 0, 16)])
-        elif t == 1:
-            tt(V("g1", 0, E), V("s1", 0, E), V("s2", 0, E), ADD, [("s1", 0, E), ("s2", 0, E)], [("g1", 0, E)])
-        else:
-            tt(V("eqs", 0, E), V("ks", 1, E + 1), V("ks", 0, E), EQ, [("ks", 0, E + 1)], [("eqs", 0, E)])
-            op("v", [("ones", 0, 512), ("eqs", 0, E)], [("rr", 0, E)], g.vector.tensor_tensor_scan, V("rr", 0, E), V("ones", 0, E), V("eqs", 0, E), 0.0, ADD, MUL)
-        update(128, C, 4)
-        quant(qn, sn, xn, 128, C, xr(t + 1, 128, C))
-        if t == 1:
-            quant("qc", "cs", "ct", 0, 512, [("ct", 0, 16)])
-            quant("qv", "sv", "vt", 0, 128, [("vt", 0, 128)])
-            fill("ks", 0, 8, -9.0e6)
+            dma("s", "dca", T.oc[:, 0:4 * cut], bytes8(V(qn, 0, cut)))
+            mx(0, "qv", 0, qn, 0, cut)
+            act(V("yr", 0, cut), bank(0, 0, cut), COPY)
+            dma("s", "dya", T.y[:, 0:cut], V("yr", 0, cut))
+        fused(2, cut, C)
+        fused(3, cut, C)
+        product(cut, C, 4)
         if not last:
-            words(t + 1, 0, 0, 128, 0, 128)
-            planes(128, C)
-            if t == 0:
-                for q in range(16):
-                    o = 512 * (q // 4)
-                    act(T.ct[:, o + q % 4:o + 512:4], T.ident[:, :], COPY, [("ident", 0, 128), ("behind", 0, 16)], [("ct", q, q + 1)], scale=T.behind[:, q:q + 1])
+            words(t + 1, 0, 0, cut)
         else:
-            tt(V("lw", 0, E), V("iof", 0, E), V("rr", 0, E), SUB, [("iof", 0, E), ("rr", 0, E)], [("lw", 0, E)])
+            tt(V("dk", 0, E), V("ks", 1, E + 1), V("ks", 0, E), SUB)
+        update(cut, C, 4)
+        quant(qn, xn, cut, C)
+        if t == 1:
+            quant("qv", "vt", 0, 128)
+        if not last:
+            planes(cut, C)
 
     q, s = "qx%d" % NR, "sx%d" % NR
-    mx(1, C - 128, "qv", "sv", 0, q, s, 128, C)
-    dma("s", "dcb", [(q, 128, C)], [], T.oc[:, 512:1536], V(q, 128, C).bitcast(dt.uint8))
+    mx(1, "qv", 0, q, cut, C)
+    scan(V("lw", 0, E), V("dk", 0, E), V("iof", 0, E), 0.0, ADD, MIN)
+    dma("s", "dcb", T.oc[:, 4 * cut:4 * C], bytes8(V(q, cut, C)))
     for k in range(4):
-        dma("s", "ds%d" % k, [(q, 0, C)], [], T.osc[4 * k:4 * k + 4, 0:C], T[s][32 * k:32 * k + 4, 0:C])
-    act(V("yr", 128, C), bank(1, 0, C - 128), COPY, [("b1", 0, 1)], [("yr", 128, C)])
-    dma("a", "dyb", [("yr", 128, C)], [], T.y[:, 128:C], T.yr[:, 128:C])
-    act(V("lvr", 0, E), V("lw", 0, E).indirect(V("pos", 0, 28)), COPY, [("lw", 0, E), ("pos", 0, 28)], [("lvr", 0, E)])
-    dma("s", "dlv", [("lvr", 0, E)], [], T.lv[:, :], T.lvr[0:128:16, 0:E])
+        dma("s", "ds%d" % k, T.osc[4 * k:4 * k + 4, 0:C], (T[s][32 * k:32 * k + 4, 0:C], V(s, 0, C)[1]))
+    act(V("yr", cut, C), bank(1, 0, C - cut), COPY)
+    dma("a", "dyb", T.y[:, cut:C], V("yr", cut, C))
+    act(V("lvr", 0, E), by(V("lw", 0, E), V("pos", 0, 28)), IDEN, bias=-1.0)
+    dma("s", "dlv", T.lv[:, :], (T.lvr[0:128:16, 0:E], V("lvr", 0, E)[1]))
     for sem in count:
         g.wait_ge(T.sem[sem], count[sem])
     for sem in DMAS:

@@ -2,28 +2,33 @@ from concourse.mybir import dt, AluOpType, ActivationFunctionType
 
 C, H, E, NR = 384, 64, 448, 3
 NV = (0, 11, 10)
-NE = (0, 22, 22)
-PL = 912
+NE = (0, 24, 24)
+X2 = E + 16
+PL = 2 * X2
 BIG = 1.0e29
 CAP = 2.0 ** 25
 WHOLE = 12582912.0
+HW = 328
+CUTS = ((0, 128, 256, C), (0, 256, C))
+TAIL = ("N0 M0 G0 M1 M2 G1 M3 E2 E3 F2 P0 F3 U0 P1 P2 Q0 U1 Q1 U2 B0 Q2 K0 V0 B1 A0 V1 K1",
+        "N0 M0 L0 G0 M1 M2 G1 M3 F2 E3 E2 F3 P0 L1 U0 L2 Q0 P1 U1 Q1")
 
 SCRATCH = {}
 for _k, _n in (("qu", 128), ("qur", 256), ("qv", 128), ("qw", 512), ("qe", 512), ("qz", C), ("qg", 128), ("qh", E)):
     SCRATCH[_k] = ("sbuf", [128, _n], "float8_e4m3fn_x4")
     SCRATCH["s" + _k[1:]] = ("sbuf", [128, _n], "uint8")
 for _k, _n in (("ut", 512), ("vt", 512), ("et", 2048), ("gt", 512), ("hl", 4 * E), ("zt", 4 * C), ("vp", 4 * E), ("x32", 4 * C),
-               ("vs", 4 * PL), ("mm", 4 * PL), ("hb", 128), ("ident", 128), ("grp", 128), ("ones", E), ("t1", E), ("t2", E), ("w", E + 16),
-               ("w6", E), ("er", E + 16), ("junk", 4 * E), ("cb", 16 * E), ("sc", 8 * E), ("lane", E), ("cap", E), ("tri", E), ("hit", E),
-               ("hw", 4 * E), ("eq", E), ("eqs", E)):
+               ("vs", 4 * PL), ("mm", 4 * PL), ("hb", 128), ("ident", 128), ("grp", 128), ("ones", X2), ("t1", E), ("t2", E), ("w", E + 16),
+               ("w6", E), ("er", E + 16), ("junk", 4 * E), ("cb", 16 * E), ("sc", 8 * E), ("lane", E), ("cap", E), ("cap2", X2), ("tri", E),
+               ("hit", E), ("c0", 32), ("hw", 4 * HW), ("eq", E), ("eqs", E)):
     SCRATCH[_k] = ("sbuf", [128, _n], "bfloat16")
-for _k, _n in (("iof", E), ("iq", E), ("pl", 1), ("pq", 1), ("pg", 1), ("lama", 1), ("lam", 1), ("lamb", 1), ("lams", 1), ("acc0", 2),
-               ("hin", 4 * E), ("kr", 4 * E), ("held", E), ("own", 28), ("acc", 28), ("eq2", 28), ("posf", 28), ("d2", 2 * E),
-               ("ordr", E), ("held2", E), ("yl", E), ("ks", E + 16), ("dk", E), ("lw", E), ("lvr", E), ("yr", C)):
+for _k, _n in (("iof", E), ("iq", E), ("pl", 1), ("pl1", 1), ("pq", 1), ("pg", 1), ("lama", 1), ("lam", 1), ("lamb", 1), ("lams", 1), ("acc0", 2),
+               ("hin", 4 * E), ("kr", 8 * E), ("held", E), ("own", 28), ("nown", 28), ("acc", 28), ("eq2", 28), ("posf", 28),
+               ("ordr", X2), ("held2", X2), ("yl", E), ("ks", X2), ("dk", E), ("lw", X2), ("lvr", E), ("yr", C)):
     SCRATCH[_k] = ("sbuf", [128, _n], "float32")
 for _k, _n in (("uo", 16), ("bo", 28), ("pin", 1), ("pla", 1), ("plq", 1), ("plg", 1)):
     SCRATCH[_k] = ("sbuf", [128, _n], "int32")
-for _k, _n in (("uo16", 16), ("bo16", 28), ("pos", 28), ("pos2", 28), ("ordl", 28)):
+for _k, _n in (("uo16", 16), ("bo16", 28), ("pos", 28), ("pos2", 28), ("ordl", 30), ("ord4", 30)):
     SCRATCH[_k] = ("sbuf", [128, _n], "uint16")
 SCRATCH["ps"] = ("psum", [128, 4096], "float32")
 for _t in range(NR + 1):
@@ -152,8 +157,8 @@ def rank_program(g, core, T, topo):
         g.remote_dma(V(s, C, E)[0], V(s, 0, H)[0], T.sem["arr%d" % t], T.sem.left, pid, rid, m)
         note("remote", [], V(q, C, E)[1] + V(s, C, E)[1], "arr%d" % t, 2 * len(send_engines(nxt, core)))
 
-    def hold(out, row):
-        scan(V(out, 0, E), row, V("cap", 0, E), 0.0, MAX, MUL)
+    def hold(out, row, cap, k):
+        scan(V(out, 0, k), row, V(cap, 0, k), 0.0, MAX, MUL)
 
     def ends(name, lo=0, hi=28):
         return V(name, 16 * lo + 15, 16 * hi, 16)
@@ -162,29 +167,28 @@ def rank_program(g, core, T, topo):
     dma("s", "dxa", V("xt0", 0, 512), T.x[:, 0:512])
     dma("a", "du", V("ut", 0, 512), T.u[:, :])
     dma("s", "dxb", V("xt0", 512, 1536), T.x[:, 512:1536])
-    fill(V("hb", 0, 128), 0.5)
     iota(V("pin", 0, 1), [[0, 1]], 0, 1)
-    op("g", 1, g.affine_select, V("ident", 0, 128), V("hb", 0, 128), [[-1, 128]], EQ, 0.0, 0, 1)
-    iota(V("uo", 0, 16), [[1, 2], [16, 8]], 0, 0)
     iota(V("lane", 0, E), [[0, 28], [1, 16]], 0, 0, **FL)
+    fill(V("hb", 0, 128), 0.5)
+    fill(V("ones", 0, X2), 1.0)
+    iota(V("uo", 0, 16), [[1, 2], [16, 8]], 0, 0)
     iota(V("grp", 0, 128), [[1, 8], [0, 16]], 0, 0, **FL)
-    fill(V("ones", 0, E), 1.0)
-    fill(V("et", 0, 2048), 0.0)
+    op("g", 1, g.affine_select, V("ident", 0, 128), V("hb", 0, 128), [[-1, 128]], EQ, 0.0, 0, 1)
     ts(V("pla", 0, 1), V("pin", 0, 1), 15, None, AND)
     ts(V("plq", 0, 1), V("pin", 0, 1), 2, 3, SHR, AND)
     ts(V("plg", 0, 1), V("pin", 0, 1), 4, None, SHR)
     for nm, src in (("pl", "pla"), ("pq", "plq"), ("pg", "plg")):
         tc(V(nm, 0, 1), V(src, 0, 1))
+    ts(V("tri", 0, E), V("lane", 0, E), V("pl", 0, 1), None, GT)
+    ts(V("hit", 0, E), V("lane", 0, E), V("pl", 0, 1), CAP, EQ, MUL)
     tc(V("uo16", 0, 16), V("uo", 0, 16))
+    tt(V("cap", 0, E), V("tri", 0, E), V("hit", 0, E), ADD)
+    for b, c in enumerate((1.0, 1.0, 256.0, 0.0)):
+        ts(V("gt", b, 512, 4), V("grp", 0, 128), V("pg", 0, 1), c, EQ, MUL)
+    for lo in range(0, 2048, 416):
+        const(V("et", lo, min(lo + 416, 2048)), min(416, 2048 - lo), 0.0)
     for b in range(4):
         act(V("et", 512 * b + b, 512 * b + 512, 4), V("ident", 0, 128), COPY)
-    const(V("w", E, E + 16), 16, -0.5)
-    const(V("er", E, E + 16), 16, -0.75)
-    const(V("hl", 3, 4 * E, 4), E, 0.0)
-    act(V("lama", 0, 1), V("pq", 0, 1), IDEN, scale=0.5, bias=0.5)
-    act(V("lam", 0, 1), V("pl", 0, 1), IDEN, bias=V("lama", 0, 1))
-    act(V("lamb", 0, 1), V("lam", 0, 1), IDEN, bias=-0.5)
-    act(V("lams", 0, 1), V("lam", 0, 1), IDEN, bias=-0.25)
     quant("qx0", "xt0", 0, 128)
     send(0)
     iota(V("iof", 0, E), [[1, E]], 1, 0, **FL)
@@ -194,6 +198,17 @@ def rank_program(g, core, T, topo):
     act(V("sur", 0, 256), by(V("su", 0, 128), V("uo16", 0, 16)), COPY)
     quant("qx0", "xt0", 128, C)
     quant("qe", "et", 0, 512)
+    quant("qg", "gt", 0, 128)
+    act(V("lama", 0, 1), V("pq", 0, 1), IDEN, scale=0.5, bias=0.5)
+    const(V("w", E, E + 16), 16, -0.5)
+    const(V("er", E, E + 16), 16, -0.75)
+    act(V("lam", 0, 1), V("pl", 0, 1), IDEN, bias=V("lama", 0, 1))
+    const(V("hl", 3, 4 * E, 4), E, 0.0)
+    act(V("lamb", 0, 1), V("lam", 0, 1), IDEN, bias=-0.5)
+    act(V("lams", 0, 1), V("lam", 0, 1), IDEN, bias=-0.25)
+    act(ends("cap"), ends("cap"), COPY, scale=-1.0 / CAP)
+    for b in range(4):
+        act(V("vp", E * b, E * b + C), V("xt0", b, 4 * C, 4), COPY, scale=0.5)
     waits("s", V("qx0", C, E)[1], [])
     dma("s", "dwc", bytes8(V("qw", 0, 512)), T.wc[:, :])
     dma("s", "dws", V("sw", 0, 512), T.ws[:, :])
@@ -206,139 +221,140 @@ def rank_program(g, core, T, topo):
         ts(V("w6", klo, khi), V("w", klo, khi), 4.5, 0.5, MUL, ADD)
         tt(V("er", klo, khi), V("w6", klo, khi), V("w", klo + 1, khi + 1), ADD)
 
-    def words(t, k, lo, hi):
+    def span(t, lo, hi):
         d = 2 ** t
+        return d, max(lo - d, 0), hi if hi == E else hi - d
+
+    def bits(t, k, lo, hi):
+        d, klo, khi = span(t, lo, hi)
         top = hi - 1 if (t, hi) == (1, E) else hi
-        klo, khi = max(lo - d, 0), hi if hi == E else hi - d
-        ts(V("hin", 4 * lo + 1, 4 * top, 4), bank(k, 0, top - lo), 0.0, 2.0, GT, MUL)
-        act(V("hin", 4 * klo + 3, 4 * (top - d), 4), bank(k + 1, klo + d - lo, top - lo), SIGN, bias=-1.0e-36)
+        act(V("hin", 4 * klo + 3, 4 * (top - d), 4), bank(k, klo + d - lo, top - lo), SIGN, bias=-1.0e-36)
+        ts(V("hin", 4 * lo + 1, 4 * top, 4), bank(k + 1, 0, top - lo), 0.0, 2.0, GT, MUL)
+
+    def keys(t, lo, hi):
+        d, klo, khi = span(t, lo, hi)
         scan(V("kr", 4 * klo, 4 * khi), V("hw", 0, 4 * (khi - klo)), V("hin", 4 * klo, 4 * khi), 0.0, MUL, ADD)
-        if t == NR - 1:
-            for o, e in ((0, 1.0), (E, -1.0)):
-                act(V("d2", o + klo, o + khi), V("kr", 4 * klo + 3, 4 * khi, 4), IDEN, bias=e)
+
+    def unpack(t, k):
+        for b in range(4):
+            mx(k + b, "qe", 128 * b, "qx%d" % t, E - 128, E)
+        for b in range(4):
+            act(V("vp", E * b + C, E * b + E), bank(k + b, 64, 128), COPY)
+
+    def scatter(lo, hi):
+        tc(by(V("ordr", 0, X2), V("pos", lo, hi)), V("iof", 16 * lo, 16 * hi))
 
     K = V("kr", 3, 4 * E, 4)
 
     for t in range(NR):
         qx = "qx%d" % t
         last = t == NR - 1
-        if t == 0:
-            mx(0, "qur", 0, qx, 0, C)
-            mx(1, "qur", 128, qx, 0, C)
-            words0(0, 0, 0, C, 0, C - 1)
-            act(V("junk", 0, C - 1), V("er", 0, C - 1), SIGN, bias=V("lams", 0, 1), scale=-1.0, accum_out=V("acc0", 0, 1))
-            O = lambda lo, hi: V("hl", 4 * lo + 2, 4 * hi, 4)
-            ts(O(0, C - 1), V("er", 0, C - 1), V("lam", 0, 1), None, EQ)
-            ts(V("tri", 0, E), V("lane", 0, E), V("pl", 0, 1), None, GT)
-            ts(V("hit", 0, E), V("lane", 0, E), V("pl", 0, 1), CAP, EQ, MUL)
-            for b, c in enumerate((1.0, 1.0, 256.0, 0.0)):
-                ts(V("gt", b, 512, 4), V("grp", 0, 128), V("pg", 0, 1), c, EQ, MUL)
-            act(V("acc0", 0, 1), V("acc0", 0, 1), IDEN, scale=0.5, bias=31.0)
-            tt(V("cap", 0, E), V("tri", 0, E), V("hit", 0, E), ADD)
-            ts(ends("cap"), ends("cap"), -1.0 / CAP, None, MUL)
-            quant("qg", "gt", 0, 128)
-            mx(2, "qur", 0, qx, E - 128, E)
-            mx(3, "qur", 128, qx, E - 128, E)
-            for b in range(4):
-                act(V("vp", E * b, E * b + C), V("xt0", b, 4 * C, 4), COPY, scale=0.5)
-        else:
-            mx(2, "qur", 0, qx, 128, E)
-            mx(3, "qur", 0, qx, 128, E)
-        for b in range(4):
-            mx(4 + b, "qe", 128 * b, qx, E - 128, E)
-        if t == 0:
-            words0(2, 64, C, E, C - 1, E)
-            act(V("junk", E, E + 65), V("er", C - 1, E), SIGN, bias=V("lams", 0, 1), scale=-1.0, accum_out=V("acc0", 1, 2))
-        else:
-            words(t, 2, 128, E)
-
-        def halo_planes():
-            for b in range(4):
-                act(V("vp", E * b + C, E * b + E), bank(4 + b, 64, 128), COPY)
-
-        def scatter(lo, hi):
-            tc(by(V("ordr", 0, E), V("pos", lo, hi)), V("iof", 16 * lo, 16 * hi))
-
         nv, ne = NV[t], NE[t]
         if t == 0:
-            halo_planes()
+            O = lambda lo, hi: V("hl", 4 * lo + 2, 4 * hi, 4)
+            mx(0, "qur", 0, qx, 0, C)
+            mx(1, "qur", 128, qx, 0, C)
+            mx(2, "qur", 0, qx, E - 128, E)
+            mx(3, "qur", 128, qx, E - 128, E)
+            words0(0, 0, 0, C, 0, C - 1)
+            act(V("junk", 0, C - 1), V("er", 0, C - 1), SIGN, bias=V("lams", 0, 1), scale=-1.0, accum_out=V("acc0", 0, 1))
+            ts(O(0, C - 1), V("er", 0, C - 1), V("lam", 0, 1), None, EQ)
+            act(V("acc0", 0, 1), V("acc0", 0, 1), IDEN, scale=0.5, bias=31.0)
+            words0(2, 64, C, E, C - 1, E)
+            act(V("junk", E, E + 65), V("er", C - 1, E), SIGN, bias=V("lams", 0, 1), scale=-1.0, accum_out=V("acc0", 1, 2))
             ts(O(C - 1, E - 1), V("er", C - 1, E - 1), V("lam", 0, 1), None, EQ)
             ts(O(E - 1, E), V("er", E - 1, E), V("lamb", 0, 1), None, EQ)
+            ts(V("pl1", 0, 1), V("pl", 0, 1), 1.0, None, MAX)
             ts(V("t1", E - 1, E), V("acc0", 1, 2), 0.5, V("acc0", 0, 1), MUL, ADD)
+            ts(V("c0", 0, 16), V("lane", 0, 16), V("pl1", 0, 1), None, GT)
             scan(V("t1", 0, E - 1), V("ones", 0, E - 1), O(0, E - 1), V("t1", E - 1, E), MUL, ADD)
+            ts(V("c0", 16, 32), V("lane", 0, 16), V("pl1", 0, 1), CAP, EQ, MUL)
             tt(V("t2", 0, E), V("t1", 0, E), O(0, E), MUL)
+            tt(V("cap2", 0, 16), V("c0", 0, 16), V("c0", 16, 32), ADD)
             ts(V("hl", 0, 4 * E, 4), V("t2", 0, E), 16 * WHOLE, -16 * WHOLE, ADD, ADD)
+            tc(V("bo16", 0, 28), V("bo", 0, 28))
             tt(V("hl", 1, 4 * E, 4), V("t2", 0, E), V("hl", 0, 4 * E, 4), SUB)
             quant("qh", "hl", 0, E)
-            mx(3, "qg", 0, "qh", 0, E)
+            act(V("iq", 0, E), V("iof", 0, E), IDEN, scale=1.0 / 1024, bias=1.25 - 225.0 / 1024)
+            unpack(t, 4)
+            mx(0, "qg", 0, "qh", 0, E)
+            const(V("ordr", 0, X2), X2, 0.0)
+            act(V("cap2", 15, 16), V("cap2", 15, 16), COPY, scale=-1.0 / CAP)
+            act(V("cap2", 16, E), V("cap", 16, E), COPY)
+            const(V("cap2", E + 1, X2 - 1), 14, 1.0)
+            const(V("cap2", E, E + 1), 1, CAP)
+            const(V("cap2", X2 - 1, X2), 1, -1.0 / CAP)
             for b in range(4):
-                const(V("vs", PL * b, PL * b + 896, 2), E, BIG)
-                const(V("vs", PL * b + 896, PL * b + 904, 2), 4, BIG)
+                const(V("vs", PL * b, PL * b + PL, 2), X2, BIG)
             for b in range(4):
                 act(V("x32", C * b, C * b + C), V("xt0", b, 4 * C, 4), COPY, scale=32.0)
-            hold("held", bank(3, 0, E))
-            ts(V("pos", 0, 28), ends("held"), -1.0, -64.0, MUL, ADD)
+            tt(V("hin", 2, 4 * E, 4), V("er", 2, E + 2), V("iq", 0, E), ADD)
+            hold("held", bank(0, 0, E), "cap", E)
+            ts(V("pos", 0, 28), ends("held"), -1.0, -63.0, MUL, ADD)
             scatter(0, 28)
         else:
-            hold("held", K)
-            halo_planes()
-            row = lambda c, lo=0, hi=E: V("d2", 16 * c + 16, 16 * c + 16 + E) if last else K
+            hold("held", K, "cap", E)
+            row = lambda c: V("kr", 4 * (16 * c + 16) + 3, 4 * (16 * c + 16 + E), 4) if last else K
+            if last:
+                act(V("kr", 4 * E + 3, 8 * E, 4), K, IDEN, bias=-2.0)
+                act(V("nown", 0, 28), ends("held"), IDEN, bias=1.0)
             for c in range(nv, 28):
-                act(V("junk", E * (c % 4), E * (c % 4) + E), row(c), SIGN, bias=ends("held", c, c + 1), accum_out=V("acc", c, c + 1))
+                act(V("junk", E * (c % 4), E * (c % 4) + E), row(c), SIGN, bias=V("nown", c, c + 1) if last else ends("held", c, c + 1),
+                    accum_out=V("acc", c, c + 1))
+            unpack(t, 4 - free)
             if last:
                 ts(V("own", 0, 28), ends("held"), -1.0, None, MUL)
-                tt(V("eq", 0, E), by(V("own", 0, 28), V("bo16", 0, 28)), K, EQ)
-                scan(V("eqs", 0, E), V("eq", 0, E), V("tri", 0, E), 0.0, ADD, MUL)
             for c in range(nv):
                 if last:
                     ts(V("cb", E * c, E * c + E), row(c), V("own", c, c + 1), -0.5, GE, ADD)
                 else:
                     ts(V("cb", E * c, E * c + E), row(c), ends("held", c, c + 1), 0.0, ADD, LT)
+                if last and c == 0:
+                    tt(V("eq", 0, E), by(V("own", 0, 28), V("bo16", 0, 28)), K, EQ)
+                if last and c == 1:
+                    scan(V("eqs", 0, E), V("eq", 0, E), V("tri", 0, E), 0.0, ADD, MUL)
             if last:
                 ts(V("eq2", 0, 28), ends("eqs"), 2.0, None, MUL)
             for c in range(nv):
                 scan(V("sc", 224 * c, 224 * c + 224), V("cb", E * c, E * c + 224), V("cb", E * c + 224, E * c + E),
                      ends("eqs", c, c + 1) if last else -192.0, ADD, ADD)
+                if last and c == nv - 2:
+                    tt(V("posf", nv, ne), V("acc", nv, ne), V("eq2", nv, ne), ADD)
 
             def signs(lo, hi):
-                if last:
-                    tt(V("posf", lo, hi), V("acc", lo, hi), V("eq2", lo, hi), ADD)
-                    ts(V("pos", lo, hi), V("posf", lo, hi), -0.5, 223.0, MUL, ADD)
-                else:
-                    ts(V("pos", lo, hi), V("acc", lo, hi), -0.5, 223.5, MUL, ADD)
+                ts(V("pos", lo, hi), V("posf" if last else "acc", lo, hi), -0.5, 224.0 if last else 224.5, MUL, ADD)
 
             signs(nv, ne)
-            ts(V("pos", 0, nv), V("sc", 223, 224 * nv, 224), *((-1.0, 223.0) if last else (1.0, 192.0)), MUL, ADD)
+            ts(V("pos", 0, nv), V("sc", 223, 224 * nv, 224), *((-1.0, 224.0) if last else (1.0, 193.0)), MUL, ADD)
             scatter(0, ne)
-            if ne < 28:
-                signs(ne, 28)
-                scatter(ne, 28)
-        hold("held2", V("ordr", 0, E))
-        ts(V("ordl", 0, 28), ends("held2"), -1.0, -1.0, MUL, ADD)
-        for b in range(4):
-            o = PL * b
-            act(V("vs", o + 3, o + 3 + 2 * E - 1, 2), by(V("vp", E * b, E * b + E), V("ordl", 0, 28)), COPY)
-            act(V("vs", o + 1, o + 900, 898), V("vs", o + 3, o + 898, 894), COPY)
-        ts(V("pos2", 0, 28), V("pos", 0, 28), 2.0, 1.0, MUL, ADD)
+            if last:
+                tt(V("posf", ne, 28), V("acc", ne, 28), V("eq2", ne, 28), ADD)
+            signs(ne, 28)
+            scatter(ne, 28)
+        hold("held2", V("ordr", 0, X2), "cap2", X2)
+        ts(V("ordl", 0, 29), ends("held2", 0, 29), -1.0, -1.0, MUL, ADD)
+        into = lambda b, lo, hi: (V("vs", PL * b + 32 * lo + 1, PL * b + 32 * hi, 2), by(V("vp", E * b, E * b + E), V("ordl", lo, hi)))
+        act(*into(0, 14, 29), COPY)
+        tc(*into(0, 0, 14))
+        for b in range(1, 4):
+            act(*into(b, 0, 29), COPY)
         if t == 0:
-            act(V("iq", 0, E), V("iof", 0, E), IDEN, scale=1.0 / 1024, bias=1.25 - 225.0 / 1024)
             act(V("hin", 0, 4 * E, 4), V("er", 0, E), COPY)
             for b, c in enumerate((0.0, 4.0, 9.25, 4.0)):
-                const(V("hw", b, 1296, 4), 324, c)
+                const(V("hw", b, 4 * HW, 4), HW, c)
             const(V("hin", 4 * (E - 2) + 3, 4 * E, 4), 2, 0.0)
             const(V("hin", 4 * (E - 3) + 3, 4 * (E - 2)), 1, -1.0)
             const(V("hin", 4 * (E - 1) + 1, 4 * (E - 1) + 2), 1, 0.0)
-            tc(V("bo16", 0, 28), V("bo", 0, 28))
         elif t == 1:
             act(V("yl", 0, E), K, IDEN, scale=0.5, bias=WHOLE)
+            const(V("hw", 2, 4 * HW, 4), HW, 668.0)
             act(V("hin", 0, 4 * E, 4), V("yl", 0, E), IDEN, bias=-WHOLE)
             act(V("hin", 2, 4 * (E - 4), 4), V("yl", 4, E), IDEN, bias=-WHOLE)
-            const(V("hw", 2, 1296, 4), 324, 668.0)
             for b in (2, 3):
                 const(V("hin", 4 * (E - 4) + b, 4 * E, 4), 4, 0.0)
-            const(V("ks", 0, 8), 8, 0.0)
-        else:
-            act(V("ks", 1, 1 + E), by(V("d2", 0, E), V("ordl", 0, 28)), COPY, scale=256.0)
+
+        cuts = CUTS[last]
+        free = 4 * ((len(cuts) + 1) % 2)
 
         def most(b):
             o = PL * b
@@ -347,73 +363,71 @@ def rank_program(g, core, T, topo):
         def fused(b, lo, hi):
             tt(V("zt", 4 * lo + b, 4 * hi, 4), by(V("mm", PL * b, PL * b + 2 * E), V("pos2", lo // 16, hi // 16)), V("vp", E * b + lo, E * b + hi), ADD)
 
-        def product(lo, hi, b0):
-            quant("qz", "zt", lo, hi)
-            for b in range(4):
-                mx(b0 + b, "qw", 128 * b, "qz", lo, hi)
-
         xn, qn = "xt%d" % (t + 1), "qx%d" % (t + 1)
 
-        def update(lo, hi, b0):
+        def product(k):
+            lo, hi = cuts[k:k + 2]
+            quant("qz", "zt", lo, hi)
+            for b in range(4):
+                mx(4 * (k % 2) + b, "qw", 128 * b, "qz", lo, hi)
+
+        def update(k):
+            lo, hi = cuts[k:k + 2]
             for b in range(4):
                 x = V("x32", C * b + lo, C * b + hi)
-                tt(x, bank(b0 + b, 0, hi - lo), x, ADD)
+                tt(x, bank(4 * (k % 2) + b, 0, hi - lo), x, ADD)
             for b in range(4):
                 o, i = V(xn, 4 * lo + b, 4 * hi, 4), V("x32", C * b + lo, C * b + hi)
-                if b < 3:
+                if b < 3 or hi < C:
                     act(o, i, COPY, scale=0.03125)
                 else:
                     ts(o, i, 0.03125, None, MUL)
 
-        def planes(lo, hi):
+        def state(k):
+            lo, hi = cuts[k:k + 2]
+            quant(qn, xn, lo, hi)
+            if k == 0 and not last:
+                send(t + 1)
+            if hi < cuts[-2]:
+                return
+            k, lo = (0, 0) if hi < C else (1, lo)
+            if last:
+                dma("s", "dc" + "ab"[k], T.oc[:, 4 * lo:4 * hi], bytes8(V(qn, lo, hi)))
+                mx(free + k, "qv", 0, qn, lo, hi)
+                act(V("yr", lo, hi), bank(free + k, 0, hi - lo), COPY)
+                dma("a", "dy" + "ab"[k], T.y[:, lo:hi], V("yr", lo, hi))
+            else:
+                for j in range(2):
+                    mx(free + 2 * k + j, "qur", 0, qn, lo, E if k else hi)
+
+        def planes(k):
+            lo, hi = ((0, cuts[-2]), (cuts[-2], C))[k]
             for b in range(4):
                 act(V("vp", E * b + lo, E * b + hi), V("x32", C * b + lo, C * b + hi), COPY, scale=2.0 ** -6)
 
-        cut = 256 if last else 128
-        for b in range(4):
-            most(b)
-            fused(b, 0, cut)
-        product(0, cut, 0)
-        if t == 0:
-            tt(V("hin", 2, 4 * E, 4), V("er", 2, E + 2), V("iq", 0, E), ADD)
-        fused(0, cut, C)
-        update(0, cut, 0)
-        fused(1, cut, C)
-        quant(qn, xn, 0, cut)
-        if not last:
-            send(t + 1)
-            mx(0, "qur", 0, qn, 0, cut)
-            mx(1, "qur", 0, qn, 0, cut)
-            planes(0, cut)
-        else:
-            dma("s", "dca", T.oc[:, 0:4 * cut], bytes8(V(qn, 0, cut)))
-            mx(0, "qv", 0, qn, 0, cut)
-            act(V("yr", 0, cut), bank(0, 0, cut), COPY)
-            dma("s", "dya", T.y[:, 0:cut], V("yr", 0, cut))
-        fused(2, cut, C)
-        fused(3, cut, C)
-        product(cut, C, 4)
-        if not last:
-            words(t + 1, 0, 0, cut)
-        else:
-            tt(V("dk", 0, E), V("ks", 1, E + 1), V("ks", 0, E), SUB)
-        update(cut, C, 4)
-        quant(qn, xn, cut, C)
-        if t == 1:
-            quant("qv", "vt", 0, 128)
-        if not last:
-            planes(cut, C)
+        def levels(k):
+            if k == 0:
+                ts(V("ord4", 0, 29), V("ordl", 0, 29), 4.0, 3.0, MUL, ADD)
+                act(V("ks", 0, X2), by(V("kr", 0, 4 * E), V("ord4", 0, 29)), COPY, scale=256.0)
+            elif k == 1:
+                tt(V("dk", 0, E), V("ks", 1, E + 1), V("ks", 0, E), SUB)
+            else:
+                scan(V("lw", 1, E + 1), V("dk", 0, E), V("iof", 0, E), 1.0, ADD, MIN)
+                act(V("lvr", 0, E), by(V("lw", 0, X2), V("pos", 0, 28)), IDEN, bias=-1.0)
+                dma("s", "dlv", T.lv[:, :], (T.lvr[0:128:16, 0:E], V("lvr", 0, E)[1]))
 
-    q, s = "qx%d" % NR, "sx%d" % NR
-    mx(1, "qv", 0, q, cut, C)
-    scan(V("lw", 0, E), V("dk", 0, E), V("iof", 0, E), 0.0, ADD, MIN)
-    dma("s", "dcb", T.oc[:, 4 * cut:4 * C], bytes8(V(q, cut, C)))
+        part = lambda k: ((0, cuts[-2]), (cuts[-2], E))[k]
+        steps = {"M": most, "E": lambda b: fused(b, 0, cuts[1]), "F": lambda b: fused(b, cuts[1], C), "G": lambda b: fused(b, 0, C),
+                 "P": product, "U": update, "Q": state, "V": planes, "L": levels,
+                 "N": lambda k: ts(V("pos2", 0, 28), V("pos", 0, 28), 2.0, -1.0, MUL, ADD),
+                 "B": lambda k: bits(t + 1, free + 2 * k, *part(k)), "K": lambda k: keys(t + 1, *part(k)),
+                 "A": lambda k: quant("qv", "vt", 0, 128) if t == 0 else None}
+        for step in TAIL[last].split():
+            steps[step[0]](int(step[1]))
+
+    s = "sx%d" % NR
     for k in range(4):
         dma("s", "ds%d" % k, T.osc[4 * k:4 * k + 4, 0:C], (T[s][32 * k:32 * k + 4, 0:C], V(s, 0, C)[1]))
-    act(V("yr", cut, C), bank(1, 0, C - cut), COPY)
-    dma("a", "dyb", T.y[:, cut:C], V("yr", cut, C))
-    act(V("lvr", 0, E), by(V("lw", 0, E), V("pos", 0, 28)), IDEN, bias=-1.0)
-    dma("s", "dlv", T.lv[:, :], (T.lvr[0:128:16, 0:E], V("lvr", 0, E)[1]))
     for sem in count:
         g.wait_ge(T.sem[sem], count[sem])
     for sem in DMAS:

@@ -4,31 +4,37 @@ C, H, E, NR = 384, 64, 448, 3
 NV = (0, 11, 10)
 NE = (0, 24, 24)
 X2 = E + 16
-PL = 2 * X2
-BIG = 1.0e29
+SPLIT = 14
+HOME = (2, 3)
 CAP = 2.0 ** 25
 WHOLE = 12582912.0
-HW = 328
 CUTS = ((0, 128, 256, C), (0, 256, C))
-TAIL = ("N0 M0 G0 M1 M2 G1 M3 E2 E3 F2 P0 F3 U0 P1 P2 Q0 U1 Q1 U2 B0 Q2 K0 V0 B1 A0 V1 K1",
-        "N0 M0 L0 G0 M1 M2 G1 M3 F2 E3 E2 F3 P0 L1 U0 L2 Q0 P1 U1 Q1")
+MID = CUTS[0][-2]
+HW = max(MID, E - MID + 4)
+TURNS = ("M0 G0 M1 M2 M3 G1 G2 E3 F3 P0 U0 P1 U1 X1 X0 Q0 P2 U2 Q1 B1 X2 B0 K0 Q2 B2 H0 K1 H1",
+         "M0 G0 M1 M2 M3 G1 L0 G2 E3 P0 F3 L1 U0 X0 P1 L2 Q0 U1 X1 Q1 B0 B1")
+XS = ("444", "av")
+AHEAD = 40
+PASSES = 1
+EARLY = 300
+CYCLE, CALL, WAKE, TOL, GATHER, SCATTER, LOCAL, REMOTE, FIRST = 0.83, 45, 120, 60, 1.56, 3.5, 1500, 1700, 1500
 
 SCRATCH = {}
 for _k, _n in (("qu", 128), ("qur", 256), ("qv", 128), ("qw", 512), ("qe", 512), ("qz", C), ("qg", 128), ("qh", E)):
     SCRATCH[_k] = ("sbuf", [128, _n], "float8_e4m3fn_x4")
     SCRATCH["s" + _k[1:]] = ("sbuf", [128, _n], "uint8")
 for _k, _n in (("ut", 512), ("vt", 512), ("et", 2048), ("gt", 512), ("hl", 4 * E), ("zt", 4 * C), ("vp", 4 * E), ("x32", 4 * C),
-               ("vs", 4 * PL), ("mm", 4 * PL), ("hb", 128), ("ident", 128), ("grp", 128), ("ones", X2), ("t1", E), ("t2", E), ("w", E + 16),
-               ("w6", E), ("er", E + 16), ("junk", 4 * E), ("cb", 16 * E), ("sc", 8 * E), ("lane", E), ("cap", E), ("cap2", X2), ("tri", E),
-               ("hit", E), ("c0", 32), ("hw", 4 * HW), ("eq", E), ("eqs", E)):
+               ("vs", 4 * X2), ("mm", 4 * X2), ("mb", 4 * C), ("hb", 128), ("ident", 128), ("grp", 128), ("ones", 512), ("t1", E), ("t2", E),
+               ("t3", E), ("t4", E), ("w", E + 16), ("w6", E), ("er", E + 16), ("junk", 4 * E), ("cb", 16 * E), ("sc", 8 * E), ("lane", E),
+               ("cap", E), ("cap2", X2), ("tri", E), ("hit", E), ("c0", 32), ("hw1", 4 * HW), ("hw2", 4 * HW), ("eq", E), ("eqs", E)):
     SCRATCH[_k] = ("sbuf", [128, _n], "bfloat16")
-for _k, _n in (("iof", E), ("iq", E), ("pl", 1), ("pl1", 1), ("pq", 1), ("pg", 1), ("lama", 1), ("lam", 1), ("lamb", 1), ("lams", 1), ("acc0", 2),
-               ("hin", 4 * E), ("kr", 8 * E), ("held", E), ("own", 28), ("nown", 28), ("acc", 28), ("eq2", 28), ("posf", 28),
-               ("ordr", X2), ("held2", X2), ("yl", E), ("ks", X2), ("dk", E), ("lw", X2), ("lvr", E), ("yr", C)):
+for _k, _n in (("iof", E), ("iq", E), ("pl", 1), ("pl1", 1), ("pin", 1), ("pq", 3), ("pg", 3), ("lama", 1), ("lam", 1), ("lamb", 1), ("lams", 1), ("acc0", 2),
+               ("hin1", 4 * E), ("hin2", 4 * E), ("kr1", 4 * E), ("kr2", 8 * E), ("held", E), ("own", 28), ("nown", 28), ("acc", 28), ("eq2", 28),
+               ("posf", 28), ("ordr", X2), ("held2", X2), ("yl", E), ("ks", X2), ("dk", E), ("lw", X2), ("lvr", E), ("yr", C)):
     SCRATCH[_k] = ("sbuf", [128, _n], "float32")
-for _k, _n in (("uo", 16), ("bo", 28), ("pin", 1), ("pla", 1), ("plq", 1), ("plg", 1)):
+for _k, _n in (("uo", 16), ("bo", 28)):
     SCRATCH[_k] = ("sbuf", [128, _n], "int32")
-for _k, _n in (("uo16", 16), ("bo16", 28), ("pos", 28), ("pos2", 28), ("ordl", 30), ("ord4", 30)):
+for _k, _n in (("uo16", 16), ("bo16", 28), ("pos", 28), ("ordl", 30), ("ord4", 30)):
     SCRATCH[_k] = ("sbuf", [128, _n], "uint16")
 SCRATCH["ps"] = ("psum", [128, 4096], "float32")
 for _t in range(NR + 1):
@@ -54,111 +60,179 @@ def rank_program(g, core, T, topo):
     def send_engines(src, dst):
         return topo.engines(src, dst)[:8]
 
-    queue = {"v": g.vector, "a": g.scalar, "t": g.tensor, "g": g, "s": g.sync}
-    semof = {"v": "vec", "a": "act", "t": "ten", "g": "pool"}
-    count = {"vec": 0, "act": 0, "ten": 0, "pool": 0}
-    seen = {q: {} for q in queue}
+    calls = []
     hist = {}
+    turn = [None]
+    aside = [False]
 
     def V(name, lo, hi, step=1):
         k = (hi - lo + step - 1) // step
         mask = ((1 << (k * step)) - 1) // ((1 << step) - 1) << lo
-        return (T[name][:, lo:hi] if step == 1 else T[name][:, lo:hi:step], [(name, mask)])
+        return {"ap": T[name][:, lo:hi] if step == 1 else T[name][:, lo:hi:step], "at": [(name, mask)], "n": k,
+                "half": SCRATCH[name][2] in ("bfloat16", "uint16")}
 
     def bank(k, lo, hi):
-        return (T.ps[:, 512 * k + lo:512 * k + hi], [("ps", 1 << k)])
+        return {"ap": T.ps[:, 512 * k + lo:512 * k + hi], "at": [("ps", 1 << k)], "n": hi - lo, "half": False, "psum": True}
 
     def by(win, off):
-        return (win[0].indirect(off[0]), win[1], off[1])
+        return {"ap": win["ap"].indirect(off["ap"]), "at": win["at"], "n": 16 * off["n"], "half": False, "list": off["at"]}
 
-    def words32(v):
-        return (v[0].bitcast(dt.uint32), v[1])
+    def cast(v, d):
+        return dict(v, ap=v["ap"].bitcast(d))
 
-    def bytes8(v):
-        return (v[0].bitcast(dt.uint8), v[1])
-
-    def waits(q, reads, writes):
-        need = {}
+    def note(q, busy, done, issue, reads, writes, sem=None):
+        me, behind = len(calls), {}
         for regs, isw in ((reads, False), (writes, True)):
             for name, mask in regs:
-                for m, w, oq, sem, val in hist.get(name, ()):
-                    if m & mask and (w or (oq != q and (isw or name == "ps"))):
-                        need[sem] = max(need.get(sem, 0), val)
-        for sem in sorted(need):
-            if seen[q].get(sem, 0) < need[sem]:
-                queue[q].wait_ge(T.sem[sem], need[sem])
-                seen[q][sem] = need[sem]
-
-    def note(q, reads, writes, sem, val):
+                for m, w, k in hist.get(name, ()):
+                    other = calls[k]["q"] != q or calls[k]["sem"] is not None
+                    if m & mask and (w or isw or (other and name == "ps")):
+                        behind[k] = True
         for name, mask in writes:
-            hist[name] = [e for e in hist.get(name, ()) if e[0] & ~mask] + [(mask, True, q, sem, val)]
+            hist[name] = [e for e in hist.get(name, ()) if e[0] & ~mask] + [(mask, True, me)]
         for name, mask in reads:
-            hist.setdefault(name, []).append((mask, False, q, sem, val))
+            hist.setdefault(name, []).append((mask, False, me))
+        calls.append({"q": q, "busy": busy, "done": done, "issue": issue, "behind": behind, "place": me, "turn": turn[0], "aside": aside[0], "sem": sem})
 
-    def op(q, nout, fn, *args, **kw):
+    def op(q, nout, time, fn, *args, **kw):
         reads, writes = [], []
         for k, a in list(enumerate(args)) + list(kw.items()):
-            if isinstance(a, tuple):
-                (writes if k == "accum_out" or (k in range(nout)) else reads).extend(a[1])
-                if len(a) == 3:
-                    reads.extend(a[2])
-        waits(q, reads, writes)
-        sem = semof[q]
-        plain = lambda a: a[0] if isinstance(a, tuple) else a
-        fn(*[plain(a) for a in args], **{k: plain(a) for k, a in kw.items()}).then_inc(T.sem[sem], 1)
-        count[sem] += 1
-        note(q, reads, writes, sem, count[sem])
+            if isinstance(a, dict):
+                (writes if k == "accum_out" or k in range(nout) else reads).extend(a["at"])
+                reads.extend(a.get("list", []))
+        plain = lambda a: a["ap"] if isinstance(a, dict) else a
+        note(q, time, time, lambda: fn(*[plain(a) for a in args], **{k: plain(a) for k, a in kw.items()}), reads, writes)
 
-    def dma(q, sem, out, in_):
-        reads, writes = (in_[1] if isinstance(in_, tuple) else []), (out[1] if isinstance(out, tuple) else [])
-        waits(q, reads, writes)
-        queue[q].dma_start(out[0] if writes else out, in_[0] if reads else in_).then_inc(T.sem[sem], 16)
-        note("dma", reads, writes, sem, 16)
+    def dma(q, sem, out, in_, after=()):
+        reads, writes = (in_["at"] if isinstance(in_, dict) else []), (out["at"] if isinstance(out, dict) else [])
+        eng = {"s": g.sync, "a": g.scalar}[q]
+        side = out if writes else in_
+        note(q, 60, LOCAL + side["n"], lambda: eng.dma_start(out["ap"] if writes else out, in_["ap"] if reads else in_), reads + list(after), writes, (sem, 16))
+
+    def span(out, *ins, both=1.0):
+        if "list" in out or "list" in ins[0]:
+            return CALL + CYCLE * out["n"] * (SCATTER if "list" in out else GATHER)
+        return CALL + CYCLE * max(64, out["n"] * both * (0.5 if all(a["half"] for a in (out,) + ins) else 1.0))
 
     def tt(out, a, b, o):
-        op("v", 1, g.vector.tensor_tensor, out, a, b, o)
+        op("v", 1, span(out, a, b, both=1.0 if "psum" in a else 2.0), g.vector.tensor_tensor, out, a, b, o)
 
     def ts(out, a, s1, s2, *o):
-        op("v", 1, g.vector.tensor_scalar, out, a, s1, s2, *o)
+        op("v", 1, span(out, a), g.vector.tensor_scalar, out, a, s1, s2, *o)
 
     def tc(out, in_):
-        op("v", 1, g.vector.tensor_copy, out, in_)
+        op("v", 1, span(out, in_), g.vector.tensor_copy, out, in_)
 
     def scan(out, d0, d1, init, o0, o1):
-        op("v", 1, g.vector.tensor_tensor_scan, out, d0, d1, init, o0, o1)
+        op("v", 1, span(out, d0, d1), g.vector.tensor_tensor_scan, out, d0, d1, init, o0, o1)
 
     def act(out, in_, f, **kw):
-        op("a", 1, g.scalar.activation, out, in_, f, **kw)
+        op("a", 1, span(dict(out, half=False), in_) + 20 * ("accum_out" in kw), g.scalar.activation, out, in_, f, **kw)
 
     def fill(v, c):
-        op("v", 1, g.vector.memset, v, c)
+        op("v", 1, span(v, v), g.vector.memset, v, c)
 
-    def const(v, k, c):
-        act(v, V("ones", 0, k), COPY, scale=c)
+    def const(v, c):
+        act(v, V("ones", 0, v["n"]), COPY, scale=c)
 
     def iota(v, pattern, base, mult, **kw):
-        op("g", 1, g.iota, v, pattern, base, mult, **kw)
+        op("g", 1, 130 + 2 * CYCLE * v["n"], g.iota, v, pattern, base, mult, **kw)
 
     def quant(codes, src, lo, hi):
-        op("v", 2, g.vector.quantize_mx, V(codes, lo, hi), V("s" + codes[1:], lo, hi), V(src, 4 * lo, 4 * hi))
+        op("v", 2, CALL + 12 + 0.88 * (hi - lo), g.vector.quantize_mx, V(codes, lo, hi), V("s" + codes[1:], lo, hi), V(src, 4 * lo, 4 * hi))
 
     def mx(k, l, llo, r, rlo, rhi):
-        op("t", 1, g.tensor.matmul_mx, bank(k, 0, rhi - rlo), V(l, llo, llo + 128), V("s" + l[1:], llo, llo + 128),
+        op("t", 1, CYCLE * (rhi - rlo + 16), g.tensor.matmul_mx, bank(k, 0, rhi - rlo), V(l, llo, llo + 128), V("s" + l[1:], llo, llo + 128),
            V(r, rlo, rhi), V("s" + r[1:], rlo, rhi), True, True)
 
     def send(t):
         q, s = "qx%d" % t, "sx%d" % t
-        waits("g", V(q, 0, H)[1] + V(s, 0, H)[1], [])
-        rid, pid = topo.addr(prev)[0], topo.addr(prev)[1]
-        m = 0
-        for e in send_engines(core, prev):
-            m |= 1 << e
-        g.remote_dma(bytes8(V(q, C, E))[0], bytes8(V(q, 0, H))[0], T.sem["arr%d" % t], T.sem.left, pid, rid, m)
-        g.remote_dma(V(s, C, E)[0], V(s, 0, H)[0], T.sem["arr%d" % t], T.sem.left, pid, rid, m)
-        note("remote", [], V(q, C, E)[1] + V(s, C, E)[1], "arr%d" % t, 2 * len(send_engines(nxt, core)))
 
-    def hold(out, row, cap, k):
-        scan(V(out, 0, k), row, V(cap, 0, k), 0.0, MAX, MUL)
+        def issue():
+            rid, pid = topo.addr(prev)[0], topo.addr(prev)[1]
+            m = 0
+            for e in send_engines(core, prev):
+                m |= 1 << e
+            g.remote_dma(T[q][:, C:E].bitcast(dt.uint8), T[q][:, 0:H].bitcast(dt.uint8), T.sem["arr%d" % t], T.sem.left, pid, rid, m)
+            g.remote_dma(T[s][:, C:E], T[s][:, 0:H], T.sem["arr%d" % t], T.sem.left, pid, rid, m)
+
+        late = FIRST * (t == 0)
+        note("g", late + 500, late + 300 + REMOTE, issue, V(q, 0, H)["at"] + V(s, 0, H)["at"], V(q, C, E)["at"] + V(s, C, E)["at"],
+             ("arr%d" % t, 2 * len(send_engines(nxt, core))))
+
+    def issue_all():
+        queue = {"v": g.vector, "a": g.scalar, "t": g.tensor, "g": g, "s": g.sync}
+        semof = {"v": "vec", "a": "act", "t": "ten", "g": "pool"}
+        after = [[] for c in calls]
+        for k, c in enumerate(calls):
+            for j in c["behind"]:
+                after[j].append(k)
+        for k in reversed(range(len(calls))):
+            calls[k]["way"] = min([calls[j]["way"] - 0.001 for j in after[k]] + [len(calls) if calls[k]["aside"] else calls[k]["place"]])
+        gap = lambda j, hard: calls[j]["done"] + WAKE if hard else calls[j]["busy"]
+
+        def place(due):
+            todo = {q: sorted((k for k, c in enumerate(calls) if c["q"] == q), key=lambda k: (calls[k]["way"], k)) for q in queue}
+            free = {q: 0.0 for q in queue}
+            at, order = {}, []
+
+            def soonest(k, known):
+                if k not in known:
+                    known[k] = max([(at[j] if j in at else soonest(j, known)) + gap(j, hard) for j, hard in calls[k]["behind"].items()] + [free[calls[k]["q"]]])
+                return known[k]
+
+            for _ in calls:
+                known, offers = {}, []
+                for q in queue:
+                    limit = 1e18
+                    for k in todo[q][:AHEAD]:
+                        if all(j in at for j in calls[k]["behind"]) and soonest(k, known) + calls[k]["busy"] <= limit:
+                            offers.append((known[k], calls[k]["way"], k))
+                        limit = min(limit, max(soonest(k, known) + TOL, due.get(k, 0)))
+                        if limit < free[q] + CALL + TOL:
+                            break
+                t, _, k = min(offers)
+                todo[calls[k]["q"]].remove(k)
+                at[k], free[calls[k]["q"]] = t, t + calls[k]["busy"]
+                order.append(k)
+            return at, order
+
+        at, order = place({})
+        for _ in range(PASSES):
+            due = {}
+            for k in reversed(range(len(calls))):
+                if calls[k]["aside"]:
+                    due[k] = min([due.get(j, at[j]) - gap(k, calls[j]["behind"][k]) - EARLY for j in after[k]] + [1e18])
+            at, order = place(due)
+        count = {s: 0 for s in semof.values()}
+        seen = {q: {} for q in queue}
+        for k in order:
+            c = calls[k]
+            q = c["q"]
+            need = {}
+            for j, hard in c["behind"].items():
+                if hard:
+                    sem, val = calls[j]["sem"]
+                    need[sem] = max(need.get(sem, 0), val)
+            for sem in sorted(need):
+                if seen[q].get(sem, 0) < need[sem]:
+                    queue[q].wait_ge(T.sem[sem], need[sem])
+                    seen[q][sem] = need[sem]
+            made = c["issue"]()
+            if c["sem"] is None:
+                count[semof[q]] += 1
+                c["sem"] = (semof[q], count[semof[q]])
+                made.then_inc(T.sem[semof[q]], 1)
+            elif made is not None:
+                made.then_inc(T.sem[c["sem"][0]], 16)
+        for sem in count:
+            g.wait_ge(T.sem[sem], count[sem])
+        for sem in DMAS:
+            g.wait_ge(T.sem[sem], 16)
+        g.wait_ge(T.sem.left, 2 * NR * len(send_engines(core, prev)))
+
+    def hold(out, row, cap):
+        scan(out, row, V(cap, 0, out["n"]), 0.0, MAX, MUL)
 
     def ends(name, lo=0, hi=28):
         return V(name, 16 * lo + 15, 16 * hi, 16)
@@ -167,84 +241,113 @@ def rank_program(g, core, T, topo):
     dma("s", "dxa", V("xt0", 0, 512), T.x[:, 0:512])
     dma("a", "du", V("ut", 0, 512), T.u[:, :])
     dma("s", "dxb", V("xt0", 512, 1536), T.x[:, 512:1536])
-    iota(V("pin", 0, 1), [[0, 1]], 0, 1)
-    iota(V("lane", 0, E), [[0, 28], [1, 16]], 0, 0, **FL)
-    fill(V("hb", 0, 128), 0.5)
-    fill(V("ones", 0, X2), 1.0)
-    iota(V("uo", 0, 16), [[1, 2], [16, 8]], 0, 0)
-    iota(V("grp", 0, 128), [[1, 8], [0, 16]], 0, 0, **FL)
-    op("g", 1, g.affine_select, V("ident", 0, 128), V("hb", 0, 128), [[-1, 128]], EQ, 0.0, 0, 1)
-    ts(V("pla", 0, 1), V("pin", 0, 1), 15, None, AND)
-    ts(V("plq", 0, 1), V("pin", 0, 1), 2, 3, SHR, AND)
-    ts(V("plg", 0, 1), V("pin", 0, 1), 4, None, SHR)
-    for nm, src in (("pl", "pla"), ("pq", "plq"), ("pg", "plg")):
-        tc(V(nm, 0, 1), V(src, 0, 1))
-    ts(V("tri", 0, E), V("lane", 0, E), V("pl", 0, 1), None, GT)
-    ts(V("hit", 0, E), V("lane", 0, E), V("pl", 0, 1), CAP, EQ, MUL)
-    tc(V("uo16", 0, 16), V("uo", 0, 16))
-    tt(V("cap", 0, E), V("tri", 0, E), V("hit", 0, E), ADD)
-    for b, c in enumerate((1.0, 1.0, 256.0, 0.0)):
-        ts(V("gt", b, 512, 4), V("grp", 0, 128), V("pg", 0, 1), c, EQ, MUL)
-    for lo in range(0, 2048, 416):
-        const(V("et", lo, min(lo + 416, 2048)), min(416, 2048 - lo), 0.0)
-    for b in range(4):
-        act(V("et", 512 * b + b, 512 * b + 512, 4), V("ident", 0, 128), COPY)
     quant("qx0", "xt0", 0, 128)
     send(0)
+    halo = V("qx0", C, E)["at"]
+    dma("s", "dwc", cast(V("qw", 0, 512), dt.uint8), T.wc[:, :], halo)
+    dma("s", "dws", V("sw", 0, 512), T.ws[:, :], halo)
+    dma("s", "dv", V("vt", 0, 512), T.v[:, :], halo)
+    aside[0] = True
+    iota(V("pin", 0, 1), [[0, 1]], 0, 1, **FL)
+    iota(V("lane", 0, 16), [[1, 16]], 0, 0, **FL)
+    iota(V("uo", 0, 16), [[1, 2], [16, 8]], 0, 0)
+    iota(V("grp", 0, 128), [[1, 8], [0, 16]], 0, 0, **FL)
     iota(V("iof", 0, E), [[1, E]], 1, 0, **FL)
     iota(V("bo", 0, 28), [[1, 28]], 0, 0)
+    fill(V("ones", 0, 512), 1.0)
+    op("g", 1, 170 + 2 * CYCLE * 128, g.affine_select, V("ident", 0, 128), V("ones", 0, 128), [[-1, 128]], EQ, 0.0, 0, 1)
+    for nm, src, k in (("uo16", "uo", 16), ("bo16", "bo", 28)):
+        tc(V(nm, 0, k), V(src, 0, k))
+
+    def whole(out, src, by_):
+        act(V(out, 1, 2), V(src, 0, 1), IDEN, scale=1.0 / by_, bias=0.5 / by_ - 0.5)
+        act(V(out, 2, 3), V(out, 1, 2), IDEN, bias=WHOLE)
+        act(V(out, 0, 1), V(out, 2, 3), IDEN, bias=-WHOLE)
+
+    whole("pg", "pin", 16)
+    act(V("pl", 0, 1), V("pg", 0, 1), IDEN, scale=-16.0, bias=V("pin", 0, 1))
+    whole("pq", "pl", 4)
+    ts(V("pl1", 0, 1), V("pl", 0, 1), 1.0, None, MAX)
+    for out, tri, p in (("cap", V("tri", 0, 16), "pl"), ("cap2", V("c0", 0, 16), "pl1")):
+        ts(tri, V("lane", 0, 16), V(p, 0, 1), None, GT)
+        ts(V("c0", 16, 32), V("lane", 0, 16), V(p, 0, 1), CAP, EQ, MUL)
+        tt(V(out, 0, 16), tri, V("c0", 16, 32), ADD)
+        act(V(out, 15, 16), V(out, 15, 16), COPY, scale=-1.0 / CAP)
+    for name in ("cap", "tri"):
+        for k in (16, 32, 64, 128, 256):
+            act(V(name, k, min(2 * k, E)), V(name, 0, min(k, E - k)), COPY)
+    act(V("cap2", 16, E), V("cap", 16, E), COPY)
+    const(V("cap2", E + 1, X2 - 1), 1.0)
+    const(V("cap2", E, E + 1), CAP)
+    const(V("cap2", X2 - 1, X2), -1.0 / CAP)
+    ts(V("gt", 0, 512, 4), V("grp", 0, 128), V("pg", 0, 1), None, EQ)
+    for b, c in ((1, 1.0), (2, 256.0), (3, 0.0)):
+        act(V("gt", b, 512, 4), V("gt", 0, 512, 4), COPY, scale=c)
+    quant("qg", "gt", 0, 128)
+    for b in range(4):
+        const(V("et", 512 * b, 512 * b + 512), 0.0)
+        act(V("et", 512 * b + b, 512 * b + 512, 4), V("ident", 0, 128), COPY, scale=0.5)
+        quant("qe", "et", 128 * b, 128 * b + 128)
+    act(V("lama", 0, 1), V("pq", 0, 1), IDEN, bias=1.0)
+    act(V("lam", 0, 1), V("pl", 0, 1), IDEN, scale=2.0, bias=V("lama", 0, 1))
+    act(V("lamb", 0, 1), V("lam", 0, 1), IDEN, bias=-1.0)
+    act(V("lams", 0, 1), V("lam", 0, 1), IDEN, bias=-0.5)
+    const(V("w", E, E + 16), -2.0)
+    const(V("er", E, E + 16), -1.5)
+    const(V("hl", 3, 4 * E, 4), 0.0)
+    const(V("ordr", 0, X2, X2 - 1), 0.0)
+    const(V("ordr", E + 1, X2 - 1), 0.0)
+    for lo, hi, c in ((0, MID, 18.5), (MID, E, 0.0)):
+        act(V("iq", lo, hi), V("iof", lo, hi), IDEN, scale=1.0 / 512, bias=c + 2.5 - 225.0 / 512)
+    for t, far in ((1, 18.5), (2, 1336.0)):
+        for b, c in enumerate((0.0, 2.0, far, 2.0)):
+            const(V("hw%d" % t, b, 4 * HW, 4), c)
+    const(V("hin1", 4 * (E - 2) + 3, 4 * E, 4), 0.0)
+    const(V("hin1", 4 * (E - 3) + 3, 4 * (E - 2)), -1.0)
+    const(V("hin1", 4 * (E - 1) + 1, 4 * (E - 1) + 2), 0.0)
+    for b in (2, 3):
+        const(V("hin2", 4 * (E - 4) + b, 4 * E, 4), 0.0)
     quant("qu", "ut", 0, 128)
-    tc(words32(V("qur", 0, 256)), by(words32(V("qu", 0, 128)), V("uo16", 0, 16)))
+    tc(cast(V("qur", 0, 256), dt.uint32), by(cast(V("qu", 0, 128), dt.uint32), V("uo16", 0, 16)))
     act(V("sur", 0, 256), by(V("su", 0, 128), V("uo16", 0, 16)), COPY)
     quant("qx0", "xt0", 128, C)
-    quant("qe", "et", 0, 512)
-    quant("qg", "gt", 0, 128)
-    act(V("lama", 0, 1), V("pq", 0, 1), IDEN, scale=0.5, bias=0.5)
-    const(V("w", E, E + 16), 16, -0.5)
-    const(V("er", E, E + 16), 16, -0.75)
-    act(V("lam", 0, 1), V("pl", 0, 1), IDEN, bias=V("lama", 0, 1))
-    const(V("hl", 3, 4 * E, 4), E, 0.0)
-    act(V("lamb", 0, 1), V("lam", 0, 1), IDEN, bias=-0.5)
-    act(V("lams", 0, 1), V("lam", 0, 1), IDEN, bias=-0.25)
-    act(ends("cap"), ends("cap"), COPY, scale=-1.0 / CAP)
+    quant("qv", "vt", 0, 128)
     for b in range(4):
         act(V("vp", E * b, E * b + C), V("xt0", b, 4 * C, 4), COPY, scale=0.5)
-    waits("s", V("qx0", C, E)[1], [])
-    dma("s", "dwc", bytes8(V("qw", 0, 512)), T.wc[:, :])
-    dma("s", "dws", V("sw", 0, 512), T.ws[:, :])
-    dma("s", "dv", V("vt", 0, 512), T.v[:, :])
+        act(V("x32", C * b, C * b + C), V("xt0", C * b, C * b + C), COPY, scale=32.0)
+    aside[0] = False
 
     def words0(k, sl, lo, hi, klo, khi):
-        ts(V("t1", lo, hi), bank(k, sl, sl + hi - lo), 0.0, 2.0, GT, MUL)
-        ts(V("t2", lo, hi), bank(k + 1, sl, sl + hi - lo), 0.0, None, GT)
+        act(V("t2", lo, hi), bank(k, sl, sl + hi - lo), SIGN, bias=-1.0e-36)
+        ts(V("t1", lo, hi), bank(k + 1, sl, sl + hi - lo), 0.0, 4.0, GT, MUL)
         tt(V("w", lo, hi), V("t1", lo, hi), V("t2", lo, hi), ADD)
-        ts(V("w6", klo, khi), V("w", klo, khi), 4.5, 0.5, MUL, ADD)
+        ts(V("w6", klo, khi), V("w", klo, khi), 4.5, 6.5, MUL, ADD)
         tt(V("er", klo, khi), V("w6", klo, khi), V("w", klo + 1, khi + 1), ADD)
 
-    def span(t, lo, hi):
-        d = 2 ** t
-        return d, max(lo - d, 0), hi if hi == E else hi - d
-
-    def bits(t, k, lo, hi):
-        d, klo, khi = span(t, lo, hi)
+    def keys(t, k, lo, hi):
+        d, hin = 2 ** t, "hin%d" % t
+        klo, khi = max(lo - d, 0), hi if hi == E else hi - d
         top = hi - 1 if (t, hi) == (1, E) else hi
-        act(V("hin", 4 * klo + 3, 4 * (top - d), 4), bank(k, klo + d - lo, top - lo), SIGN, bias=-1.0e-36)
-        ts(V("hin", 4 * lo + 1, 4 * top, 4), bank(k + 1, 0, top - lo), 0.0, 2.0, GT, MUL)
-
-    def keys(t, lo, hi):
-        d, klo, khi = span(t, lo, hi)
-        scan(V("kr", 4 * klo, 4 * khi), V("hw", 0, 4 * (khi - klo)), V("hin", 4 * klo, 4 * khi), 0.0, MUL, ADD)
+        act(V(hin, 4 * klo + 3, 4 * (top - d), 4), bank(k, klo + d - lo, top - lo), SIGN, bias=-1.0e-36)
+        if hi < E:
+            act(V(hin, 4 * lo + 1, 4 * top, 4), bank(k, 0, top - lo), SIGN, bias=-1.0e-36)
+        else:
+            ts(V(hin, 4 * lo + 1, 4 * top, 4), bank(k + 1, 0, top - lo), 0.0, 2.0, GT, MUL)
+        if hi < MID:
+            return
+        klo = klo if hi == E else 0
+        turn[0] = "K%d" % (hi == E)
+        scan(V("kr%d" % t, 4 * klo, 4 * khi), V("hw%d" % t, 0, 4 * (khi - klo)), V(hin, 4 * klo, 4 * khi), 0.0, MUL, ADD)
 
     def unpack(t, k):
+        aside[0] = True
         for b in range(4):
             mx(k + b, "qe", 128 * b, "qx%d" % t, E - 128, E)
-        for b in range(4):
             act(V("vp", E * b + C, E * b + E), bank(k + b, 64, 128), COPY)
+        aside[0] = False
 
     def scatter(lo, hi):
         tc(by(V("ordr", 0, X2), V("pos", lo, hi)), V("iof", 16 * lo, 16 * hi))
-
-    K = V("kr", 3, 4 * E, 4)
 
     for t in range(NR):
         qx = "qx%d" % t
@@ -252,184 +355,155 @@ def rank_program(g, core, T, topo):
         nv, ne = NV[t], NE[t]
         if t == 0:
             O = lambda lo, hi: V("hl", 4 * lo + 2, 4 * hi, 4)
-            mx(0, "qur", 0, qx, 0, C)
-            mx(1, "qur", 128, qx, 0, C)
-            mx(2, "qur", 0, qx, E - 128, E)
-            mx(3, "qur", 128, qx, E - 128, E)
-            words0(0, 0, 0, C, 0, C - 1)
-            act(V("junk", 0, C - 1), V("er", 0, C - 1), SIGN, bias=V("lams", 0, 1), scale=-1.0, accum_out=V("acc0", 0, 1))
-            ts(O(0, C - 1), V("er", 0, C - 1), V("lam", 0, 1), None, EQ)
-            act(V("acc0", 0, 1), V("acc0", 0, 1), IDEN, scale=0.5, bias=31.0)
-            words0(2, 64, C, E, C - 1, E)
-            act(V("junk", E, E + 65), V("er", C - 1, E), SIGN, bias=V("lams", 0, 1), scale=-1.0, accum_out=V("acc0", 1, 2))
-            ts(O(C - 1, E - 1), V("er", C - 1, E - 1), V("lam", 0, 1), None, EQ)
-            ts(O(E - 1, E), V("er", E - 1, E), V("lamb", 0, 1), None, EQ)
-            ts(V("pl1", 0, 1), V("pl", 0, 1), 1.0, None, MAX)
-            ts(V("t1", E - 1, E), V("acc0", 1, 2), 0.5, V("acc0", 0, 1), MUL, ADD)
-            ts(V("c0", 0, 16), V("lane", 0, 16), V("pl1", 0, 1), None, GT)
-            scan(V("t1", 0, E - 1), V("ones", 0, E - 1), O(0, E - 1), V("t1", E - 1, E), MUL, ADD)
-            ts(V("c0", 16, 32), V("lane", 0, 16), V("pl1", 0, 1), CAP, EQ, MUL)
-            tt(V("t2", 0, E), V("t1", 0, E), O(0, E), MUL)
-            tt(V("cap2", 0, 16), V("c0", 0, 16), V("c0", 16, 32), ADD)
-            ts(V("hl", 0, 4 * E, 4), V("t2", 0, E), 16 * WHOLE, -16 * WHOLE, ADD, ADD)
-            tc(V("bo16", 0, 28), V("bo", 0, 28))
-            tt(V("hl", 1, 4 * E, 4), V("t2", 0, E), V("hl", 0, 4 * E, 4), SUB)
-            quant("qh", "hl", 0, E)
-            act(V("iq", 0, E), V("iof", 0, E), IDEN, scale=1.0 / 1024, bias=1.25 - 225.0 / 1024)
+            mx(0, "qur", 128, qx, 0, C)
+            mx(1, "qur", 0, qx, 0, C)
+            mx(2, "qur", 128, qx, E - 128, E)
+            mx(3, "qur", 0, qx, E - 128, E)
             unpack(t, 4)
-            mx(0, "qg", 0, "qh", 0, E)
-            const(V("ordr", 0, X2), X2, 0.0)
-            act(V("cap2", 15, 16), V("cap2", 15, 16), COPY, scale=-1.0 / CAP)
-            act(V("cap2", 16, E), V("cap", 16, E), COPY)
-            const(V("cap2", E + 1, X2 - 1), 14, 1.0)
-            const(V("cap2", E, E + 1), 1, CAP)
-            const(V("cap2", X2 - 1, X2), 1, -1.0 / CAP)
-            for b in range(4):
-                const(V("vs", PL * b, PL * b + PL, 2), X2, BIG)
-            for b in range(4):
-                act(V("x32", C * b, C * b + C), V("xt0", b, 4 * C, 4), COPY, scale=32.0)
-            tt(V("hin", 2, 4 * E, 4), V("er", 2, E + 2), V("iq", 0, E), ADD)
-            hold("held", bank(0, 0, E), "cap", E)
+            words0(0, 0, 0, C, 0, C - 1)
+            words0(2, 64, C, E, C - 1, E)
+            for k, (lo, hi) in enumerate(((0, C - 1), (C - 1, E))):
+                act(V("junk", lo, hi), V("er", lo, hi), SIGN, bias=V("lams", 0, 1), scale=-1.0, accum_out=V("acc0", k, k + 1))
+                ts(O(lo, min(hi, E - 1)), V("er", lo, min(hi, E - 1)), V("lam", 0, 1), None, EQ)
+            act(V("acc0", 0, 1), V("acc0", 0, 1), IDEN, scale=0.5, bias=31.0)
+            ts(O(E - 1, E), V("er", E - 1, E), V("lamb", 0, 1), None, EQ)
+            ts(V("t3", E - 1, E), V("acc0", 1, 2), 0.5, V("acc0", 0, 1), MUL, ADD)
+            scan(V("t3", 0, E - 1), V("ones", 0, E - 1), O(0, E - 1), V("t3", E - 1, E), MUL, ADD)
+            halves = ((0, 224), (224, E))
+            for lo, hi in halves:
+                tt(V("t4", lo, hi), V("t3", lo, hi), O(lo, hi), MUL)
+            for lo, hi in halves:
+                ts(V("hl", 4 * lo, 4 * hi, 4), V("t4", lo, hi), 16 * WHOLE, -16 * WHOLE, ADD, ADD)
+            for lo, hi in halves:
+                tt(V("hl", 4 * lo + 1, 4 * hi, 4), V("t4", lo, hi), V("hl", 4 * lo, 4 * hi, 4), SUB)
+            for k, (lo, hi) in enumerate(halves):
+                quant("qh", "hl", lo, hi)
+                mx(k, "qg", 0, "qh", lo, hi)
+            for k, (lo, hi) in enumerate(halves):
+                hold(V("held", lo, hi), bank(k, 0, hi - lo), "cap")
             ts(V("pos", 0, 28), ends("held"), -1.0, -63.0, MUL, ADD)
             scatter(0, 28)
+            aside[0] = True
+            act(V("hin1", 0, 4 * E, 4), V("er", 0, E), COPY)
+            for lo in range(0, E, 112):
+                tt(V("hin1", 4 * lo + 2, 4 * lo + 448, 4), V("er", lo + 2, lo + 114), V("iq", lo, lo + 112), ADD)
+            aside[0] = False
         else:
-            hold("held", K, "cap", E)
-            row = lambda c: V("kr", 4 * (16 * c + 16) + 3, 4 * (16 * c + 16 + E), 4) if last else K
+            kr = "kr%d" % t
+            K = V(kr, 3, 4 * E, 4)
+            unpack(t, 4 - free)
+            row = lambda c: V(kr, 4 * (16 * c + 16) + 3, 4 * (16 * c + 16 + E), 4) if last else K
             if last:
-                act(V("kr", 4 * E + 3, 8 * E, 4), K, IDEN, bias=-2.0)
+                act(V(kr, 4 * E + 3, 8 * E, 4), K, IDEN, bias=-2.0)
                 act(V("nown", 0, 28), ends("held"), IDEN, bias=1.0)
+                ts(V("own", 0, 28), ends("held"), -1.0, None, MUL)
+                tt(V("eq", 0, E), by(V("own", 0, 28), V("bo16", 0, 28)), K, EQ)
+                scan(V("eqs", 0, E), V("eq", 0, E), V("tri", 0, E), 0.0, ADD, MUL)
+                ts(V("eq2", 0, 28), ends("eqs"), 2.0, None, MUL)
+            else:
+                aside[0] = True
+                act(V("yl", 0, E), K, IDEN, scale=0.5, bias=WHOLE)
+                act(V("hin2", 0, 4 * E, 4), V("yl", 0, E), IDEN, scale=2.0, bias=-2 * WHOLE)
+                act(V("hin2", 2, 4 * MID, 4), V("yl", 4, MID + 4), IDEN, scale=2.0, bias=1336.0 - 2 * WHOLE)
+                act(V("hin2", 4 * MID + 2, 4 * (E - 4), 4), V("yl", MID + 4, E), IDEN, scale=2.0, bias=-2 * WHOLE)
+                aside[0] = False
             for c in range(nv, 28):
                 act(V("junk", E * (c % 4), E * (c % 4) + E), row(c), SIGN, bias=V("nown", c, c + 1) if last else ends("held", c, c + 1),
                     accum_out=V("acc", c, c + 1))
-            unpack(t, 4 - free)
-            if last:
-                ts(V("own", 0, 28), ends("held"), -1.0, None, MUL)
             for c in range(nv):
                 if last:
                     ts(V("cb", E * c, E * c + E), row(c), V("own", c, c + 1), -0.5, GE, ADD)
                 else:
                     ts(V("cb", E * c, E * c + E), row(c), ends("held", c, c + 1), 0.0, ADD, LT)
-                if last and c == 0:
-                    tt(V("eq", 0, E), by(V("own", 0, 28), V("bo16", 0, 28)), K, EQ)
-                if last and c == 1:
-                    scan(V("eqs", 0, E), V("eq", 0, E), V("tri", 0, E), 0.0, ADD, MUL)
-            if last:
-                ts(V("eq2", 0, 28), ends("eqs"), 2.0, None, MUL)
             for c in range(nv):
                 scan(V("sc", 224 * c, 224 * c + 224), V("cb", E * c, E * c + 224), V("cb", E * c + 224, E * c + E),
                      ends("eqs", c, c + 1) if last else -192.0, ADD, ADD)
-                if last and c == nv - 2:
-                    tt(V("posf", nv, ne), V("acc", nv, ne), V("eq2", nv, ne), ADD)
-
-            def signs(lo, hi):
-                ts(V("pos", lo, hi), V("posf" if last else "acc", lo, hi), -0.5, 224.0 if last else 224.5, MUL, ADD)
-
-            signs(nv, ne)
             ts(V("pos", 0, nv), V("sc", 223, 224 * nv, 224), *((-1.0, 224.0) if last else (1.0, 193.0)), MUL, ADD)
-            scatter(0, ne)
-            if last:
-                tt(V("posf", ne, 28), V("acc", ne, 28), V("eq2", ne, 28), ADD)
-            signs(ne, 28)
-            scatter(ne, 28)
-        hold("held2", V("ordr", 0, X2), "cap2", X2)
-        ts(V("ordl", 0, 29), ends("held2", 0, 29), -1.0, -1.0, MUL, ADD)
-        into = lambda b, lo, hi: (V("vs", PL * b + 32 * lo + 1, PL * b + 32 * hi, 2), by(V("vp", E * b, E * b + E), V("ordl", lo, hi)))
-        act(*into(0, 14, 29), COPY)
-        tc(*into(0, 0, 14))
-        for b in range(1, 4):
-            act(*into(b, 0, 29), COPY)
-        if t == 0:
-            act(V("hin", 0, 4 * E, 4), V("er", 0, E), COPY)
-            for b, c in enumerate((0.0, 4.0, 9.25, 4.0)):
-                const(V("hw", b, 4 * HW, 4), HW, c)
-            const(V("hin", 4 * (E - 2) + 3, 4 * E, 4), 2, 0.0)
-            const(V("hin", 4 * (E - 3) + 3, 4 * (E - 2)), 1, -1.0)
-            const(V("hin", 4 * (E - 1) + 1, 4 * (E - 1) + 2), 1, 0.0)
-        elif t == 1:
-            act(V("yl", 0, E), K, IDEN, scale=0.5, bias=WHOLE)
-            const(V("hw", 2, 4 * HW, 4), HW, 668.0)
-            act(V("hin", 0, 4 * E, 4), V("yl", 0, E), IDEN, bias=-WHOLE)
-            act(V("hin", 2, 4 * (E - 4), 4), V("yl", 4, E), IDEN, bias=-WHOLE)
-            for b in (2, 3):
-                const(V("hin", 4 * (E - 4) + b, 4 * E, 4), 4, 0.0)
-
+            for lo, hi in ((nv, ne), (ne, 28)):
+                if last:
+                    tt(V("posf", lo, hi), V("acc", lo, hi), V("eq2", lo, hi), ADD)
+                ts(V("pos", lo, hi), V("posf" if last else "acc", lo, hi), -0.5, 224.0 if last else 224.5, MUL, ADD)
+                scatter(0 if lo == nv else lo, hi)
+        for lo, hi in ((0, SPLIT), (SPLIT, 29)):
+            scan(V("held2", 16 * lo, 16 * hi), V("ordr", 16 * lo, 16 * hi), V("cap2", 16 * lo, 16 * hi), 0.0, MAX, MUL)
+        for lo, hi in ((0, SPLIT), (SPLIT, 29)):
+            ts(V("ordl", lo, hi), ends("held2", lo, hi), -1.0, -1.0, MUL, ADD)
         cuts = CUTS[last]
+        pieces = list(enumerate(zip(cuts, cuts[1:])))
         free = 4 * ((len(cuts) + 1) % 2)
-
-        def most(b):
-            o = PL * b
-            scan(V("mm", o, o + 2 * E), V("vs", o + 4, o + 4 + 2 * E), V("vs", o + 1, o + 1 + 2 * E), 0.0, MAX, MIN)
-
-        def fused(b, lo, hi):
-            tt(V("zt", 4 * lo + b, 4 * hi, 4), by(V("mm", PL * b, PL * b + 2 * E), V("pos2", lo // 16, hi // 16)), V("vp", E * b + lo, E * b + hi), ADD)
-
+        into = lambda b, lo, hi: (V("vs", X2 * b + 16 * lo, X2 * b + 16 * hi), by(V("vp", E * b, E * b + E), V("ordl", lo, hi)))
+        back = lambda b, lo, hi: by(V("mm", X2 * b, X2 * b + X2), V("pos", lo // 16, hi // 16))
+        tc(*into(0, SPLIT, 29))
+        for b in range(4):
+            act(*into(b, 0, SPLIT if b == 0 else 29), COPY)
+        turns = TURNS[last].split()
+        first = len(calls)
+        for b in range(4):
+            o = X2 * b
+            turn[0] = "M%d" % b
+            tt(V("mm", o + 1, o + 1 + E), V("vs", o, o + E), V("vs", o + 2, o + 2 + E), MAX)
+            if b in HOME:
+                act(V("mb", C * b, C * b + C), back(b, 0, C), COPY)
+            for name, lo, hi in (("G", 0, C), ("E", 0, cuts[1]), ("F", cuts[1], C)):
+                turn[0] = name + str(b)
+                if turn[0] in turns:
+                    tt(V("zt", 4 * lo + b, 4 * hi, 4), V("mb", C * b + lo, C * b + hi) if b in HOME else back(b, lo, hi), V("vp", E * b + lo, E * b + hi), ADD)
+        if last:
+            turn[0] = "L0"
+            ts(V("ord4", 0, 29), V("ordl", 0, 29), 4.0, 3.0, MUL, ADD)
+            act(V("ks", 0, X2), by(V(kr, 0, 4 * E), V("ord4", 0, 29)), COPY, scale=256.0)
+            turn[0] = "L1"
+            for lo in (0, 224):
+                tt(V("dk", lo, lo + 224), V("ks", lo + 1, lo + 225), V("ks", lo, lo + 224), SUB)
+            turn[0] = "L2"
+            scan(V("lw", 1, E + 1), V("dk", 0, E), V("iof", 0, E), 1.0, ADD, MIN)
+            act(V("lvr", 0, E), by(V("lw", 0, X2), V("pos", 0, 28)), IDEN, bias=-1.0)
+            dma("s", "dlv", T.lv[:, :], dict(V("lvr", 0, E), ap=T.lvr[0:128:16, 0:E], n=0))
         xn, qn = "xt%d" % (t + 1), "qx%d" % (t + 1)
-
-        def product(k):
-            lo, hi = cuts[k:k + 2]
+        for k, (lo, hi) in pieces:
+            turn[0] = "P%d" % k
             quant("qz", "zt", lo, hi)
             for b in range(4):
                 mx(4 * (k % 2) + b, "qw", 128 * b, "qz", lo, hi)
-
-        def update(k):
-            lo, hi = cuts[k:k + 2]
             for b in range(4):
-                x = V("x32", C * b + lo, C * b + hi)
+                x = V("x32", 4 * lo + b, 4 * hi, 4)
+                turn[0] = "U%d" % k
                 tt(x, bank(4 * (k % 2) + b, 0, hi - lo), x, ADD)
-            for b in range(4):
-                o, i = V(xn, 4 * lo + b, 4 * hi, 4), V("x32", C * b + lo, C * b + hi)
-                if b < 3 or hi < C:
-                    act(o, i, COPY, scale=0.03125)
-                else:
-                    ts(o, i, 0.03125, None, MUL)
-
-        def state(k):
-            lo, hi = cuts[k:k + 2]
+                turn[0] = "X%d" % k
+                if XS[last][k] == "4":
+                    act(V(xn, 4 * lo + b, 4 * hi, 4), x, COPY, scale=0.03125)
+            if XS[last][k] == "a":
+                act(V(xn, 4 * lo, 4 * hi), V("x32", 4 * lo, 4 * hi), COPY, scale=0.03125)
+            elif XS[last][k] == "v":
+                ts(V(xn, 4 * lo, 4 * hi), V("x32", 4 * lo, 4 * hi), 0.03125, None, MUL)
+            turn[0] = "Q%d" % k
             quant(qn, xn, lo, hi)
             if k == 0 and not last:
                 send(t + 1)
-            if hi < cuts[-2]:
-                return
-            k, lo = (0, 0) if hi < C else (1, lo)
+        for k, (lo, hi) in enumerate(((0, cuts[-2]), (cuts[-2], C))):
+            turn[0] = "B%d" % k
             if last:
-                dma("s", "dc" + "ab"[k], T.oc[:, 4 * lo:4 * hi], bytes8(V(qn, lo, hi)))
+                dma("s", "dc" + "ab"[k], T.oc[:, 4 * lo:4 * hi], cast(V(qn, lo, hi), dt.uint8))
                 mx(free + k, "qv", 0, qn, lo, hi)
                 act(V("yr", lo, hi), bank(free + k, 0, hi - lo), COPY)
                 dma("a", "dy" + "ab"[k], T.y[:, lo:hi], V("yr", lo, hi))
             else:
-                for j in range(2):
-                    mx(free + 2 * k + j, "qur", 0, qn, lo, E if k else hi)
-
-        def planes(k):
-            lo, hi = ((0, cuts[-2]), (cuts[-2], C))[k]
-            for b in range(4):
-                act(V("vp", E * b + lo, E * b + hi), V("x32", C * b + lo, C * b + hi), COPY, scale=2.0 ** -6)
-
-        def levels(k):
-            if k == 0:
-                ts(V("ord4", 0, 29), V("ordl", 0, 29), 4.0, 3.0, MUL, ADD)
-                act(V("ks", 0, X2), by(V("kr", 0, 4 * E), V("ord4", 0, 29)), COPY, scale=256.0)
-            elif k == 1:
-                tt(V("dk", 0, E), V("ks", 1, E + 1), V("ks", 0, E), SUB)
-            else:
-                scan(V("lw", 1, E + 1), V("dk", 0, E), V("iof", 0, E), 1.0, ADD, MIN)
-                act(V("lvr", 0, E), by(V("lw", 0, X2), V("pos", 0, 28)), IDEN, bias=-1.0)
-                dma("s", "dlv", T.lv[:, :], (T.lvr[0:128:16, 0:E], V("lvr", 0, E)[1]))
-
-        part = lambda k: ((0, cuts[-2]), (cuts[-2], E))[k]
-        steps = {"M": most, "E": lambda b: fused(b, 0, cuts[1]), "F": lambda b: fused(b, cuts[1], C), "G": lambda b: fused(b, 0, C),
-                 "P": product, "U": update, "Q": state, "V": planes, "L": levels,
-                 "N": lambda k: ts(V("pos2", 0, 28), V("pos", 0, 28), 2.0, -1.0, MUL, ADD),
-                 "B": lambda k: bits(t + 1, free + 2 * k, *part(k)), "K": lambda k: keys(t + 1, *part(k)),
-                 "A": lambda k: quant("qv", "vt", 0, 128) if t == 0 else None}
-        for step in TAIL[last].split():
-            steps[step[0]](int(step[1]))
+                for j, (a, z) in pieces[:-1] if k == 0 else ((2, (lo, E)),):
+                    turn[0] = "B%d" % j
+                    for i in range(k + 1):
+                        mx(free + j + i, "qur", 0, qn, a, z)
+                    keys(t + 1, free + j, a, z)
+                a, z = ((0, MID - 16), (MID - 16, E))[k]
+                turn[0] = "H%d" % k
+                hold(V("held", a, z), V("kr%d" % (t + 1), 4 * a + 3, 4 * z, 4), "cap")
+                aside[0] = True
+                for b in range(4):
+                    act(V("vp", E * b + lo, E * b + hi), V("x32", 4 * lo + b, 4 * hi, 4), COPY, scale=2.0 ** -6)
+                aside[0] = False
+        for i, k in enumerate(sorted(range(first, len(calls)), key=lambda k: (turns.index(calls[k]["turn"]), k))):
+            calls[k]["place"] = first + i
 
     s = "sx%d" % NR
     for k in range(4):
-        dma("s", "ds%d" % k, T.osc[4 * k:4 * k + 4, 0:C], (T[s][32 * k:32 * k + 4, 0:C], V(s, 0, C)[1]))
-    for sem in count:
-        g.wait_ge(T.sem[sem], count[sem])
-    for sem in DMAS:
-        g.wait_ge(T.sem[sem], 16)
-    g.wait_ge(T.sem.left, 2 * NR * len(send_engines(core, prev)))
+        dma("s", "ds%d" % k, T.osc[4 * k:4 * k + 4, 0:C], dict(V(s, 0, C), ap=T[s][32 * k:32 * k + 4, 0:C], n=0))
+    issue_all()

@@ -1,23 +1,27 @@
 from concourse.mybir import dt, AluOpType, ActivationFunctionType
 
 C, H, E, NR = 384, 64, 448, 3
-NV = (0, 11, 10)
-NE = (0, 24, 24)
+NV = (0, 10, 10)
+NE = (0, 22, 22)
 X2 = E + 16
 SPLIT = 14
-HOME = (2, 3)
+HOME = ((2, 3), (2, 3))
 CAP = 2.0 ** 25
 WHOLE = 12582912.0
 CUTS = ((0, 128, 256, C), (0, 256, C))
 MID = CUTS[0][-2]
 HW = max(MID, E - MID + 4)
-TURNS = ("M0 G0 M1 M2 M3 G1 G2 E3 F3 P0 U0 P1 U1 X1 X0 Q0 P2 U2 Q1 B1 X2 B0 K0 Q2 B2 H0 K1 H1",
-         "M0 G0 M1 M2 M3 G1 L0 G2 E3 P0 F3 L1 U0 X0 P1 L2 Q0 U1 X1 Q1 B0 B1")
-XS = ("444", "av")
-AHEAD = 40
+TURNS = ("M0 M1 G0 M2 S2 M3 S3 G1 G2 E3 P0 F3 P1 R0 P2 U0 X0 U1 X1 Q0 B0 U2 Q1 B1 X2 Q2 K0 B2 H0 K1 D0 C0 C1 C2 H1",
+         "M0 M1 G0 M2 S2 M3 S3 G1 G2 E3 P0 F3 L0 P1 L1 U0 X0 U1 Q0 X1 L2 Q1 B0 B1")
+XS = ("44v", "4v")
+AHEAD = 300
+W0 = 384
+KN = MID - 16
+SOON = (None, (0, 2), (0, 2))
+COLUMN = 1.1
 PASSES = 1
 EARLY = 300
-CYCLE, CALL, WAKE, TOL, GATHER, SCATTER, LOCAL, REMOTE, FIRST = 0.83, 45, 120, 60, 1.56, 3.5, 1500, 1700, 1500
+CYCLE, CALL, WAKE, TOL, GATHER, SCATTER, LOCAL, REMOTE, FIRST = 0.83, 45, 120, 60, 1.56, 3.5, 700, 900, 700
 
 SCRATCH = {}
 for _k, _n in (("qu", 128), ("qur", 256), ("qv", 128), ("qw", 512), ("qe", 512), ("qz", C), ("qg", 128), ("qh", E)):
@@ -25,12 +29,12 @@ for _k, _n in (("qu", 128), ("qur", 256), ("qv", 128), ("qw", 512), ("qe", 512),
     SCRATCH["s" + _k[1:]] = ("sbuf", [128, _n], "uint8")
 for _k, _n in (("ut", 512), ("vt", 512), ("et", 2048), ("gt", 512), ("hl", 4 * E), ("zt", 4 * C), ("vp", 4 * E), ("x32", 4 * C),
                ("vs", 4 * X2), ("mm", 4 * X2), ("mb", 4 * C), ("hb", 128), ("ident", 128), ("grp", 128), ("ones", 512), ("t1", E), ("t2", E),
-               ("t3", E), ("t4", E), ("w", E + 16), ("w6", E), ("er", E + 16), ("junk", 4 * E), ("cb", 16 * E), ("sc", 8 * E), ("lane", E),
-               ("cap", E), ("cap2", X2), ("tri", E), ("hit", E), ("c0", 32), ("hw1", 4 * HW), ("hw2", 4 * HW), ("eq", E), ("eqs", E)):
+               ("t3", E), ("t4", E), ("w", E + 16), ("w6", E), ("er", E + 64), ("junk", 4 * E), ("cb", 16 * E), ("sc", 8 * E), ("lane", E),
+               ("cap", E), ("cap2", X2), ("tri", E), ("hit", E), ("c0", 32), ("hw1", 3 * HW), ("hw2", 3 * HW), ("eq", E), ("eqs", E)):
     SCRATCH[_k] = ("sbuf", [128, _n], "bfloat16")
 for _k, _n in (("iof", E), ("iq", E), ("pl", 1), ("pl1", 1), ("pin", 1), ("pq", 3), ("pg", 3), ("lama", 1), ("lam", 1), ("lamb", 1), ("lams", 1), ("acc0", 2),
-               ("hin1", 4 * E), ("hin2", 4 * E), ("kr1", 4 * E), ("kr2", 8 * E), ("held", E), ("own", 28), ("nown", 28), ("acc", 28), ("eq2", 28),
-               ("posf", 28), ("ordr", X2), ("held2", X2), ("yl", E), ("ks", X2), ("dk", E), ("lw", X2), ("lvr", E), ("yr", C)):
+               ("soon1", 28), ("soon2", 28), ("hin1", 3 * E), ("hin2", 3 * E), ("kr1", 3 * E), ("kr2", 6 * E), ("held", E), ("own", 28), ("nown", 28), ("acc", 28), ("eq2", 28),
+               ("posf", 28), ("ordr", X2), ("held2", X2), ("yl", E), ("l4", E), ("g1", E), ("g2", E), ("ks", X2), ("dk", E), ("lw", X2), ("lvr", E), ("yr", C)):
     SCRATCH[_k] = ("sbuf", [128, _n], "float32")
 for _k, _n in (("uo", 16), ("bo", 28)):
     SCRATCH[_k] = ("sbuf", [128, _n], "int32")
@@ -41,7 +45,7 @@ for _t in range(NR + 1):
     SCRATCH["xt%d" % _t] = ("sbuf", [128, 4 * C], "bfloat16")
     SCRATCH["qx%d" % _t] = ("sbuf", [128, E], "float8_e4m3fn_x4")
     SCRATCH["sx%d" % _t] = ("sbuf", [128, E], "uint8")
-DMAS = ["dxa", "dxb", "du", "dv", "dwc", "dws", "dlv", "dya", "dyb", "dca", "dcb"] + ["ds%d" % k for k in range(4)]
+DMAS = ["dxa", "dxb", "du", "dv", "dwc", "dws", "dlv", "dya", "dyb", "dca", "dcb", "aa", "ab", "ac"] + ["ds%d" % k for k in range(4)]
 SEMAPHORES = ["vec", "act", "ten", "pool", "left"] + ["arr%d" % t for t in range(NR)] + DMAS
 
 ADD, SUB, MUL, MAX, MIN = AluOpType.add, AluOpType.subtract, AluOpType.mult, AluOpType.max, AluOpType.min
@@ -109,6 +113,9 @@ def rank_program(g, core, T, topo):
         side = out if writes else in_
         note(q, 60, LOCAL + side["n"], lambda: eng.dma_start(out["ap"] if writes else out, in_["ap"] if reads else in_), reads + list(after), writes, (sem, 16))
 
+    def add(sem, out, in_):
+        note("g", 300, LOCAL + 6 * out["n"], lambda: g.dma_start(out["ap"], in_["ap"], accum_op=ADD), in_["at"] + out["at"], out["at"], (sem, 16))
+
     def span(out, *ins, both=1.0):
         if "list" in out or "list" in ins[0]:
             return CALL + CYCLE * out["n"] * (SCATTER if "list" in out else GATHER)
@@ -141,9 +148,11 @@ def rank_program(g, core, T, topo):
     def quant(codes, src, lo, hi):
         op("v", 2, CALL + 12 + 0.88 * (hi - lo), g.vector.quantize_mx, V(codes, lo, hi), V("s" + codes[1:], lo, hi), V(src, 4 * lo, 4 * hi))
 
-    def mx(k, l, llo, r, rlo, rhi):
-        op("t", 1, CYCLE * (rhi - rlo + 16), g.tensor.matmul_mx, bank(k, 0, rhi - rlo), V(l, llo, llo + 128), V("s" + l[1:], llo, llo + 128),
-           V(r, rlo, rhi), V("s" + r[1:], rlo, rhi), True, True)
+    def mx(k, l, llo, r, rlo, rhi, start=True, stop=True):
+        op("t", 1, COLUMN * (rhi - rlo + 16), g.tensor.matmul_mx, bank(k, 0, rhi - rlo), V(l, llo, llo + 128), V("s" + l[1:], llo, llo + 128),
+           V(r, rlo, rhi), V("s" + r[1:], rlo, rhi), start, stop)
+        if not start:
+            calls[-1]["behind"][len(calls) - 2] = False
 
     def send(t):
         q, s = "qx%d" % t, "sx%d" % t
@@ -285,7 +294,7 @@ def rank_program(g, core, T, topo):
         act(V("gt", b, 512, 4), V("gt", 0, 512, 4), COPY, scale=c)
     quant("qg", "gt", 0, 128)
     for b in range(4):
-        const(V("et", 512 * b, 512 * b + 512), 0.0)
+        fill(V("et", 512 * b, 512 * b + 512), 0.0)
         act(V("et", 512 * b + b, 512 * b + 512, 4), V("ident", 0, 128), COPY, scale=0.5)
         quant("qe", "et", 128 * b, 128 * b + 128)
     act(V("lama", 0, 1), V("pq", 0, 1), IDEN, bias=1.0)
@@ -293,20 +302,19 @@ def rank_program(g, core, T, topo):
     act(V("lamb", 0, 1), V("lam", 0, 1), IDEN, bias=-1.0)
     act(V("lams", 0, 1), V("lam", 0, 1), IDEN, bias=-0.5)
     const(V("w", E, E + 16), -2.0)
-    const(V("er", E, E + 16), -1.5)
+    const(V("er", E, E + 64), -1.5)
     const(V("hl", 3, 4 * E, 4), 0.0)
     const(V("ordr", 0, X2, X2 - 1), 0.0)
     const(V("ordr", E + 1, X2 - 1), 0.0)
-    for lo, hi, c in ((0, MID, 18.5), (MID, E, 0.0)):
-        act(V("iq", lo, hi), V("iof", lo, hi), IDEN, scale=1.0 / 512, bias=c + 2.5 - 225.0 / 512)
-    for t, far in ((1, 18.5), (2, 1336.0)):
-        for b, c in enumerate((0.0, 2.0, far, 2.0)):
-            const(V("hw%d" % t, b, 4 * HW, 4), c)
-    const(V("hin1", 4 * (E - 2) + 3, 4 * E, 4), 0.0)
-    const(V("hin1", 4 * (E - 3) + 3, 4 * (E - 2)), -1.0)
-    const(V("hin1", 4 * (E - 1) + 1, 4 * (E - 1) + 2), 0.0)
-    for b in (2, 3):
-        const(V("hin2", 4 * (E - 4) + b, 4 * E, 4), 0.0)
+    act(V("iq", 0, E), V("iof", 0, E), IDEN, scale=1.0 / 512, bias=22.5 - 225.0 / 512)
+    for t, far in ((1, 40.0), (2, 2816.0)):
+        const(V("soon%d" % t, 0, 28), 0.0)
+        for b, c in enumerate((0.0, far, 0.5)):
+            (fill if t == 1 else const)(V("hw%d" % t, b, 3 * HW, 3), c)
+    const(V("hin1", 3 * (E - 3) + 1, 3 * (E - 3) + 2), -1.0)
+    const(V("hin1", 3 * (E - 1), 3 * (E - 1) + 1), 0.0)
+    const(V("hin1", 3 * (E - 2) + 1, 3 * E, 3), 0.0)
+    const(V("hin2", 3 * (E - 4) + 1, 3 * E, 3), 0.0)
     quant("qu", "ut", 0, 128)
     tc(cast(V("qur", 0, 256), dt.uint32), by(cast(V("qu", 0, 128), dt.uint32), V("uo16", 0, 16)))
     act(V("sur", 0, 256), by(V("su", 0, 128), V("uo16", 0, 16)), COPY)
@@ -324,20 +332,23 @@ def rank_program(g, core, T, topo):
         ts(V("w6", klo, khi), V("w", klo, khi), 4.5, 6.5, MUL, ADD)
         tt(V("er", klo, khi), V("w6", klo, khi), V("w", klo + 1, khi + 1), ADD)
 
+    def key(t, lo, hi):
+        return V("kr%d" % t, 3 * lo + 2, 3 * hi, 3)
+
     def keys(t, k, lo, hi):
-        d, hin = 2 ** t, "hin%d" % t
-        klo, khi = max(lo - d, 0), hi if hi == E else hi - d
+        d = 2 ** t
         top = hi - 1 if (t, hi) == (1, E) else hi
-        act(V(hin, 4 * klo + 3, 4 * (top - d), 4), bank(k, klo + d - lo, top - lo), SIGN, bias=-1.0e-36)
+        hin, klo = "hin%d" % t, max(lo - d, 0)
+        act(V(hin, 3 * klo + 1, 3 * (top - d), 3), bank(k, klo + d - lo, top - lo), SIGN, bias=-1.0e-36)
         if hi < E:
-            act(V(hin, 4 * lo + 1, 4 * top, 4), bank(k, 0, top - lo), SIGN, bias=-1.0e-36)
+            act(V(hin, 3 * lo, 3 * top, 3), bank(k, 0, top - lo), SIGN, bias=-1.0e-36)
         else:
-            ts(V(hin, 4 * lo + 1, 4 * top, 4), bank(k + 1, 0, top - lo), 0.0, 2.0, GT, MUL)
+            ts(V(hin, 3 * lo, 3 * top, 3), bank(k + 1, 0, top - lo), 0.0, 2.0, GT, MUL)
         if hi < MID:
             return
-        klo = klo if hi == E else 0
+        klo, khi = (MID - d, E) if hi == E else (0, MID - d)
         turn[0] = "K%d" % (hi == E)
-        scan(V("kr%d" % t, 4 * klo, 4 * khi), V("hw%d" % t, 0, 4 * (khi - klo)), V(hin, 4 * klo, 4 * khi), 0.0, MUL, ADD)
+        scan(V("kr%d" % t, 3 * klo, 3 * khi), V("hw%d" % t, 0, 3 * (khi - klo)), V(hin, 3 * klo, 3 * khi), 0.0, MUL, ADD)
 
     def unpack(t, k):
         aside[0] = True
@@ -345,6 +356,28 @@ def rank_program(g, core, T, topo):
             mx(k + b, "qe", 128 * b, "qx%d" % t, E - 128, E)
             act(V("vp", E * b + C, E * b + E), bank(k + b, 64, 128), COPY)
         aside[0] = False
+
+    def before(lo, hi):
+        act(key(2, E + lo, E + hi), key(2, lo, hi), IDEN, bias=-1.0)
+        act(V("nown", lo // 16, hi // 16), ends("held", lo // 16, hi // 16), IDEN, bias=0.5)
+
+    def compare(t, c, soon):
+        w = 16 * c + 16 if t == 2 else 0
+        lo, hi = (w, KN) if soon else (KN if c < SOON[t][0] else w, w + E)
+        out, row = V("cb", E * c + lo - w, E * c + hi - w), key(t, lo, hi)
+        if t == 2:
+            ts(out, row, V("own", c, c + 1), -0.5, GE, ADD)
+        else:
+            ts(out, row, ends("held", c, c + 1), 0.0, ADD, LT)
+
+    def signs(t, c, soon):
+        split = c < NV[t] + SOON[t][1]
+        if t == 2:
+            lo, hi = (E, 16 * c + 16 + E) if soon else (16 * c + 16, E if split else 16 * c + 16 + E)
+        else:
+            lo, hi = (0, KN) if soon else (KN if split else 0, E)
+        act(V("junk", E * (c % 4), E * (c % 4) + hi - lo), key(t, lo, hi), SIGN, bias=V("nown", c, c + 1) if t == 2 else ends("held", c, c + 1),
+            accum_out=V("soon%d" % t if soon else "acc", c, c + 1))
 
     def scatter(lo, hi):
         tc(by(V("ordr", 0, X2), V("pos", lo, hi)), V("iof", 16 * lo, 16 * hi))
@@ -355,20 +388,20 @@ def rank_program(g, core, T, topo):
         nv, ne = NV[t], NE[t]
         if t == 0:
             O = lambda lo, hi: V("hl", 4 * lo + 2, 4 * hi, 4)
-            mx(0, "qur", 128, qx, 0, C)
-            mx(1, "qur", 0, qx, 0, C)
-            mx(2, "qur", 128, qx, E - 128, E)
-            mx(3, "qur", 0, qx, E - 128, E)
+            for k, lo, hi in ((0, 0, 128), (2, 128, C), (0, C, E)):
+                mx(k, "qur", 128, qx, min(lo, E - 128), hi)
+                mx(k + 1, "qur", 0, qx, min(lo, E - 128), hi)
+                words0(k, max(lo - E + 128, 0), lo, hi, max(lo - 1, 0), hi - (hi < E))
             unpack(t, 4)
-            words0(0, 0, 0, C, 0, C - 1)
-            words0(2, 64, C, E, C - 1, E)
-            for k, (lo, hi) in enumerate(((0, C - 1), (C - 1, E))):
+            for k, (lo, hi) in enumerate(((0, C - 1), (C - 1, E + 62))):
                 act(V("junk", lo, hi), V("er", lo, hi), SIGN, bias=V("lams", 0, 1), scale=-1.0, accum_out=V("acc0", k, k + 1))
                 ts(O(lo, min(hi, E - 1)), V("er", lo, min(hi, E - 1)), V("lam", 0, 1), None, EQ)
-            act(V("acc0", 0, 1), V("acc0", 0, 1), IDEN, scale=0.5, bias=31.0)
             ts(O(E - 1, E), V("er", E - 1, E), V("lamb", 0, 1), None, EQ)
-            ts(V("t3", E - 1, E), V("acc0", 1, 2), 0.5, V("acc0", 0, 1), MUL, ADD)
+            ts(V("t3", E - 1, E), V("acc0", 1, 2), V("acc0", 0, 1), 0.5, ADD, MUL)
             scan(V("t3", 0, E - 1), V("ones", 0, E - 1), O(0, E - 1), V("t3", E - 1, E), MUL, ADD)
+            act(V("g1", 0, E), V("er", 0, E), COPY, scale=39.0)
+            add("aa", V("iq", 0, E), V("er", 2, E + 2))
+            add("ab", V("g1", 0, E), V("iq", 0, E))
             halves = ((0, 224), (224, E))
             for lo, hi in halves:
                 tt(V("t4", lo, hi), V("t3", lo, hi), O(lo, hi), MUL)
@@ -383,46 +416,34 @@ def rank_program(g, core, T, topo):
                 hold(V("held", lo, hi), bank(k, 0, hi - lo), "cap")
             ts(V("pos", 0, 28), ends("held"), -1.0, -63.0, MUL, ADD)
             scatter(0, 28)
-            aside[0] = True
-            act(V("hin1", 0, 4 * E, 4), V("er", 0, E), COPY)
-            for lo in range(0, E, 112):
-                tt(V("hin1", 4 * lo + 2, 4 * lo + 448, 4), V("er", lo + 2, lo + 114), V("iq", lo, lo + 112), ADD)
-            aside[0] = False
         else:
-            kr = "kr%d" % t
-            K = V(kr, 3, 4 * E, 4)
-            unpack(t, 4 - free)
-            row = lambda c: V(kr, 4 * (16 * c + 16) + 3, 4 * (16 * c + 16 + E), 4) if last else K
+            K = key(t, 0, E)
             if last:
-                act(V(kr, 4 * E + 3, 8 * E, 4), K, IDEN, bias=-2.0)
-                act(V("nown", 0, 28), ends("held"), IDEN, bias=1.0)
-                ts(V("own", 0, 28), ends("held"), -1.0, None, MUL)
-                tt(V("eq", 0, E), by(V("own", 0, 28), V("bo16", 0, 28)), K, EQ)
-                scan(V("eqs", 0, E), V("eq", 0, E), V("tri", 0, E), 0.0, ADD, MUL)
-                ts(V("eq2", 0, 28), ends("eqs"), 2.0, None, MUL)
-            else:
-                aside[0] = True
-                act(V("yl", 0, E), K, IDEN, scale=0.5, bias=WHOLE)
-                act(V("hin2", 0, 4 * E, 4), V("yl", 0, E), IDEN, scale=2.0, bias=-2 * WHOLE)
-                act(V("hin2", 2, 4 * MID, 4), V("yl", 4, MID + 4), IDEN, scale=2.0, bias=1336.0 - 2 * WHOLE)
-                act(V("hin2", 4 * MID + 2, 4 * (E - 4), 4), V("yl", MID + 4, E), IDEN, scale=2.0, bias=-2 * WHOLE)
-                aside[0] = False
+                ties = [lambda: ts(V("own", 15, 28), ends("held", 15, 28), -1.0, None, MUL),
+                        lambda: tt(V("eq", 0, E), by(V("own", 0, 28), V("bo16", 0, 28)), K, EQ),
+                        lambda: scan(V("eqs", 0, E), V("eq", 0, E), V("tri", 0, E), 0.0, ADD, MUL),
+                        lambda: ts(V("eq2", 0, 28), ends("eqs"), 2.0, None, MUL),
+                        lambda: tt(V("eq2", 0, 28), V("eq2", 0, 28), V("soon2", 0, 28), ADD)]
             for c in range(nv, 28):
-                act(V("junk", E * (c % 4), E * (c % 4) + E), row(c), SIGN, bias=V("nown", c, c + 1) if last else ends("held", c, c + 1),
-                    accum_out=V("acc", c, c + 1))
+                if last and c == KN // 16 - 1:
+                    before(KN, E)
+                signs(t, c, False)
+            unpack(t, 4 - free)
+            if not last:
+                act(V("yl", 0, E), K, IDEN, bias=WHOLE)
+                act(V("l4", 0, E), V("yl", 0, E), IDEN, scale=2.0, bias=-2 * WHOLE)
             for c in range(nv):
-                if last:
-                    ts(V("cb", E * c, E * c + E), row(c), V("own", c, c + 1), -0.5, GE, ADD)
-                else:
-                    ts(V("cb", E * c, E * c + E), row(c), ends("held", c, c + 1), 0.0, ADD, LT)
+                compare(t, c, False)
+                if last and c < len(ties):
+                    ties[c]()
             for c in range(nv):
                 scan(V("sc", 224 * c, 224 * c + 224), V("cb", E * c, E * c + 224), V("cb", E * c + 224, E * c + E),
                      ends("eqs", c, c + 1) if last else -192.0, ADD, ADD)
             ts(V("pos", 0, nv), V("sc", 223, 224 * nv, 224), *((-1.0, 224.0) if last else (1.0, 193.0)), MUL, ADD)
             for lo, hi in ((nv, ne), (ne, 28)):
-                if last:
-                    tt(V("posf", lo, hi), V("acc", lo, hi), V("eq2", lo, hi), ADD)
-                ts(V("pos", lo, hi), V("posf" if last else "acc", lo, hi), -0.5, 224.0 if last else 224.5, MUL, ADD)
+                if last or lo == nv:
+                    tt(V("posf", lo, hi), V("acc", lo, hi), V("eq2" if last else "soon1", lo, hi), ADD)
+                ts(V("pos", lo, hi), V("posf" if last or lo == nv else "acc", lo, hi), -0.5, 224.0 if last else 224.5, MUL, ADD)
                 scatter(0 if lo == nv else lo, hi)
         for lo, hi in ((0, SPLIT), (SPLIT, 29)):
             scan(V("held2", 16 * lo, 16 * hi), V("ordr", 16 * lo, 16 * hi), V("cap2", 16 * lo, 16 * hi), 0.0, MAX, MUL)
@@ -436,22 +457,30 @@ def rank_program(g, core, T, topo):
         tc(*into(0, SPLIT, 29))
         for b in range(4):
             act(*into(b, 0, SPLIT if b == 0 else 29), COPY)
+        if t == 1:
+            act(V("g2", 0, E), V("l4", 0, E), COPY, scale=2816.0)
+            add("ac", V("g2", 0, E - 4), V("l4", 4, E))
         turns = TURNS[last].split()
         first = len(calls)
         for b in range(4):
             o = X2 * b
             turn[0] = "M%d" % b
             tt(V("mm", o + 1, o + 1 + E), V("vs", o, o + E), V("vs", o + 2, o + 2 + E), MAX)
-            if b in HOME:
+            if b in HOME[last]:
+                turn[0] = "S%d" % b
                 act(V("mb", C * b, C * b + C), back(b, 0, C), COPY)
             for name, lo, hi in (("G", 0, C), ("E", 0, cuts[1]), ("F", cuts[1], C)):
                 turn[0] = name + str(b)
                 if turn[0] in turns:
-                    tt(V("zt", 4 * lo + b, 4 * hi, 4), V("mb", C * b + lo, C * b + hi) if b in HOME else back(b, lo, hi), V("vp", E * b + lo, E * b + hi), ADD)
-        if last:
+                    tt(V("zt", 4 * lo + b, 4 * hi, 4), V("mb", C * b + lo, C * b + hi) if b in HOME[last] else back(b, lo, hi), V("vp", E * b + lo, E * b + hi), ADD)
+        if not last:
+            turn[0] = "R0"
+            for lo, hi, c in ((0, MID, 0.0), (MID, E, (-20.0, -1408.0)[t])):
+                act(V("hin%d" % (t + 1), 3 * lo + 2, 3 * hi, 3), V("g%d" % (t + 1), lo, hi), IDEN, bias=c)
+        else:
             turn[0] = "L0"
-            ts(V("ord4", 0, 29), V("ordl", 0, 29), 4.0, 3.0, MUL, ADD)
-            act(V("ks", 0, X2), by(V(kr, 0, 4 * E), V("ord4", 0, 29)), COPY, scale=256.0)
+            ts(V("ord4", 0, 29), V("ordl", 0, 29), 3.0, 2.0, MUL, ADD)
+            act(V("ks", 0, X2), by(V("kr2", 0, 3 * E), V("ord4", 0, 29)), COPY, scale=512.0)
             turn[0] = "L1"
             for lo in (0, 224):
                 tt(V("dk", lo, lo + 224), V("ks", lo + 1, lo + 225), V("ks", lo, lo + 224), SUB)
@@ -485,7 +514,10 @@ def rank_program(g, core, T, topo):
             if last:
                 dma("s", "dc" + "ab"[k], T.oc[:, 4 * lo:4 * hi], cast(V(qn, lo, hi), dt.uint8))
                 mx(free + k, "qv", 0, qn, lo, hi)
-                act(V("yr", lo, hi), bank(free + k, 0, hi - lo), COPY)
+                if k:
+                    tc(V("yr", lo, hi), bank(free + k, 0, hi - lo))
+                else:
+                    act(V("yr", lo, hi), bank(free + k, 0, hi - lo), COPY)
                 dma("a", "dy" + "ab"[k], T.y[:, lo:hi], V("yr", lo, hi))
             else:
                 for j, (a, z) in pieces[:-1] if k == 0 else ((2, (lo, E)),):
@@ -495,7 +527,18 @@ def rank_program(g, core, T, topo):
                     keys(t + 1, free + j, a, z)
                 a, z = ((0, MID - 16), (MID - 16, E))[k]
                 turn[0] = "H%d" % k
-                hold(V("held", a, z), V("kr%d" % (t + 1), 4 * a + 3, 4 * z, 4), "cap")
+                hold(V("held", a, z), key(t + 1, a, z), "cap")
+                if k == 0:
+                    if t == 1:
+                        turn[0] = "D0"
+                        ts(V("own", 0, 15), ends("held", 0, 15), -1.0, None, MUL)
+                        before(0, KN)
+                    for c in range(SOON[t + 1][0]):
+                        turn[0] = "C%d" % min(c, 2)
+                        compare(t + 1, c, True)
+                    for c in range(SOON[t + 1][1]):
+                        turn[0] = "D0"
+                        signs(t + 1, NV[t + 1] + c, True)
                 aside[0] = True
                 for b in range(4):
                     act(V("vp", E * b + lo, E * b + hi), V("x32", 4 * lo + b, 4 * hi, 4), COPY, scale=2.0 ** -6)

from concourse.mybir import dt, AluOpType, ActivationFunctionType

C, H, E, NR = 384, 64, 448, 3
NV = (0, 10, 10)
NE = (0, 22, 22)
X2 = E + 16
SPLIT = 14
HOME = ((2, 3), (2, 3))
CAP = 2.0 ** 25
WHOLE = 12582912.0
CUTS = ((0, 128, 256, C), (0, 256, C))
MID = CUTS[0][-2]
HW = max(MID, E - MID + 4)
TURNS = ("M0 M1 G0 M2 S2 M3 S3 G1 G2 E3 P0 F3 P1 R0 P2 U0 X0 U1 X1 Q0 B0 U2 Q1 B1 X2 Q2 K0 B2 H0 K1 D0 C0 C1 C2 H1",
         "M0 M1 G0 M2 S2 M3 S3 G1 G2 E3 P0 F3 L0 P1 L1 U0 X0 U1 Q0 X1 L2 Q1 B0 B1")
XS = ("44v", "4v")
AHEAD = 300
W0 = 384
KN = MID - 16
SOON = (None, (0, 2), (0, 2))
COLUMN = 1.1
PASSES = 1
EARLY = 300
CYCLE, CALL, WAKE, TOL, GATHER, SCATTER, LOCAL, REMOTE, FIRST = 0.83, 45, 120, 60, 1.56, 3.5, 700, 900, 700

SCRATCH = {}
for _k, _n in (("qu", 128), ("qur", 256), ("qv", 128), ("qw", 512), ("qe", 512), ("qz", C), ("qg", 128), ("qh", E)):
    SCRATCH[_k] = ("sbuf", [128, _n], "float8_e4m3fn_x4")
    SCRATCH["s" + _k[1:]] = ("sbuf", [128, _n], "uint8")
for _k, _n in (("ut", 512), ("vt", 512), ("et", 2048), ("gt", 512), ("hl", 4 * E), ("zt", 4 * C), ("vp", 4 * E), ("x32", 4 * C),
               ("vs", 4 * X2), ("mm", 4 * X2), ("mb", 4 * C), ("hb", 128), ("ident", 128), ("grp", 128), ("ones", 512), ("t1", E), ("t2", E),
               ("t3", E), ("t4", E), ("w", E + 16), ("w6", E), ("er", E + 64), ("junk", 4 * E), ("cb", 16 * E), ("sc", 8 * E), ("lane", E),
               ("cap", E), ("cap2", X2), ("tri", E), ("hit", E), ("c0", 32), ("hw1", 3 * HW), ("hw2", 3 * HW), ("eq", E), ("eqs", E)):
    SCRATCH[_k] = ("sbuf", [128, _n], "bfloat16")
for _k, _n in (("iof", E), ("iq", E), ("pl", 1), ("pl1", 1), ("pin", 1), ("pq", 3), ("pg", 3), ("lama", 1), ("lam", 1), ("lamb", 1), ("lams", 1), ("acc0", 2),
               ("soon1", 28), ("soon2", 28), ("hin1", 3 * E), ("hin2", 3 * E), ("kr1", 3 * E), ("kr2", 6 * E), ("held", E), ("own", 28), ("nown", 28), ("acc", 28), ("eq2", 28),
               ("posf", 28), ("ordr", X2), ("held2", X2), ("yl", E), ("l4", E), ("g1", E), ("g2", E), ("ks", X2), ("dk", E), ("lw", X2), ("lvr", E), ("yr", C)):
    SCRATCH[_k] = ("sbuf", [128, _n], "float32")
for _k, _n in (("uo", 16), ("bo", 28)):
    SCRATCH[_k] = ("sbuf", [128, _n], "int32")
for _k, _n in (("uo16", 16), ("bo16", 28), ("pos", 28), ("ordl", 30), ("ord4", 30)):
    SCRATCH[_k] = ("sbuf", [128, _n], "uint16")
SCRATCH["ps"] = ("psum", [128, 4096], "float32")
for _t in range(NR + 1):
    SCRATCH["xt%d" % _t] = ("sbuf", [128, 4 * C], "bfloat16")
    SCRATCH["qx%d" % _t] = ("sbuf", [128, E], "float8_e4m3fn_x4")
    SCRATCH["sx%d" % _t] = ("sbuf", [128, E], "uint8")
DMAS = ["dxa", "dxb", "du", "dv", "dwc", "dws", "dlv", "dya", "dyb", "dca", "dcb", "aa", "ab", "ac"] + ["ds%d" % k for k in range(4)]
SEMAPHORES = ["vec", "act", "ten", "pool", "left"] + ["arr%d" % t for t in range(NR)] + DMAS

ADD, SUB, MUL, MAX, MIN = AluOpType.add, AluOpType.subtract, AluOpType.mult, AluOpType.max, AluOpType.min
GT, LT, GE, EQ = AluOpType.is_gt, AluOpType.is_lt, AluOpType.is_ge, AluOpType.is_equal
SHR, AND = AluOpType.logical_shift_right, AluOpType.bitwise_and
COPY, IDEN, SIGN = ActivationFunctionType.Copy, ActivationFunctionType.Identity, ActivationFunctionType.Sign


def rank_program(g, core, T, topo):
    rank = T.rank_of(core)
    if rank is None:
        return
    n = len(T.cores)
    prev, nxt = T.cores[(rank - 1) % n], T.cores[(rank + 1) % n]

    def send_engines(src, dst):
        return topo.engines(src, dst)[:8]

    calls = []
    hist = {}
    turn = [None]
    aside = [False]

    def V(name, lo, hi, step=1):
        k = (hi - lo + step - 1) // step
        mask = ((1 << (k * step)) - 1) // ((1 << step) - 1) << lo
        return {"ap": T[name][:, lo:hi] if step == 1 else T[name][:, lo:hi:step], "at": [(name, mask)], "n": k,
                "half": SCRATCH[name][2] in ("bfloat16", "uint16")}

    def bank(k, lo, hi):
        return {"ap": T.ps[:, 512 * k + lo:512 * k + hi], "at": [("ps", 1 << k)], "n": hi - lo, "half": False, "psum": True}

    def by(win, off):
        return {"ap": win["ap"].indirect(off["ap"]), "at": win["at"], "n": 16 * off["n"], "half": False, "list": off["at"]}

    def cast(v, d):
        return dict(v, ap=v["ap"].bitcast(d))

    def note(q, busy, done, issue, reads, writes, sem=None):
        me, behind = len(calls), {}
        for regs, isw in ((reads, False), (writes, True)):
            for name, mask in regs:
                for m, w, k in hist.get(name, ()):
                    other = calls[k]["q"] != q or calls[k]["sem"] is not None
                    if m & mask and (w or isw or (other and name == "ps")):
                        behind[k] = True
        for name, mask in writes:
            hist[name] = [e for e in hist.get(name, ()) if e[0] & ~mask] + [(mask, True, me)]
        for name, mask in reads:
            hist.setdefault(name, []).append((mask, False, me))
        calls.append({"q": q, "busy": busy, "done": done, "issue": issue, "behind": behind, "place": me, "turn": turn[0], "aside": aside[0], "sem": sem})

    def op(q, nout, time, fn, *args, **kw):
        reads, writes = [], []
        for k, a in list(enumerate(args)) + list(kw.items()):
            if isinstance(a, dict):
                (writes if k == "accum_out" or k in range(nout) else reads).extend(a["at"])
                reads.extend(a.get("list", []))
        plain = lambda a: a["ap"] if isinstance(a, dict) else a
        note(q, time, time, lambda: fn(*[plain(a) for a in args], **{k: plain(a) for k, a in kw.items()}), reads, writes)

    def dma(q, sem, out, in_, after=()):
        reads, writes = (in_["at"] if isinstance(in_, dict) else []), (out["at"] if isinstance(out, dict) else [])
        eng = {"s": g.sync, "a": g.scalar}[q]
        side = out if writes else in_
        note(q, 60, LOCAL + side["n"], lambda: eng.dma_start(out["ap"] if writes else out, in_["ap"] if reads else in_), reads + list(after), writes, (sem, 16))

    def add(sem, out, in_):
        note("g", 300, LOCAL + 6 * out["n"], lambda: g.dma_start(out["ap"], in_["ap"], accum_op=ADD), in_["at"] + out["at"], out["at"], (sem, 16))

    def span(out, *ins, both=1.0):
        if "list" in out or "list" in ins[0]:
            return CALL + CYCLE * out["n"] * (SCATTER if "list" in out else GATHER)
        return CALL + CYCLE * max(64, out["n"] * both * (0.5 if all(a["half"] for a in (out,) + ins) else 1.0))

    def tt(out, a, b, o):
        op("v", 1, span(out, a, b, both=1.0 if "psum" in a else 2.0), g.vector.tensor_tensor, out, a, b, o)

    def ts(out, a, s1, s2, *o):
        op("v", 1, span(out, a), g.vector.tensor_scalar, out, a, s1, s2, *o)

    def tc(out, in_):
        op("v", 1, span(out, in_), g.vector.tensor_copy, out, in_)

    def scan(out, d0, d1, init, o0, o1):
        op("v", 1, span(out, d0, d1), g.vector.tensor_tensor_scan, out, d0, d1, init, o0, o1)

    def act(out, in_, f, **kw):
        op("a", 1, span(dict(out, half=False), in_) + 20 * ("accum_out" in kw), g.scalar.activation, out, in_, f, **kw)

    def fill(v, c):
        op("v", 1, span(v, v), g.vector.memset, v, c)

    def const(v, c):
        act(v, V("ones", 0, v["n"]), COPY, scale=c)

    def iota(v, pattern, base, mult, **kw):
        op("g", 1, 130 + 2 * CYCLE * v["n"], g.iota, v, pattern, base, mult, **kw)

    def quant(codes, src, lo, hi):
        op("v", 2, CALL + 12 + 0.88 * (hi - lo), g.vector.quantize_mx, V(codes, lo, hi), V("s" + codes[1:], lo, hi), V(src, 4 * lo, 4 * hi))

    def mx(k, l, llo, r, rlo, rhi, start=True, stop=True):
        op("t", 1, COLUMN * (rhi - rlo + 16), g.tensor.matmul_mx, bank(k, 0, rhi - rlo), V(l, llo, llo + 128), V("s" + l[1:], llo, llo + 128),
           V(r, rlo, rhi), V("s" + r[1:], rlo, rhi), start, stop)
        if not start:
            calls[-1]["behind"][len(calls) - 2] = False

    def send(t):
        q, s = "qx%d" % t, "sx%d" % t

        def issue():
            rid, pid = topo.addr(prev)[0], topo.addr(prev)[1]
            m = 0
            for e in send_engines(core, prev):
                m |= 1 << e
            g.remote_dma(T[q][:, C:E].bitcast(dt.uint8), T[q][:, 0:H].bitcast(dt.uint8), T.sem["arr%d" % t], T.sem.left, pid, rid, m)
            g.remote_dma(T[s][:, C:E], T[s][:, 0:H], T.sem["arr%d" % t], T.sem.left, pid, rid, m)

        late = FIRST * (t == 0)
        note("g", late + 500, late + 300 + REMOTE, issue, V(q, 0, H)["at"] + V(s, 0, H)["at"], V(q, C, E)["at"] + V(s, C, E)["at"],
             ("arr%d" % t, 2 * len(send_engines(nxt, core))))

    def issue_all():
        queue = {"v": g.vector, "a": g.scalar, "t": g.tensor, "g": g, "s": g.sync}
        semof = {"v": "vec", "a": "act", "t": "ten", "g": "pool"}
        after = [[] for c in calls]
        for k, c in enumerate(calls):
            for j in c["behind"]:
                after[j].append(k)
        for k in reversed(range(len(calls))):
            calls[k]["way"] = min([calls[j]["way"] - 0.001 for j in after[k]] + [len(calls) if calls[k]["aside"] else calls[k]["place"]])
        gap = lambda j, hard: calls[j]["done"] + WAKE if hard else calls[j]["busy"]

        def place(due):
            todo = {q: sorted((k for k, c in enumerate(calls) if c["q"] == q), key=lambda k: (calls[k]["way"], k)) for q in queue}
            free = {q: 0.0 for q in queue}
            at, order = {}, []

            def soonest(k, known):
                if k not in known:
                    known[k] = max([(at[j] if j in at else soonest(j, known)) + gap(j, hard) for j, hard in calls[k]["behind"].items()] + [free[calls[k]["q"]]])
                return known[k]

            for _ in calls:
                known, offers = {}, []
                for q in queue:
                    limit = 1e18
                    for k in todo[q][:AHEAD]:
                        if all(j in at for j in calls[k]["behind"]) and soonest(k, known) + calls[k]["busy"] <= limit:
                            offers.append((known[k], calls[k]["way"], k))
                        limit = min(limit, max(soonest(k, known) + TOL, due.get(k, 0)))
                        if limit < free[q] + CALL + TOL:
                            break
                t, _, k = min(offers)
                todo[calls[k]["q"]].remove(k)
                at[k], free[calls[k]["q"]] = t, t + calls[k]["busy"]
                order.append(k)
            return at, order

        at, order = place({})
        for _ in range(PASSES):
            due = {}
            for k in reversed(range(len(calls))):
                if calls[k]["aside"]:
                    due[k] = min([due.get(j, at[j]) - gap(k, calls[j]["behind"][k]) - EARLY for j in after[k]] + [1e18])
            at, order = place(due)
        count = {s: 0 for s in semof.values()}
        seen = {q: {} for q in queue}
        for k in order:
            c = calls[k]
            q = c["q"]
            need = {}
            for j, hard in c["behind"].items():
                if hard:
                    sem, val = calls[j]["sem"]
                    need[sem] = max(need.get(sem, 0), val)
            for sem in sorted(need):
                if seen[q].get(sem, 0) < need[sem]:
                    queue[q].wait_ge(T.sem[sem], need[sem])
                    seen[q][sem] = need[sem]
            made = c["issue"]()
            if c["sem"] is None:
                count[semof[q]] += 1
                c["sem"] = (semof[q], count[semof[q]])
                made.then_inc(T.sem[semof[q]], 1)
            elif made is not None:
                made.then_inc(T.sem[c["sem"][0]], 16)
        for sem in count:
            g.wait_ge(T.sem[sem], count[sem])
        for sem in DMAS:
            g.wait_ge(T.sem[sem], 16)
        g.wait_ge(T.sem.left, 2 * NR * len(send_engines(core, prev)))

    def hold(out, row, cap):
        scan(out, row, V(cap, 0, out["n"]), 0.0, MAX, MUL)

    def ends(name, lo=0, hi=28):
        return V(name, 16 * lo + 15, 16 * hi, 16)

    FL = {"allow_small_or_imprecise_dtypes": True}
    dma("s", "dxa", V("xt0", 0, 512), T.x[:, 0:512])
    dma("a", "du", V("ut", 0, 512), T.u[:, :])
    dma("s", "dxb", V("xt0", 512, 1536), T.x[:, 512:1536])
    quant("qx0", "xt0", 0, 128)
    send(0)
    halo = V("qx0", C, E)["at"]
    dma("s", "dwc", cast(V("qw", 0, 512), dt.uint8), T.wc[:, :], halo)
    dma("s", "dws", V("sw", 0, 512), T.ws[:, :], halo)
    dma("s", "dv", V("vt", 0, 512), T.v[:, :], halo)
    aside[0] = True
    iota(V("pin", 0, 1), [[0, 1]], 0, 1, **FL)
    iota(V("lane", 0, 16), [[1, 16]], 0, 0, **FL)
    iota(V("uo", 0, 16), [[1, 2], [16, 8]], 0, 0)
    iota(V("grp", 0, 128), [[1, 8], [0, 16]], 0, 0, **FL)
    iota(V("iof", 0, E), [[1, E]], 1, 0, **FL)
    iota(V("bo", 0, 28), [[1, 28]], 0, 0)
    fill(V("ones", 0, 512), 1.0)
    op("g", 1, 170 + 2 * CYCLE * 128, g.affine_select, V("ident", 0, 128), V("ones", 0, 128), [[-1, 128]], EQ, 0.0, 0, 1)
    for nm, src, k in (("uo16", "uo", 16), ("bo16", "bo", 28)):
        tc(V(nm, 0, k), V(src, 0, k))

    def whole(out, src, by_):
        act(V(out, 1, 2), V(src, 0, 1), IDEN, scale=1.0 / by_, bias=0.5 / by_ - 0.5)
        act(V(out, 2, 3), V(out, 1, 2), IDEN, bias=WHOLE)
        act(V(out, 0, 1), V(out, 2, 3), IDEN, bias=-WHOLE)

    whole("pg", "pin", 16)
    act(V("pl", 0, 1), V("pg", 0, 1), IDEN, scale=-16.0, bias=V("pin", 0, 1))
    whole("pq", "pl", 4)
    ts(V("pl1", 0, 1), V("pl", 0, 1), 1.0, None, MAX)
    for out, tri, p in (("cap", V("tri", 0, 16), "pl"), ("cap2", V("c0", 0, 16), "pl1")):
        ts(tri, V("lane", 0, 16), V(p, 0, 1), None, GT)
        ts(V("c0", 16, 32), V("lane", 0, 16), V(p, 0, 1), CAP, EQ, MUL)
        tt(V(out, 0, 16), tri, V("c0", 16, 32), ADD)
        act(V(out, 15, 16), V(out, 15, 16), COPY, scale=-1.0 / CAP)
    for name in ("cap", "tri"):
        for k in (16, 32, 64, 128, 256):
            act(V(name, k, min(2 * k, E)), V(name, 0, min(k, E - k)), COPY)
    act(V("cap2", 16, E), V("cap", 16, E), COPY)
    const(V("cap2", E + 1, X2 - 1), 1.0)
    const(V("cap2", E, E + 1), CAP)
    const(V("cap2", X2 - 1, X2), -1.0 / CAP)
    ts(V("gt", 0, 512, 4), V("grp", 0, 128), V("pg", 0, 1), None, EQ)
    for b, c in ((1, 1.0), (2, 256.0), (3, 0.0)):
        act(V("gt", b, 512, 4), V("gt", 0, 512, 4), COPY, scale=c)
    quant("qg", "gt", 0, 128)
    for b in range(4):
        fill(V("et", 512 * b, 512 * b + 512), 0.0)
        act(V("et", 512 * b + b, 512 * b + 512, 4), V("ident", 0, 128), COPY, scale=0.5)
        quant("qe", "et", 128 * b, 128 * b + 128)
    act(V("lama", 0, 1), V("pq", 0, 1), IDEN, bias=1.0)
    act(V("lam", 0, 1), V("pl", 0, 1), IDEN, scale=2.0, bias=V("lama", 0, 1))
    act(V("lamb", 0, 1), V("lam", 0, 1), IDEN, bias=-1.0)
    act(V("lams", 0, 1), V("lam", 0, 1), IDEN, bias=-0.5)
    const(V("w", E, E + 16), -2.0)
    const(V("er", E, E + 64), -1.5)
    const(V("hl", 3, 4 * E, 4), 0.0)
    const(V("ordr", 0, X2, X2 - 1), 0.0)
    const(V("ordr", E + 1, X2 - 1), 0.0)
    act(V("iq", 0, E), V("iof", 0, E), IDEN, scale=1.0 / 512, bias=22.5 - 225.0 / 512)
    for t, far in ((1, 40.0), (2, 2816.0)):
        const(V("soon%d" % t, 0, 28), 0.0)
        for b, c in enumerate((0.0, far, 0.5)):
            (fill if t == 1 else const)(V("hw%d" % t, b, 3 * HW, 3), c)
    const(V("hin1", 3 * (E - 3) + 1, 3 * (E - 3) + 2), -1.0)
    const(V("hin1", 3 * (E - 1), 3 * (E - 1) + 1), 0.0)
    const(V("hin1", 3 * (E - 2) + 1, 3 * E, 3), 0.0)
    const(V("hin2", 3 * (E - 4) + 1, 3 * E, 3), 0.0)
    quant("qu", "ut", 0, 128)
    tc(cast(V("qur", 0, 256), dt.uint32), by(cast(V("qu", 0, 128), dt.uint32), V("uo16", 0, 16)))
    act(V("sur", 0, 256), by(V("su", 0, 128), V("uo16", 0, 16)), COPY)
    quant("qx0", "xt0", 128, C)
    quant("qv", "vt", 0, 128)
    for b in range(4):
        act(V("vp", E * b, E * b + C), V("xt0", b, 4 * C, 4), COPY, scale=0.5)
        act(V("x32", C * b, C * b + C), V("xt0", C * b, C * b + C), COPY, scale=32.0)
    aside[0] = False

    def words0(k, sl, lo, hi, klo, khi):
        act(V("t2", lo, hi), bank(k, sl, sl + hi - lo), SIGN, bias=-1.0e-36)
        ts(V("t1", lo, hi), bank(k + 1, sl, sl + hi - lo), 0.0, 4.0, GT, MUL)
        tt(V("w", lo, hi), V("t1", lo, hi), V("t2", lo, hi), ADD)
        ts(V("w6", klo, khi), V("w", klo, khi), 4.5, 6.5, MUL, ADD)
        tt(V("er", klo, khi), V("w6", klo, khi), V("w", klo + 1, khi + 1), ADD)

    def key(t, lo, hi):
        return V("kr%d" % t, 3 * lo + 2, 3 * hi, 3)

    def keys(t, k, lo, hi):
        d = 2 ** t
        top = hi - 1 if (t, hi) == (1, E) else hi
        hin, klo = "hin%d" % t, max(lo - d, 0)
        act(V(hin, 3 * klo + 1, 3 * (top - d), 3), bank(k, klo + d - lo, top - lo), SIGN, bias=-1.0e-36)
        if hi < E:
            act(V(hin, 3 * lo, 3 * top, 3), bank(k, 0, top - lo), SIGN, bias=-1.0e-36)
        else:
            ts(V(hin, 3 * lo, 3 * top, 3), bank(k + 1, 0, top - lo), 0.0, 2.0, GT, MUL)
        if hi < MID:
            return
        klo, khi = (MID - d, E) if hi == E else (0, MID - d)
        turn[0] = "K%d" % (hi == E)
        scan(V("kr%d" % t, 3 * klo, 3 * khi), V("hw%d" % t, 0, 3 * (khi - klo)), V(hin, 3 * klo, 3 * khi), 0.0, MUL, ADD)

    def unpack(t, k):
        aside[0] = True
        for b in range(4):
            mx(k + b, "qe", 128 * b, "qx%d" % t, E - 128, E)
            act(V("vp", E * b + C, E * b + E), bank(k + b, 64, 128), COPY)
        aside[0] = False

    def before(lo, hi):
        act(key(2, E + lo, E + hi), key(2, lo, hi), IDEN, bias=-1.0)
        act(V("nown", lo // 16, hi // 16), ends("held", lo // 16, hi // 16), IDEN, bias=0.5)

    def compare(t, c, soon):
        w = 16 * c + 16 if t == 2 else 0
        lo, hi = (w, KN) if soon else (KN if c < SOON[t][0] else w, w + E)
        out, row = V("cb", E * c + lo - w, E * c + hi - w), key(t, lo, hi)
        if t == 2:
            ts(out, row, V("own", c, c + 1), -0.5, GE, ADD)
        else:
            ts(out, row, ends("held", c, c + 1), 0.0, ADD, LT)

    def signs(t, c, soon):
        split = c < NV[t] + SOON[t][1]
        if t == 2:
            lo, hi = (E, 16 * c + 16 + E) if soon else (16 * c + 16, E if split else 16 * c + 16 + E)
        else:
            lo, hi = (0, KN) if soon else (KN if split else 0, E)
        act(V("junk", E * (c % 4), E * (c % 4) + hi - lo), key(t, lo, hi), SIGN, bias=V("nown", c, c + 1) if t == 2 else ends("held", c, c + 1),
            accum_out=V("soon%d" % t if soon else "acc", c, c + 1))

    def scatter(lo, hi):
        tc(by(V("ordr", 0, X2), V("pos", lo, hi)), V("iof", 16 * lo, 16 * hi))

    for t in range(NR):
        qx = "qx%d" % t
        last = t == NR - 1
        nv, ne = NV[t], NE[t]
        if t == 0:
            O = lambda lo, hi: V("hl", 4 * lo + 2, 4 * hi, 4)
            for k, lo, hi in ((0, 0, 128), (2, 128, C), (0, C, E)):
                mx(k, "qur", 128, qx, min(lo, E - 128), hi)
                mx(k + 1, "qur", 0, qx, min(lo, E - 128), hi)
                words0(k, max(lo - E + 128, 0), lo, hi, max(lo - 1, 0), hi - (hi < E))
            unpack(t, 4)
            for k, (lo, hi) in enumerate(((0, C - 1), (C - 1, E + 62))):
                act(V("junk", lo, hi), V("er", lo, hi), SIGN, bias=V("lams", 0, 1), scale=-1.0, accum_out=V("acc0", k, k + 1))
                ts(O(lo, min(hi, E - 1)), V("er", lo, min(hi, E - 1)), V("lam", 0, 1), None, EQ)
            ts(O(E - 1, E), V("er", E - 1, E), V("lamb", 0, 1), None, EQ)
            ts(V("t3", E - 1, E), V("acc0", 1, 2), V("acc0", 0, 1), 0.5, ADD, MUL)
            scan(V("t3", 0, E - 1), V("ones", 0, E - 1), O(0, E - 1), V("t3", E - 1, E), MUL, ADD)
            act(V("g1", 0, E), V("er", 0, E), COPY, scale=39.0)
            add("aa", V("iq", 0, E), V("er", 2, E + 2))
            add("ab", V("g1", 0, E), V("iq", 0, E))
            halves = ((0, 224), (224, E))
            for lo, hi in halves:
                tt(V("t4", lo, hi), V("t3", lo, hi), O(lo, hi), MUL)
            for lo, hi in halves:
                ts(V("hl", 4 * lo, 4 * hi, 4), V("t4", lo, hi), 16 * WHOLE, -16 * WHOLE, ADD, ADD)
            for lo, hi in halves:
                tt(V("hl", 4 * lo + 1, 4 * hi, 4), V("t4", lo, hi), V("hl", 4 * lo, 4 * hi, 4), SUB)
            for k, (lo, hi) in enumerate(halves):
                quant("qh", "hl", lo, hi)
                mx(k, "qg", 0, "qh", lo, hi)
            for k, (lo, hi) in enumerate(halves):
                hold(V("held", lo, hi), bank(k, 0, hi - lo), "cap")
            ts(V("pos", 0, 28), ends("held"), -1.0, -63.0, MUL, ADD)
            scatter(0, 28)
        else:
            K = key(t, 0, E)
            if last:
                ties = [lambda: ts(V("own", 15, 28), ends("held", 15, 28), -1.0, None, MUL),
                        lambda: tt(V("eq", 0, E), by(V("own", 0, 28), V("bo16", 0, 28)), K, EQ),
                        lambda: scan(V("eqs", 0, E), V("eq", 0, E), V("tri", 0, E), 0.0, ADD, MUL),
                        lambda: ts(V("eq2", 0, 28), ends("eqs"), 2.0, None, MUL),
                        lambda: tt(V("eq2", 0, 28), V("eq2", 0, 28), V("soon2", 0, 28), ADD)]
            for c in range(nv, 28):
                if last and c == KN // 16 - 1:
                    before(KN, E)
                signs(t, c, False)
            unpack(t, 4 - free)
            if not last:
                act(V("yl", 0, E), K, IDEN, bias=WHOLE)
                act(V("l4", 0, E), V("yl", 0, E), IDEN, scale=2.0, bias=-2 * WHOLE)
            for c in range(nv):
                compare(t, c, False)
                if last and c < len(ties):
                    ties[c]()
            for c in range(nv):
                scan(V("sc", 224 * c, 224 * c + 224), V("cb", E * c, E * c + 224), V("cb", E * c + 224, E * c + E),
                     ends("eqs", c, c + 1) if last else -192.0, ADD, ADD)
            ts(V("pos", 0, nv), V("sc", 223, 224 * nv, 224), *((-1.0, 224.0) if last else (1.0, 193.0)), MUL, ADD)
            for lo, hi in ((nv, ne), (ne, 28)):
                if last or lo == nv:
                    tt(V("posf", lo, hi), V("acc", lo, hi), V("eq2" if last else "soon1", lo, hi), ADD)
                ts(V("pos", lo, hi), V("posf" if last or lo == nv else "acc", lo, hi), -0.5, 224.0 if last else 224.5, MUL, ADD)
                scatter(0 if lo == nv else lo, hi)
        for lo, hi in ((0, SPLIT), (SPLIT, 29)):
            scan(V("held2", 16 * lo, 16 * hi), V("ordr", 16 * lo, 16 * hi), V("cap2", 16 * lo, 16 * hi), 0.0, MAX, MUL)
        for lo, hi in ((0, SPLIT), (SPLIT, 29)):
            ts(V("ordl", lo, hi), ends("held2", lo, hi), -1.0, -1.0, MUL, ADD)
        cuts = CUTS[last]
        pieces = list(enumerate(zip(cuts, cuts[1:])))
        free = 4 * ((len(cuts) + 1) % 2)
        into = lambda b, lo, hi: (V("vs", X2 * b + 16 * lo, X2 * b + 16 * hi), by(V("vp", E * b, E * b + E), V("ordl", lo, hi)))
        back = lambda b, lo, hi: by(V("mm", X2 * b, X2 * b + X2), V("pos", lo // 16, hi // 16))
        tc(*into(0, SPLIT, 29))
        for b in range(4):
            act(*into(b, 0, SPLIT if b == 0 else 29), COPY)
        if t == 1:
            act(V("g2", 0, E), V("l4", 0, E), COPY, scale=2816.0)
            add("ac", V("g2", 0, E - 4), V("l4", 4, E))
        turns = TURNS[last].split()
        first = len(calls)
        for b in range(4):
            o = X2 * b
            turn[0] = "M%d" % b
            tt(V("mm", o + 1, o + 1 + E), V("vs", o, o + E), V("vs", o + 2, o + 2 + E), MAX)
            if b in HOME[last]:
                turn[0] = "S%d" % b
                act(V("mb", C * b, C * b + C), back(b, 0, C), COPY)
            for name, lo, hi in (("G", 0, C), ("E", 0, cuts[1]), ("F", cuts[1], C)):
                turn[0] = name + str(b)
                if turn[0] in turns:
                    tt(V("zt", 4 * lo + b, 4 * hi, 4), V("mb", C * b + lo, C * b + hi) if b in HOME[last] else back(b, lo, hi), V("vp", E * b + lo, E * b + hi), ADD)
        if not last:
            turn[0] = "R0"
            for lo, hi, c in ((0, MID, 0.0), (MID, E, (-20.0, -1408.0)[t])):
                act(V("hin%d" % (t + 1), 3 * lo + 2, 3 * hi, 3), V("g%d" % (t + 1), lo, hi), IDEN, bias=c)
        else:
            turn[0] = "L0"
            ts(V("ord4", 0, 29), V("ordl", 0, 29), 3.0, 2.0, MUL, ADD)
            act(V("ks", 0, X2), by(V("kr2", 0, 3 * E), V("ord4", 0, 29)), COPY, scale=512.0)
            turn[0] = "L1"
            for lo in (0, 224):
                tt(V("dk", lo, lo + 224), V("ks", lo + 1, lo + 225), V("ks", lo, lo + 224), SUB)
            turn[0] = "L2"
            scan(V("lw", 1, E + 1), V("dk", 0, E), V("iof", 0, E), 1.0, ADD, MIN)
            act(V("lvr", 0, E), by(V("lw", 0, X2), V("pos", 0, 28)), IDEN, bias=-1.0)
            dma("s", "dlv", T.lv[:, :], dict(V("lvr", 0, E), ap=T.lvr[0:128:16, 0:E], n=0))
        xn, qn = "xt%d" % (t + 1), "qx%d" % (t + 1)
        for k, (lo, hi) in pieces:
            turn[0] = "P%d" % k
            quant("qz", "zt", lo, hi)
            for b in range(4):
                mx(4 * (k % 2) + b, "qw", 128 * b, "qz", lo, hi)
            for b in range(4):
                x = V("x32", 4 * lo + b, 4 * hi, 4)
                turn[0] = "U%d" % k
                tt(x, bank(4 * (k % 2) + b, 0, hi - lo), x, ADD)
                turn[0] = "X%d" % k
                if XS[last][k] == "4":
                    act(V(xn, 4 * lo + b, 4 * hi, 4), x, COPY, scale=0.03125)
            if XS[last][k] == "a":
                act(V(xn, 4 * lo, 4 * hi), V("x32", 4 * lo, 4 * hi), COPY, scale=0.03125)
            elif XS[last][k] == "v":
                ts(V(xn, 4 * lo, 4 * hi), V("x32", 4 * lo, 4 * hi), 0.03125, None, MUL)
            turn[0] = "Q%d" % k
            quant(qn, xn, lo, hi)
            if k == 0 and not last:
                send(t + 1)
        for k, (lo, hi) in enumerate(((0, cuts[-2]), (cuts[-2], C))):
            turn[0] = "B%d" % k
            if last:
                dma("s", "dc" + "ab"[k], T.oc[:, 4 * lo:4 * hi], cast(V(qn, lo, hi), dt.uint8))
                mx(free + k, "qv", 0, qn, lo, hi)
                if k:
                    tc(V("yr", lo, hi), bank(free + k, 0, hi - lo))
                else:
                    act(V("yr", lo, hi), bank(free + k, 0, hi - lo), COPY)
                dma("a", "dy" + "ab"[k], T.y[:, lo:hi], V("yr", lo, hi))
            else:
                for j, (a, z) in pieces[:-1] if k == 0 else ((2, (lo, E)),):
                    turn[0] = "B%d" % j
                    for i in range(k + 1):
                        mx(free + j + i, "qur", 0, qn, a, z)
                    keys(t + 1, free + j, a, z)
                a, z = ((0, MID - 16), (MID - 16, E))[k]
                turn[0] = "H%d" % k
                hold(V("held", a, z), key(t + 1, a, z), "cap")
                if k == 0:
                    if t == 1:
                        turn[0] = "D0"
                        ts(V("own", 0, 15), ends("held", 0, 15), -1.0, None, MUL)
                        before(0, KN)
                    for c in range(SOON[t + 1][0]):
                        turn[0] = "C%d" % min(c, 2)
                        compare(t + 1, c, True)
                    for c in range(SOON[t + 1][1]):
                        turn[0] = "D0"
                        signs(t + 1, NV[t + 1] + c, True)
                aside[0] = True
                for b in range(4):
                    act(V("vp", E * b + lo, E * b + hi), V("x32", 4 * lo + b, 4 * hi, 4), COPY, scale=2.0 ** -6)
                aside[0] = False
        for i, k in enumerate(sorted(range(first, len(calls)), key=lambda k: (turns.index(calls[k]["turn"]), k))):
            calls[k]["place"] = first + i

    s = "sx%d" % NR
    for k in range(4):
        dma("s", "ds%d" % k, T.osc[4 * k:4 * k + 4, 0:C], dict(V(s, 0, C), ap=T[s][32 * k:32 * k + 4, 0:C], n=0))
    issue_all()
